import numpy as np
import ml_dtypes


def mxq(x, axis, fmt="e4m3"):
    dtype, down = {"e4m3": (ml_dtypes.float8_e4m3fn, 7), "e5m2": (ml_dtypes.float8_e5m2, 14)}[fmt]
    v = np.moveaxis(np.asarray(x, np.float32).astype(ml_dtypes.bfloat16).astype(np.float64), axis, -1)
    blocks = v.reshape(v.shape[:-1] + (-1, 32))
    amax = np.abs(blocks).max(-1, keepdims=True)
    byte = np.maximum(np.where(amax > 0, np.frexp(amax)[1] - 1 + 127, 0) - down, 1)
    scale = np.exp2(byte - 127.0)
    codes = (blocks / scale).astype(np.float32).astype(dtype).astype(np.float64)
    return np.moveaxis((codes * scale).reshape(v.shape), -1, axis)


WIDE = False


def mx_kscale(k):
    if not WIDE:
        return np.ones(k)
    levels = np.array([10, -10, 5, -5, 0])
    if k % 512:
        return np.exp2(np.random.permutation(np.resize(levels, k // 32))).repeat(32)
    a = np.empty((k // 512, 16))
    for p in range(k // 512):
        a[p, :8] = np.random.permutation(np.resize(levels, 8))
        for g in range(8):
            far = levels[np.abs(levels - a[p, g]) >= 10]
            a[p, g + 8] = far[np.random.randint(len(far))]
    return np.exp2(a.ravel()).repeat(32)


def f64(x):
    return np.asarray(x).astype(np.float64)


def striped(idx):
    return np.tile(idx.reshape(-1, 16).T, (8, 1)).astype(np.uint16)


def unstriped(offs):
    return offs[:16].T.reshape(-1).astype(np.int64)


E2M1 = np.array([0.0, 0.5, 1.0, 1.5, 2.0, 3.0, 4.0, 6.0, -0.0, -0.5, -1.0, -1.5, -2.0, -3.0, -4.0, -6.0])


def pack_weight(w, fmt):
    k, n = w.shape
    w = f64(np.asarray(w, np.float32).astype(ml_dtypes.bfloat16)).reshape(k // 32, 32, n)
    amax = np.abs(w).max(1)
    if fmt == "e4m3":
        byte = np.frexp(amax)[1] - 1 + 127 - 7
    else:
        mant, ex = np.frexp(amax / 6.0)
        byte = np.where(mant > 0.5, ex, ex - 1) + 127
    byte = np.clip(np.where(amax > 0, byte, 1), 1, 254)
    scaled = (w * np.exp2(127.0 - byte)[:, None, :]).reshape(k, n).astype(np.float32)
    by_word = np.ascontiguousarray(scaled.reshape(k // 512, 128, 4, n).transpose(0, 1, 3, 2))
    if fmt == "e4m3":
        words = by_word.astype(ml_dtypes.float8_e4m3fn).view(np.uint8)
    else:
        c = by_word.astype(ml_dtypes.float4_e2m1fn).view(np.uint8) & 0xF
        words = (c[..., 0::2] | (c[..., 1::2] << 4)).reshape(k // 512, 128, 2 * n)
    return np.ascontiguousarray(words), np.ascontiguousarray(byte.astype(np.uint8).reshape(k // 512, 16, n))


def unpack_weight(words, scales, fmt):
    g, _, n = scales.shape
    words = np.ascontiguousarray(words).reshape(g, 128, n, -1)
    if fmt == "e4m3":
        vals = words.view(ml_dtypes.float8_e4m3fn).astype(np.float64)
    else:
        nib = np.empty((g, 128, n, 4), np.uint8)
        nib[..., 0::2] = words & 0xF
        nib[..., 1::2] = words >> 4
        vals = E2M1[nib]
    vals = vals * np.repeat(np.exp2(scales.astype(np.float64) - 127.0), 8, axis=1)[..., None]
    return vals.transpose(0, 1, 3, 2).reshape(g * 512, n)


def gelu(v):
    return 0.5 * v * (1.0 + np.tanh(np.sqrt(2.0 / np.pi) * (v + 0.044715 * v**3)))


K, H, N, T, S, T2, P = 512, 1024, 384, 4096, 1024, 2048, 1024

def setup_inputs():
    n = np.random.standard_normal
    s = mx_kscale(K)[:, None]
    u = mx_kscale(H)[:, None]
    tab_words, tab_scales = pack_weight(n((K, T)) * s, "e4m3")
    w2_words, w2_scales = pack_weight(n((K, H)) / np.sqrt(K) / s, "e2m1")
    w3_words, w3_scales = pack_weight(n((H, N)) / np.sqrt(H) / u, "e4m3")
    return {
        "tab_words": tab_words, "tab_scales": tab_scales,
        "offs": striped(np.random.permutation(T)[:S]),
        "offs2": striped(np.random.permutation(T2)[:S]),
        "offs3": striped(np.random.permutation(T2)[:P]),
        "offs4": striped(np.random.permutation(T2)[:P]),
        "w1": (n((K, H)) / np.sqrt(K) / s).astype(np.float32),
        "w2_words": w2_words, "w2_scales": w2_scales,
        "wgs": np.exp(0.3 * n((128, S))).astype(np.float32),
        "load": (0.5 * n(H)).astype(np.float32),
        "staff": (np.exp(0.3 * n((H, T2))) * u).astype(np.float32),
        "w3_words": w3_words, "w3_scales": w3_scales,
        "delay": (0.7 * n((N, P))).astype(np.float32),
        "low": (0.3 * n(N)).astype(np.float32),
        "wgo": np.exp(0.3 * n((128, P))).astype(np.float32),
    }

def reference(tab_words, tab_scales, offs, offs2, offs3, offs4, w1, w2_words, w2_scales,
              wgs, load, staff, w3_words, w3_scales, delay, low, wgo):
    v = unpack_weight(tab_words, tab_scales, "e4m3")[:, unstriped(offs)]
    w2 = unpack_weight(w2_words, w2_scales, "e2m1")
    w3 = unpack_weight(w3_words, w3_scales, "e4m3")
    h = np.maximum(mxq(f64(w1), 0, "e4m3").T @ v, w2.T @ v)
    page = np.zeros((H, T2))
    page[:, unstriped(offs2)] = np.tile(f64(wgs), (H // 128, 1)) * h
    z = f64(staff) * (page + f64(load)[:, None])
    y = w3.T @ mxq(z, 0, "e4m3")
    x = np.maximum(y[:, unstriped(offs3)] + f64(delay), f64(low)[:, None])
    out = np.zeros((N, T2))
    out[:, unstriped(offs4)] = np.tile(f64(wgo), (N // 128, 1)) * x
    return out

@@ -1,0 +1,278 @@
+from contextlib import ExitStack
+
+import concourse.mybir as mybir
+
+K, H, N, T, S, T2, PK = 512, 1024, 384, 4096, 1024, 2048, 1024
+FLOPS = 2 * 2 * K * H * S + 2 * H * N * T2
+
+F32 = mybir.dt.float32
+BF16 = mybir.dt.bfloat16
+I32 = mybir.dt.int32
+U32 = mybir.dt.uint32
+U16 = mybir.dt.uint16
+U8 = mybir.dt.uint8
+FP8X4 = mybir.dt.float8_e4m3fn_x4
+FP4X4 = mybir.dt.float4_e2m1fn_x4
+ALU = mybir.AluOpType
+ACT = mybir.ActivationFunctionType
+
+P = 128
+PACK = 4
+BANK = 512
+PASSES = H // (P * PACK)
+ROW_TILES = PASSES * PACK
+CHUNKS = T2 // BANK
+OUT_TILES = N // P
+
+
+def tile_list_theatre_turnover_slots_kernel(
+    tc, tab_words, tab_scales, offs, offs2, offs3, offs4, w1, w2_words, w2_scales,
+    wgs, load, staff, w3_words, w3_scales, delay, low, wgo, out,
+):
+    nc = tc.nc
+    with ExitStack() as ctx:
+        held = ctx.enter_context(tc.tile_pool(name="held", bufs=1))
+        ring = ctx.enter_context(tc.tile_pool(name="ring", bufs=2))
+        psum = ctx.enter_context(tc.psum_pool(name="psum", bufs=2))
+
+        def load_list(source, name):
+            tile = held.tile([P, S // 16], U16, name=name)
+            nc.sync.dma_start(tile[:], source)
+            return tile
+
+        def load_scale_rows(plane, rows):
+            for r in range(4):
+                nc.sync.dma_start(plane[r:P:32].bitcast(I32), rows[r:16:4].bitcast(I32))
+
+        v_words = held.tile([P, S], U32, align_bytes=64)
+        v_scales = held.tile([P, S], U8, align_bytes=64)
+        w1_codes = held.tile([P, H], U32, align_bytes=64)
+        w1_planes = held.tile([P, H], U8, align_bytes=64)
+        w2_codes = held.tile([P, 2 * H], U8, align_bytes=64)
+        w2_planes = held.tile([P, H], U8, align_bytes=64)
+        w3_codes = held.tile([P, PASSES, N], U32, align_bytes=64)
+        w3_planes = held.tile([P, PASSES, N], U8, align_bytes=64)
+        pages = [held.tile([P, T2], F32, name="page%d" % u) for u in range(2)]
+        gains = [held.tile([P, S], F32, name="gains%d" % t) for t in range(PACK)]
+        load_sb = held.tile([P, PASSES, PACK], F32)
+        low_sb = held.tile([P, OUT_TILES], F32)
+        neg_low = held.tile([P, OUT_TILES], F32)
+        wgo_sb = held.tile([P, PK], F32)
+        staff_rows = staff.rearrange("(b p t) c -> b t p c", p=P, t=PACK)
+        wgs_rows = wgs.rearrange("(q t) j -> t q j", t=PACK)
+        staff_sb = {}
+
+        def load_gains(t):
+            for g in (0, 2, 1, 3):
+                nc.sync.dma_start(gains[t][32 * g : 32 * (g + 1), :], wgs_rows[t])
+
+        def load_staff(i):
+            staff_sb[i] = ring.tile([P, T2], F32, name="staff", tag="staff", bufs=4)
+            nc.sync.dma_start(staff_sb[i][:], staff_rows[i // PACK, i % PACK])
+
+        with tc.tile_pool(name="head", bufs=1) as head:
+            tab_w = head.tile([P, T], U32)
+            tab_s = head.tile([P, T], U8)
+            w2_raw = head.tile([P, 2 * H], U8)
+            w2_s_raw = head.tile([P, H], U8)
+            nc.vector.memset(tab_s[:].bitcast(I32), 0)
+            nc.vector.memset(w2_s_raw[:].bitcast(I32), 0)
+            nc.sync.dma_start(tab_w[:].bitcast(I32), tab_words[0].rearrange("p t i -> p (t i)").bitcast(I32))
+            list1 = load_list(offs, "list1")
+            load_scale_rows(tab_s, tab_scales[0])
+            nc.sync.dma_start(w2_raw[:].bitcast(I32), w2_words[0].bitcast(I32))
+            load_scale_rows(w2_s_raw, w2_scales[0])
+            for page in pages:
+                nc.vector.memset(page[:], 0.0)
+
+            def quantise_w1(b, engine_copy):
+                raw = head.tile([P, PACK, BANK], F32, name="w1_raw")
+                nc.sync.dma_start(raw[:], w1[:, b * BANK : (b + 1) * BANK].rearrange("(p j) c -> p j c", j=PACK))
+                grouped = head.tile([P, PACK * BANK], BF16, name="w1_grouped", align_bytes=64)
+                engine_copy(
+                    grouped[:].rearrange("p (t m j) -> p m j t", t=PACK, j=PACK),
+                    raw[:].rearrange("p j (m t) -> p m j t", t=PACK),
+                )
+                cols = slice(b * BANK, (b + 1) * BANK)
+                nc.vector.quantize_mx(out=w1_codes[:, cols].bitcast(FP8X4), scales=w1_planes[:, cols], in_=grouped[:])
+
+            for half in range(S // BANK):
+                cols = slice(half * BANK, (half + 1) * BANK)
+                part = list1[:, half * 32 : (half + 1) * 32]
+                nc.vector.tensor_copy(v_scales[:, cols], tab_s[:].indirect(part))
+            for b in range(PASSES):
+                nc.vector.tensor_copy(
+                    w2_codes[:, 2 * b * BANK : 2 * (b + 1) * BANK].rearrange("p (t m e) -> p t m e", t=PACK, e=2),
+                    w2_raw[:, 2 * b * BANK : 2 * (b + 1) * BANK].rearrange("p (m t e) -> p t m e", t=PACK, e=2),
+                )
+                nc.vector.tensor_copy(
+                    w2_planes[:, b * BANK : (b + 1) * BANK].rearrange("p (t m) -> p t m", t=PACK),
+                    w2_s_raw[:, b * BANK : (b + 1) * BANK].rearrange("p (m t) -> p t m", t=PACK),
+                )
+            for half in range(S // BANK):
+                cols = slice(half * BANK, (half + 1) * BANK)
+                part = list1[:, half * 32 : (half + 1) * 32]
+                nc.vector.tensor_copy(v_words[:, cols], tab_w[:].indirect(part))
+            quantise_w1(0, nc.vector.tensor_copy)
+            load_gains(0)
+            list2 = load_list(offs2, "list2")
+            nc.sync.dma_start(load_sb[:], load.rearrange("(b p t) -> p b t", p=P, t=PACK))
+            load_gains(1)
+            load_staff(0)
+            load_gains(2)
+            quantise_w1(1, nc.scalar.copy)
+            load_staff(1)
+            load_gains(3)
+            load_staff(2)
+            load_staff(3)
+
+        tail = ctx.enter_context(tc.tile_pool(name="tail", bufs=1))
+        nc.vector.memset(w3_planes[:].bitcast(I32), 0)
+        nc.sync.dma_start(w3_codes[:].bitcast(I32), w3_words.rearrange("a p c i -> p a (c i)").bitcast(I32))
+        load_scale_rows(w3_planes, w3_scales.rearrange("a q c -> q a c"))
+        list3 = load_list(offs3, "list3")
+        list4 = load_list(offs4, "list4")
+        with nc.allow_non_contiguous_dma(reason="one value a partition"):
+            nc.sync.dma_start(low_sb[:], low.rearrange("(n p) -> p n", p=P))
+        nc.scalar.activation(neg_low[:], low_sb[:], ACT.Copy, scale=-1.0)
+        nc.sync.dma_start(wgo_sb[:], wgo)
+        delay_sb = [tail.tile([P, PK], F32, name="delay%d" % n) for n in range(OUT_TILES)]
+        for n in range(OUT_TILES):
+            nc.sync.dma_start(delay_sb[n][:], delay[n * P : (n + 1) * P, :])
+
+        z_rows = [held.tile([P, CHUNKS, PACK, BANK], BF16, name="z_rows%d" % b) for b in range(PASSES)]
+        z_codes = [held.tile([P, T2], U32, name="z_codes%d" % b, align_bytes=64) for b in range(PASSES)]
+        z_planes = [held.tile([P, T2], U8, name="z_planes%d" % b, align_bytes=64) for b in range(PASSES)]
+        weighted = {}
+        z_grouped = {}
+
+        def scores(i):
+            cols = slice(i * P, (i + 1) * P)
+            larger = ring.tile([P, S], F32, name="larger", tag="larger", bufs=3)
+            for half in range(S // BANK):
+                js = slice(half * BANK, (half + 1) * BANK)
+                team = psum.tile([P, BANK], F32, name="team")
+                nc.tensor.matmul_mx(
+                    out=team[:], lhsT=w2_codes[:, 2 * i * P : 2 * (i + 1) * P].bitcast(FP4X4), lhsT_scale=w2_planes[:, cols],
+                    rhs=v_words[:, js].bitcast(FP8X4), rhs_scale=v_scales[:, js], start=True, stop=True,
+                )
+                room = psum.tile([P, BANK], F32, name="room")
+                nc.tensor.matmul_mx(
+                    out=room[:], lhsT=w1_codes[:, cols].bitcast(FP8X4), lhsT_scale=w1_planes[:, cols],
+                    rhs=v_words[:, js].bitcast(FP8X4), rhs_scale=v_scales[:, js], start=True, stop=True,
+                )
+                team_sb = ring.tile([P, BANK], F32, name="team_sb", tag="team_sb", bufs=3)
+                nc.scalar.copy(team_sb[:], team[:])
+                nc.vector.tensor_tensor(larger[:, js], room[:], team_sb[:], ALU.max)
+            weighted[i] = ring.tile([P, S], F32, name="weighted", tag="weighted", bufs=3)
+            nc.gpsimd.tensor_tensor(weighted[i][:], larger[:], gains[i % PACK][:], ALU.mult)
+
+        def place(i):
+            nc.vector.tensor_copy(pages[i % 2][:].indirect(list2[:]), weighted[i][:])
+
+        def staffed(i):
+            b, t = divmod(i, PACK)
+            loaded = ring.tile([P, T2], F32, name="loaded")
+            nc.scalar.activation(loaded[:], pages[i % 2][:], ACT.Identity, bias=load_sb[:, b, t : t + 1])
+            nc.gpsimd.tensor_tensor(
+                z_rows[b][:, :, t, :], loaded[:].rearrange("p (c j) -> p c j", j=BANK),
+                staff_sb[i][:].rearrange("p (c j) -> p c j", j=BANK), ALU.mult,
+            )
+
+        def staffed_last(i, c):
+            b, t = divmod(i, PACK)
+            cols = slice(c * BANK, (c + 1) * BANK)
+            nc.vector.scalar_tensor_tensor(
+                z_rows[b][:, c, t, :], pages[i % 2][:, cols], load_sb[:, b, t : t + 1], staff_sb[i][:, cols], ALU.add, ALU.mult,
+            )
+
+        def interleave(b, c, engine_copy):
+            z_grouped[b, c] = ring.tile([P, BANK, PACK], BF16, name="z_grouped", tag="z_grouped", bufs=3, align_bytes=64)
+            engine_copy(
+                z_grouped[b, c][:].rearrange("p (c i) t -> p c t i", i=4),
+                z_rows[b][:, c].rearrange("p t (c i) -> p c t i", i=4),
+            )
+
+        def quantise_z(b, c):
+            cols = slice(c * BANK, (c + 1) * BANK)
+            nc.vector.quantize_mx(
+                out=z_codes[b][:, cols].bitcast(FP8X4), scales=z_planes[b][:, cols],
+                in_=z_grouped[b, c][:].rearrange("p c t -> p (c t)"),
+            )
+
+        last = ROW_TILES - 1
+        crew = []
+        scores(0)
+        scores(1)
+        for i in range(ROW_TILES):
+            if i + 2 <= last:
+                scores(i + 2)
+            place(i)
+            if i < last:
+                staffed(i)
+            if i + 4 <= last:
+                load_staff(i + 4)
+            if i in (4, 5):
+                crew.append(ring.tile([P, T2], F32, name="crew", tag="staff", bufs=4))
+                nc.gpsimd.memset(crew[-1][:], 0.0)
+            if i >= PACK:
+                interleave(0, i - PACK, nc.scalar.copy)
+            if i > PACK:
+                quantise_z(0, i - PACK - 1)
+        quantise_z(0, CHUNKS - 1)
+
+        y_sb = [tail.tile([P, T2], F32, name="y%d" % n) for n in range(OUT_TILES)]
+
+        def features(n, c):
+            cols = slice(c * BANK, (c + 1) * BANK)
+            acc = psum.tile([P, BANK], F32, name="acc", tag="acc", bufs=4)
+            for b in range(PASSES):
+                nc.tensor.matmul_mx(
+                    out=acc[:], lhsT=w3_codes[:, b, n * P : (n + 1) * P].bitcast(FP8X4), lhsT_scale=w3_planes[:, b, n * P : (n + 1) * P],
+                    rhs=z_codes[b][:, cols].bitcast(FP8X4), rhs_scale=z_planes[b][:, cols], start=(b == 0), stop=(b == PASSES - 1),
+                )
+            nc.scalar.copy(y_sb[n][:, cols], acc[:])
+
+        staffed_last(last, 0)
+        staffed_last(last, 1)
+        interleave(1, 0, nc.scalar.copy)
+        interleave(1, 1, nc.vector.tensor_copy)
+        staffed_last(last, 2)
+        quantise_z(1, 1)
+        staffed_last(last, 3)
+        interleave(1, 2, nc.scalar.copy)
+        quantise_z(1, 0)
+        interleave(1, 3, nc.vector.tensor_copy)
+        features(0, 1)
+        features(0, 0)
+        quantise_z(1, 3)
+        quantise_z(1, 2)
+        features(0, 3)
+        features(0, 2)
+
+        floored = {}
+
+        def pick(n):
+            picked = ring.tile([P, PK], F32, name="picked", tag="larger", bufs=3)
+            nc.vector.tensor_tensor(picked[:], y_sb[n][:].indirect(list3[:]), delay_sb[n][:], ALU.add)
+            return picked
+
+        def floor(n, picked):
+            above = ring.tile([P, PK], F32, name="above", tag="loaded")
+            nc.scalar.activation(above[:], picked[:], ACT.Relu, bias=neg_low[:, n : n + 1])
+            floored[n] = ring.tile([P, PK], F32, name="floored", tag="weighted", bufs=3)
+            nc.scalar.activation(floored[n][:], above[:], ACT.Identity, bias=low_sb[:, n : n + 1])
+
+        def hand_over(n):
+            nc.vector.tensor_tensor(crew[n % 2][:].indirect(list4[:]), floored[n][:], wgo_sb[:], ALU.mult)
+            nc.sync.dma_start(out[n * P : (n + 1) * P, :], crew[n % 2][:])
+
+        for n in range(OUT_TILES):
+            picked = pick(n)
+            if n + 1 < OUT_TILES:
+                for c in range(CHUNKS):
+                    features(n + 1, c)
+            floor(n, picked)
+            if n > 0:
+                hand_over(n - 1)
+        hand_over(OUT_TILES - 1)

@@ -23,6 +23,7 @@ PASSES = H // (P * PACK)
 ROW_TILES = PASSES * PACK
 CHUNKS = T2 // BANK
 OUT_TILES = N // P
+SLOTS = 5
 
 
 def tile_list_theatre_turnover_slots_kernel(
@@ -33,7 +34,7 @@ def tile_list_theatre_turnover_slots_kernel(
     with ExitStack() as ctx:
         held = ctx.enter_context(tc.tile_pool(name="held", bufs=1))
         ring = ctx.enter_context(tc.tile_pool(name="ring", bufs=2))
-        psum = ctx.enter_context(tc.psum_pool(name="psum", bufs=2))
+        psum = ctx.enter_context(tc.psum_pool(name="psum", bufs=8))
 
         def load_list(source, name):
             tile = held.tile([P, S // 16], U16, name=name)
@@ -46,88 +47,93 @@ def tile_list_theatre_turnover_slots_kernel(
 
         v_words = held.tile([P, S], U32, align_bytes=64)
         v_scales = held.tile([P, S], U8, align_bytes=64)
-        w1_codes = held.tile([P, H], U32, align_bytes=64)
-        w1_planes = held.tile([P, H], U8, align_bytes=64)
+        w1_codes = [held.tile([P, BANK], U32, name="w1_codes%d" % b, align_bytes=64) for b in range(PASSES)]
+        w1_planes = [held.tile([P, BANK], U8, name="w1_planes%d" % b, align_bytes=64) for b in range(PASSES)]
+        pages = [held.tile([P, T2], F32, name="page%d" % u) for u in range(2)]
         w2_codes = held.tile([P, 2 * H], U8, align_bytes=64)
         w2_planes = held.tile([P, H], U8, align_bytes=64)
-        w3_codes = held.tile([P, PASSES, N], U32, align_bytes=64)
-        w3_planes = held.tile([P, PASSES, N], U8, align_bytes=64)
-        pages = [held.tile([P, T2], F32, name="page%d" % u) for u in range(2)]
-        gains = [held.tile([P, S], F32, name="gains%d" % t) for t in range(PACK)]
-        load_sb = held.tile([P, PASSES, PACK], F32)
-        low_sb = held.tile([P, OUT_TILES], F32)
-        neg_low = held.tile([P, OUT_TILES], F32)
-        wgo_sb = held.tile([P, PK], F32)
         staff_rows = staff.rearrange("(b p t) c -> b t p c", p=P, t=PACK)
-        wgs_rows = wgs.rearrange("(q t) j -> t q j", t=PACK)
+        wgs_rows = wgs.rearrange("(q t) j -> q t j", t=PACK)
         staff_sb = {}
 
-        def load_gains(t):
+        gains = []
+
+        def load_gains(u):
+            pair = held.tile([P, 2, S], F32, name="gains", tag="gains%d" % u)
             for g in (0, 2, 1, 3):
-                nc.sync.dma_start(gains[t][32 * g : 32 * (g + 1), :], wgs_rows[t])
+                nc.sync.dma_start(pair[32 * g : 32 * (g + 1)], wgs_rows[:, 2 * u : 2 * u + 2])
+            gains.extend([pair[:, 0], pair[:, 1]])
 
         def load_staff(i):
-            staff_sb[i] = ring.tile([P, T2], F32, name="staff", tag="staff", bufs=4)
+            staff_sb[i] = ring.tile([P, T2], F32, name="staff", tag="wide", bufs=3, align_bytes=64)
             nc.sync.dma_start(staff_sb[i][:], staff_rows[i // PACK, i % PACK])
 
+        tab_s = ring.tile([P, T], U8, name="tab_s", tag="wide", bufs=3, align_bytes=64)
+        w1_grouped = [
+            held.tile([P, PACK * BANK], BF16, name="w1_grouped", tag="grouped0", align_bytes=64),
+            ring.tile([P, PACK * BANK], BF16, name="w1_grouped", tag="wide", bufs=3, align_bytes=64),
+        ]
+        w2_s_raw = ring.tile([P, H], U8, name="w2_s_raw", tag="wide", bufs=3, align_bytes=64)
+
+        def load_w1(b):
+            raw = held.tile([P, PACK, BANK], F32, name="w1_raw", tag="gains%d" % b)
+            nc.sync.dma_start(raw[:], w1[:, b * BANK : (b + 1) * BANK].rearrange("(p j) c -> p j c", j=PACK))
+            nc.scalar.copy(
+                w1_grouped[b][:].rearrange("p (t m j) -> p m j t", t=PACK, j=PACK),
+                raw[:].rearrange("p j (m t) -> p m j t", t=PACK),
+            )
+
+        def quantise_w1(b):
+            nc.vector.quantize_mx(out=w1_codes[b][:].bitcast(FP8X4), scales=w1_planes[b][:], in_=w1_grouped[b][:])
+
         with tc.tile_pool(name="head", bufs=1) as head:
-            tab_w = head.tile([P, T], U32)
-            tab_s = head.tile([P, T], U8)
             w2_raw = head.tile([P, 2 * H], U8)
-            w2_s_raw = head.tile([P, H], U8)
+            tab_w = head.tile([P, T], U32)
             nc.vector.memset(tab_s[:].bitcast(I32), 0)
-            nc.vector.memset(w2_s_raw[:].bitcast(I32), 0)
-            nc.sync.dma_start(tab_w[:].bitcast(I32), tab_words[0].rearrange("p t i -> p (t i)").bitcast(I32))
-            list1 = load_list(offs, "list1")
+            nc.gpsimd.memset(w2_s_raw[:].bitcast(I32), 0)
+            load_w1(0)
             load_scale_rows(tab_s, tab_scales[0])
+            list1 = load_list(offs, "list1")
             nc.sync.dma_start(w2_raw[:].bitcast(I32), w2_words[0].bitcast(I32))
+            load_w1(1)
             load_scale_rows(w2_s_raw, w2_scales[0])
-            for page in pages:
-                nc.vector.memset(page[:], 0.0)
+            nc.sync.dma_start(tab_w[:].bitcast(I32), tab_words[0].rearrange("p t i -> p (t i)").bitcast(I32))
+            nc.vector.tensor_copy(
+                w2_codes[:].bitcast(U16).rearrange("p (b t m) -> p b t m", b=PASSES, t=PACK),
+                w2_raw[:].bitcast(U16).rearrange("p (b m t) -> p b t m", b=PASSES, t=PACK),
+            )
 
-            def quantise_w1(b, engine_copy):
-                raw = head.tile([P, PACK, BANK], F32, name="w1_raw")
-                nc.sync.dma_start(raw[:], w1[:, b * BANK : (b + 1) * BANK].rearrange("(p j) c -> p j c", j=PACK))
-                grouped = head.tile([P, PACK * BANK], BF16, name="w1_grouped", align_bytes=64)
-                engine_copy(
-                    grouped[:].rearrange("p (t m j) -> p m j t", t=PACK, j=PACK),
-                    raw[:].rearrange("p j (m t) -> p m j t", t=PACK),
-                )
-                cols = slice(b * BANK, (b + 1) * BANK)
-                nc.vector.quantize_mx(out=w1_codes[:, cols].bitcast(FP8X4), scales=w1_planes[:, cols], in_=grouped[:])
-
-            for half in range(S // BANK):
-                cols = slice(half * BANK, (half + 1) * BANK)
-                part = list1[:, half * 32 : (half + 1) * 32]
-                nc.vector.tensor_copy(v_scales[:, cols], tab_s[:].indirect(part))
-            for b in range(PASSES):
-                nc.vector.tensor_copy(
-                    w2_codes[:, 2 * b * BANK : 2 * (b + 1) * BANK].rearrange("p (t m e) -> p t m e", t=PACK, e=2),
-                    w2_raw[:, 2 * b * BANK : 2 * (b + 1) * BANK].rearrange("p (m t e) -> p t m e", t=PACK, e=2),
-                )
+            def order_w2(b):
                 nc.vector.tensor_copy(
                     w2_planes[:, b * BANK : (b + 1) * BANK].rearrange("p (t m) -> p t m", t=PACK),
                     w2_s_raw[:, b * BANK : (b + 1) * BANK].rearrange("p (m t) -> p t m", t=PACK),
                 )
+
             for half in range(S // BANK):
                 cols = slice(half * BANK, (half + 1) * BANK)
                 part = list1[:, half * 32 : (half + 1) * 32]
                 nc.vector.tensor_copy(v_words[:, cols], tab_w[:].indirect(part))
-            quantise_w1(0, nc.vector.tensor_copy)
+                nc.vector.tensor_copy(v_scales[:, cols], tab_s[:].indirect(part))
+                order_w2(half)
+                quantise_w1(half)
+            for page in pages:
+                nc.vector.memset(page[:], 0.0)
             load_gains(0)
             list2 = load_list(offs2, "list2")
+            load_sb = held.tile([P, PASSES, PACK], F32)
             nc.sync.dma_start(load_sb[:], load.rearrange("(b p t) -> p b t", p=P, t=PACK))
-            load_gains(1)
             load_staff(0)
-            load_gains(2)
-            quantise_w1(1, nc.scalar.copy)
+            load_gains(1)
             load_staff(1)
-            load_gains(3)
             load_staff(2)
-            load_staff(3)
 
         tail = ctx.enter_context(tc.tile_pool(name="tail", bufs=1))
-        nc.vector.memset(w3_planes[:].bitcast(I32), 0)
+        w3_codes = tail.tile([P, PASSES, N], U32, align_bytes=64)
+        w3_planes = tail.tile([P, PASSES, N], U8, align_bytes=64)
+        low_sb = tail.tile([P, OUT_TILES], F32)
+        neg_low = tail.tile([P, OUT_TILES], F32)
+        wgo_sb = tail.tile([P, PK], F32)
+        nc.gpsimd.memset(w3_planes[:].bitcast(I32), 0)
         nc.sync.dma_start(w3_codes[:].bitcast(I32), w3_words.rearrange("a p c i -> p a (c i)").bitcast(I32))
         load_scale_rows(w3_planes, w3_scales.rearrange("a q c -> q a c"))
         list3 = load_list(offs3, "list3")
@@ -140,39 +146,44 @@ def tile_list_theatre_turnover_slots_kernel(
         for n in range(OUT_TILES):
             nc.sync.dma_start(delay_sb[n][:], delay[n * P : (n + 1) * P, :])
 
-        z_rows = [held.tile([P, CHUNKS, PACK, BANK], BF16, name="z_rows%d" % b) for b in range(PASSES)]
-        z_codes = [held.tile([P, T2], U32, name="z_codes%d" % b, align_bytes=64) for b in range(PASSES)]
-        z_planes = [held.tile([P, T2], U8, name="z_planes%d" % b, align_bytes=64) for b in range(PASSES)]
+        z_rows = [ring.tile([P, CHUNKS, PACK, BANK], BF16, name="z_rows", tag="z_rows", align_bytes=64) for b in range(PASSES)]
+        z_codes = [held.tile([P, T2], U32, name="z_codes", tag="z_codes%d" % b, align_bytes=64) for b in range(PASSES)]
         weighted = {}
         z_grouped = {}
+        z_planes = {}
 
         def scores(i):
             cols = slice(i * P, (i + 1) * P)
-            larger = ring.tile([P, S], F32, name="larger", tag="larger", bufs=3)
+            b, t = divmod(i, PACK)
+            larger = held.tile([P, S], F32, name="larger", tag="slot%d" % ((i - 2) % SLOTS), align_bytes=64)
+            weighted[i] = held.tile([P, S], F32, name="weighted", tag="slot%d" % (i % SLOTS), align_bytes=64)
             for half in range(S // BANK):
                 js = slice(half * BANK, (half + 1) * BANK)
-                team = psum.tile([P, BANK], F32, name="team")
+                team = psum.tile([P, BANK], F32, name="team", tag="bank")
                 nc.tensor.matmul_mx(
                     out=team[:], lhsT=w2_codes[:, 2 * i * P : 2 * (i + 1) * P].bitcast(FP4X4), lhsT_scale=w2_planes[:, cols],
                     rhs=v_words[:, js].bitcast(FP8X4), rhs_scale=v_scales[:, js], start=True, stop=True,
                 )
-                room = psum.tile([P, BANK], F32, name="room")
+                room = psum.tile([P, BANK], F32, name="room", tag="bank")
                 nc.tensor.matmul_mx(
-                    out=room[:], lhsT=w1_codes[:, cols].bitcast(FP8X4), lhsT_scale=w1_planes[:, cols],
+                    out=room[:], lhsT=w1_codes[b][:, t * P : (t + 1) * P].bitcast(FP8X4),
+                    lhsT_scale=w1_planes[b][:, t * P : (t + 1) * P],
                     rhs=v_words[:, js].bitcast(FP8X4), rhs_scale=v_scales[:, js], start=True, stop=True,
                 )
                 team_sb = ring.tile([P, BANK], F32, name="team_sb", tag="team_sb", bufs=3)
                 nc.scalar.copy(team_sb[:], team[:])
                 nc.vector.tensor_tensor(larger[:, js], room[:], team_sb[:], ALU.max)
-            weighted[i] = ring.tile([P, S], F32, name="weighted", tag="weighted", bufs=3)
-            nc.gpsimd.tensor_tensor(weighted[i][:], larger[:], gains[i % PACK][:], ALU.mult)
+                if i == 0:
+                    nc.gpsimd.tensor_tensor(weighted[i][:, js], larger[:, js], gains[t][:, js], ALU.mult)
+            if i > 0:
+                nc.gpsimd.tensor_tensor(weighted[i][:], larger[:], gains[t], ALU.mult)
 
         def place(i):
             nc.vector.tensor_copy(pages[i % 2][:].indirect(list2[:]), weighted[i][:])
 
         def staffed(i):
             b, t = divmod(i, PACK)
-            loaded = ring.tile([P, T2], F32, name="loaded")
+            loaded = held.tile([P, T2], F32, name="loaded", tag="slot%d" % ((i - 1) % SLOTS), align_bytes=64)
             nc.scalar.activation(loaded[:], pages[i % 2][:], ACT.Identity, bias=load_sb[:, b, t : t + 1])
             nc.gpsimd.tensor_tensor(
                 z_rows[b][:, :, t, :], loaded[:].rearrange("p (c j) -> p c j", j=BANK),
@@ -187,45 +198,45 @@ def tile_list_theatre_turnover_slots_kernel(
             )
 
         def interleave(b, c, engine_copy):
-            z_grouped[b, c] = ring.tile([P, BANK, PACK], BF16, name="z_grouped", tag="z_grouped", bufs=3, align_bytes=64)
             engine_copy(
-                z_grouped[b, c][:].rearrange("p (c i) t -> p c t i", i=4),
+                z_grouped[b, c].rearrange("p (c i) t -> p c t i", i=4),
                 z_rows[b][:, c].rearrange("p t (c i) -> p c t i", i=4),
             )
 
-        def quantise_z(b, c):
-            cols = slice(c * BANK, (c + 1) * BANK)
+        def quantise_z(b, cols, grouped):
             nc.vector.quantize_mx(
                 out=z_codes[b][:, cols].bitcast(FP8X4), scales=z_planes[b][:, cols],
-                in_=z_grouped[b, c][:].rearrange("p c t -> p (c t)"),
+                in_=grouped,
             )
 
         last = ROW_TILES - 1
-        crew = []
+        halves = [
+            held.tile([P, 2, BANK, PACK], BF16, name="z_half", tag="grouped%d" % u, align_bytes=64) for u in range(2)
+        ]
+        for c in range(CHUNKS):
+            z_grouped[0, c] = halves[c // 2][:, c % 2]
         scores(0)
         scores(1)
         for i in range(ROW_TILES):
+            place(i)
             if i + 2 <= last:
                 scores(i + 2)
-            place(i)
             if i < last:
                 staffed(i)
-            if i + 4 <= last:
-                load_staff(i + 4)
-            if i in (4, 5):
-                crew.append(ring.tile([P, T2], F32, name="crew", tag="staff", bufs=4))
-                nc.gpsimd.memset(crew[-1][:], 0.0)
-            if i >= PACK:
-                interleave(0, i - PACK, nc.scalar.copy)
-            if i > PACK:
-                quantise_z(0, i - PACK - 1)
-        quantise_z(0, CHUNKS - 1)
+            if i + 3 <= last:
+                load_staff(i + 3)
+            for c in {4: (0, 1), 5: (2,), 6: (3,)}.get(i, ()):
+                interleave(0, c, nc.scalar.copy)
+        for c in range(CHUNKS):
+            z_grouped[1, c] = tail.tile([P, BANK, PACK], BF16, name="z_chunk", tag="chunk%d" % c, align_bytes=64)[:]
+        z_planes[0] = held.tile([P, T2], U8, name="z_planes0", tag="slot%d" % (last % SLOTS), align_bytes=64)
+        z_planes[1] = held.tile([P, T2], U8, name="z_planes1", align_bytes=64)
 
-        y_sb = [tail.tile([P, T2], F32, name="y%d" % n) for n in range(OUT_TILES)]
+        y_sb = [ring.tile([P, T2], F32, name="y", tag="wide", bufs=3, align_bytes=64) for n in range(OUT_TILES)]
 
         def features(n, c):
             cols = slice(c * BANK, (c + 1) * BANK)
-            acc = psum.tile([P, BANK], F32, name="acc", tag="acc", bufs=4)
+            acc = psum.tile([P, BANK], F32, name="acc", tag="bank")
             for b in range(PASSES):
                 nc.tensor.matmul_mx(
                     out=acc[:], lhsT=w3_codes[:, b, n * P : (n + 1) * P].bitcast(FP8X4), lhsT_scale=w3_planes[:, b, n * P : (n + 1) * P],
@@ -233,46 +244,53 @@ def tile_list_theatre_turnover_slots_kernel(
                 )
             nc.scalar.copy(y_sb[n][:, cols], acc[:])
 
-        staffed_last(last, 0)
-        staffed_last(last, 1)
+        for c in range(CHUNKS):
+            staffed_last(last, c)
+        def quantise_chunk(c):
+            quantise_z(1, slice(c * BANK, (c + 1) * BANK), z_grouped[1, c].rearrange("p j t -> p (j t)"))
+
         interleave(1, 0, nc.scalar.copy)
-        interleave(1, 1, nc.vector.tensor_copy)
-        staffed_last(last, 2)
-        quantise_z(1, 1)
-        staffed_last(last, 3)
-        interleave(1, 2, nc.scalar.copy)
-        quantise_z(1, 0)
+        interleave(1, 1, nc.scalar.copy)
+        for u in range(2):
+            quantise_z(0, slice(2 * u * BANK, 2 * (u + 1) * BANK), halves[u][:].rearrange("p c j t -> p (c j t)"))
         interleave(1, 3, nc.vector.tensor_copy)
-        features(0, 1)
-        features(0, 0)
-        quantise_z(1, 3)
-        quantise_z(1, 2)
-        features(0, 3)
-        features(0, 2)
+        quantise_chunk(0)
+        interleave(1, 2, nc.vector.tensor_copy)
+        quantise_chunk(3)
+        quantise_chunk(2)
+        quantise_chunk(1)
+        for c in (0, 3, 2, 1):
+            features(0, c)
 
         floored = {}
 
         def pick(n):
-            picked = ring.tile([P, PK], F32, name="picked", tag="larger", bufs=3)
+            picked = held.tile([P, PK], F32, name="picked", tag="slot%d" % (3 + n % 2), align_bytes=64)
             nc.vector.tensor_tensor(picked[:], y_sb[n][:].indirect(list3[:]), delay_sb[n][:], ALU.add)
             return picked
 
         def floor(n, picked):
-            above = ring.tile([P, PK], F32, name="above", tag="loaded")
+            above = held.tile([P, PK], F32, name="above", tag="slot0", align_bytes=64)
             nc.scalar.activation(above[:], picked[:], ACT.Relu, bias=neg_low[:, n : n + 1])
-            floored[n] = ring.tile([P, PK], F32, name="floored", tag="weighted", bufs=3)
+            floored[n] = tail.tile([P, PK], F32, name="floored", tag="floored%d" % (n % 2))
             nc.scalar.activation(floored[n][:], above[:], ACT.Identity, bias=low_sb[:, n : n + 1])
 
         def hand_over(n):
             nc.vector.tensor_tensor(crew[n % 2][:].indirect(list4[:]), floored[n][:], wgo_sb[:], ALU.mult)
             nc.sync.dma_start(out[n * P : (n + 1) * P, :], crew[n % 2][:])
 
+        crew = [tail.tile([P, T2], F32, name="crew", tag="chunk1", align_bytes=64)]
+        nc.vector.memset(crew[0][:], 0.0)
+        picked = {0: pick(0)}
         for n in range(OUT_TILES):
-            picked = pick(n)
             if n + 1 < OUT_TILES:
-                for c in range(CHUNKS):
+                for c in (0, 3, 2, 1):
                     features(n + 1, c)
-            floor(n, picked)
+                picked[n + 1] = pick(n + 1)
+            if n + 2 == OUT_TILES:
+                crew.append(held.tile([P, T2], F32, name="crew", tag="z_codes1", align_bytes=64))
+                nc.gpsimd.memset(crew[1][:], 0.0)
             if n > 0:
                 hand_over(n - 1)
+            floor(n, picked[n])
         hand_over(OUT_TILES - 1)

@@ -58,11 +58,11 @@ def tile_list_theatre_turnover_slots_kernel(
 
         gains = []
 
-        def load_gains(u):
-            pair = held.tile([P, 2, S], F32, name="gains", tag="gains%d" % u)
+        def load_gains(first, count, tag):
+            rows = held.tile([P, count, S], F32, name="gains", tag=tag)
             for g in (0, 2, 1, 3):
-                nc.sync.dma_start(pair[32 * g : 32 * (g + 1)], wgs_rows[:, 2 * u : 2 * u + 2])
-            gains.extend([pair[:, 0], pair[:, 1]])
+                nc.sync.dma_start(rows[32 * g : 32 * (g + 1)], wgs_rows[:, first : first + count])
+            gains.extend([rows[:, u] for u in range(count)])
 
         def load_staff(i):
             staff_sb[i] = ring.tile([P, T2], F32, name="staff", tag="wide", bufs=3, align_bytes=64)
@@ -79,8 +79,8 @@ def tile_list_theatre_turnover_slots_kernel(
             raw = held.tile([P, PACK, BANK], F32, name="w1_raw", tag="gains%d" % b)
             nc.sync.dma_start(raw[:], w1[:, b * BANK : (b + 1) * BANK].rearrange("(p j) c -> p j c", j=PACK))
             nc.scalar.copy(
-                w1_grouped[b][:].rearrange("p (t m j) -> p m j t", t=PACK, j=PACK),
-                raw[:].rearrange("p j (m t) -> p m j t", t=PACK),
+                w1_grouped[b][:].rearrange("p (t m j) -> p m t j", t=PACK, j=PACK),
+                raw[:].rearrange("p j (m t) -> p m t j", t=PACK),
             )
 
         def quantise_w1(b):
@@ -118,12 +118,13 @@ def tile_list_theatre_turnover_slots_kernel(
                 quantise_w1(half)
             for page in pages:
                 nc.vector.memset(page[:], 0.0)
-            load_gains(0)
+            load_gains(0, 1, "gains_first")
             list2 = load_list(offs2, "list2")
             load_sb = held.tile([P, PASSES, PACK], F32)
             nc.sync.dma_start(load_sb[:], load.rearrange("(b p t) -> p b t", p=P, t=PACK))
+            load_gains(1, 1, "gains0")
             load_staff(0)
-            load_gains(1)
+            load_gains(2, 2, "gains1")
             load_staff(1)
             load_staff(2)
 
@@ -179,7 +180,12 @@ def tile_list_theatre_turnover_slots_kernel(
                 nc.gpsimd.tensor_tensor(weighted[i][:], larger[:], gains[t], ALU.mult)
 
         def place(i):
-            nc.vector.tensor_copy(pages[i % 2][:].indirect(list2[:]), weighted[i][:])
+            if i == 0:
+                for half in range(S // BANK):
+                    part = list2[:, half * 32 : (half + 1) * 32]
+                    nc.vector.tensor_copy(pages[0][:].indirect(part), weighted[0][:, half * BANK : (half + 1) * BANK])
+            else:
+                nc.vector.tensor_copy(pages[i % 2][:].indirect(list2[:]), weighted[i][:])
 
         def staffed(i):
             b, t = divmod(i, PACK)

@@ -23,7 +23,7 @@ PASSES = H // (P * PACK)
 ROW_TILES = PASSES * PACK
 CHUNKS = T2 // BANK
 OUT_TILES = N // P
-SLOTS = 5
+SLOTS = 4
 
 
 def tile_list_theatre_turnover_slots_kernel(
@@ -156,7 +156,7 @@ def tile_list_theatre_turnover_slots_kernel(
         def scores(i):
             cols = slice(i * P, (i + 1) * P)
             b, t = divmod(i, PACK)
-            larger = held.tile([P, S], F32, name="larger", tag="slot%d" % ((i - 2) % SLOTS), align_bytes=64)
+            larger = held.tile([P, S], F32, name="larger", tag="slot%d" % ((i - 2) % SLOTS) if i != 1 else "crew1", align_bytes=64)
             weighted[i] = held.tile([P, S], F32, name="weighted", tag="slot%d" % (i % SLOTS), align_bytes=64)
             for half in range(S // BANK):
                 js = slice(half * BANK, (half + 1) * BANK)
@@ -180,21 +180,20 @@ def tile_list_theatre_turnover_slots_kernel(
                 nc.gpsimd.tensor_tensor(weighted[i][:], larger[:], gains[t], ALU.mult)
 
         def place(i):
-            if i == 0:
-                for half in range(S // BANK):
-                    part = list2[:, half * 32 : (half + 1) * 32]
-                    nc.vector.tensor_copy(pages[0][:].indirect(part), weighted[0][:, half * BANK : (half + 1) * BANK])
-            else:
-                nc.vector.tensor_copy(pages[i % 2][:].indirect(list2[:]), weighted[i][:])
+            nc.vector.tensor_copy(pages[i % 2][:].indirect(list2[:]), weighted[i][:])
 
         def staffed(i):
             b, t = divmod(i, PACK)
             loaded = held.tile([P, T2], F32, name="loaded", tag="slot%d" % ((i - 1) % SLOTS), align_bytes=64)
-            nc.scalar.activation(loaded[:], pages[i % 2][:], ACT.Identity, bias=load_sb[:, b, t : t + 1])
-            nc.gpsimd.tensor_tensor(
-                z_rows[b][:, :, t, :], loaded[:].rearrange("p (c j) -> p c j", j=BANK),
-                staff_sb[i][:].rearrange("p (c j) -> p c j", j=BANK), ALU.mult,
-            )
+            parts = 2 if i == ROW_TILES - 2 else 1
+            for u in range(parts):
+                cols = slice(u * T2 // parts, (u + 1) * T2 // parts)
+                nc.scalar.activation(loaded[:, cols], pages[i % 2][:, cols], ACT.Identity, bias=load_sb[:, b, t : t + 1])
+                nc.gpsimd.tensor_tensor(
+                    z_rows[b][:, u * CHUNKS // parts : (u + 1) * CHUNKS // parts, t, :],
+                    loaded[:, cols].rearrange("p (c j) -> p c j", j=BANK),
+                    staff_sb[i][:, cols].rearrange("p (c j) -> p c j", j=BANK), ALU.mult,
+                )
 
         def staffed_last(i, c):
             b, t = divmod(i, PACK)
@@ -223,6 +222,8 @@ def tile_list_theatre_turnover_slots_kernel(
             z_grouped[0, c] = halves[c // 2][:, c % 2]
         scores(0)
         scores(1)
+        crew_odd = held.tile([P, T2], F32, name="crew_odd", tag="crew1", align_bytes=64)
+        nc.gpsimd.memset(crew_odd[:], 0.0)
         for i in range(ROW_TILES):
             place(i)
             if i + 2 <= last:
@@ -271,21 +272,21 @@ def tile_list_theatre_turnover_slots_kernel(
         floored = {}
 
         def pick(n):
-            picked = held.tile([P, PK], F32, name="picked", tag="slot%d" % (3 + n % 2), align_bytes=64)
+            picked = held.tile([P, PK], F32, name="picked", tag="slot%d" % (1 + n % 2), align_bytes=64)
             nc.vector.tensor_tensor(picked[:], y_sb[n][:].indirect(list3[:]), delay_sb[n][:], ALU.add)
             return picked
 
         def floor(n, picked):
             above = held.tile([P, PK], F32, name="above", tag="slot0", align_bytes=64)
             nc.scalar.activation(above[:], picked[:], ACT.Relu, bias=neg_low[:, n : n + 1])
-            floored[n] = tail.tile([P, PK], F32, name="floored", tag="floored%d" % (n % 2))
+            floored[n] = held.tile([P, PK], F32, name="floored", tag="grouped%d" % (n % 2), align_bytes=64)
             nc.scalar.activation(floored[n][:], above[:], ACT.Identity, bias=low_sb[:, n : n + 1])
 
         def hand_over(n):
             nc.vector.tensor_tensor(crew[n % 2][:].indirect(list4[:]), floored[n][:], wgo_sb[:], ALU.mult)
             nc.sync.dma_start(out[n * P : (n + 1) * P, :], crew[n % 2][:])
 
-        crew = [tail.tile([P, T2], F32, name="crew", tag="chunk1", align_bytes=64)]
+        crew = [tail.tile([P, T2], F32, name="crew", tag="chunk1", align_bytes=64), crew_odd]
         nc.vector.memset(crew[0][:], 0.0)
         picked = {0: pick(0)}
         for n in range(OUT_TILES):
@@ -293,9 +294,6 @@ def tile_list_theatre_turnover_slots_kernel(
                 for c in (0, 3, 2, 1):
                     features(n + 1, c)
                 picked[n + 1] = pick(n + 1)
-            if n + 2 == OUT_TILES:
-                crew.append(held.tile([P, T2], F32, name="crew", tag="z_codes1", align_bytes=64))
-                nc.gpsimd.memset(crew[1][:], 0.0)
             if n > 0:
                 hand_over(n - 1)
             floor(n, picked[n])

@@ -147,7 +147,7 @@ def tile_list_theatre_turnover_slots_kernel(
         for n in range(OUT_TILES):
             nc.sync.dma_start(delay_sb[n][:], delay[n * P : (n + 1) * P, :])
 
-        z_rows = [ring.tile([P, CHUNKS, PACK, BANK], BF16, name="z_rows", tag="z_rows", align_bytes=64) for b in range(PASSES)]
+        z_pairs = [ring.tile([P, CHUNKS, 2, BANK, 2], BF16, name="z_pairs", tag="z_pairs", align_bytes=64) for b in range(PASSES)]
         z_codes = [held.tile([P, T2], U32, name="z_codes", tag="z_codes%d" % b, align_bytes=64) for b in range(PASSES)]
         weighted = {}
         z_grouped = {}
@@ -190,28 +190,22 @@ def tile_list_theatre_turnover_slots_kernel(
                 cols = slice(u * T2 // parts, (u + 1) * T2 // parts)
                 nc.scalar.activation(loaded[:, cols], pages[i % 2][:, cols], ACT.Identity, bias=load_sb[:, b, t : t + 1])
                 nc.gpsimd.tensor_tensor(
-                    z_rows[b][:, u * CHUNKS // parts : (u + 1) * CHUNKS // parts, t, :],
+                    z_pairs[b][:, u * CHUNKS // parts : (u + 1) * CHUNKS // parts, t // 2, :, t % 2],
                     loaded[:, cols].rearrange("p (c j) -> p c j", j=BANK),
                     staff_sb[i][:, cols].rearrange("p (c j) -> p c j", j=BANK), ALU.mult,
                 )
 
-        def staffed_last(i, c):
-            b, t = divmod(i, PACK)
+        def interleave(b, c):
+            nc.scalar.copy(
+                z_grouped[b, c].rearrange("p j t -> p (j t)").bitcast(U32).rearrange("p (j u) -> p j u", u=2),
+                z_pairs[b][:, c].rearrange("p u j e -> p u (j e)").bitcast(U32).rearrange("p u j -> p j u"),
+            )
+
+        def quantise_z(b, c):
             cols = slice(c * BANK, (c + 1) * BANK)
-            nc.vector.scalar_tensor_tensor(
-                z_rows[b][:, c, t, :], pages[i % 2][:, cols], load_sb[:, b, t : t + 1], staff_sb[i][:, cols], ALU.add, ALU.mult,
-            )
-
-        def interleave(b, c, engine_copy):
-            engine_copy(
-                z_grouped[b, c].rearrange("p (c i) t -> p c t i", i=4),
-                z_rows[b][:, c].rearrange("p t (c i) -> p c t i", i=4),
-            )
-
-        def quantise_z(b, cols, grouped):
             nc.vector.quantize_mx(
                 out=z_codes[b][:, cols].bitcast(FP8X4), scales=z_planes[b][:, cols],
-                in_=grouped,
+                in_=z_grouped[b, c].rearrange("p j t -> p (j t)"),
             )
 
         last = ROW_TILES - 1
@@ -233,7 +227,7 @@ def tile_list_theatre_turnover_slots_kernel(
             if i + 3 <= last:
                 load_staff(i + 3)
             for c in {4: (0, 1), 5: (2,), 6: (3,)}.get(i, ()):
-                interleave(0, c, nc.scalar.copy)
+                interleave(0, c)
         for c in range(CHUNKS):
             z_grouped[1, c] = tail.tile([P, BANK, PACK], BF16, name="z_chunk", tag="chunk%d" % c, align_bytes=64)[:]
         z_planes[0] = held.tile([P, T2], U8, name="z_planes0", tag="slot%d" % (last % SLOTS), align_bytes=64)
@@ -251,28 +245,28 @@ def tile_list_theatre_turnover_slots_kernel(
                 )
             nc.scalar.copy(y_sb[n][:, cols], acc[:])
 
+        loaded_last = held.tile([P, T2], F32, name="loaded", tag="slot%d" % ((last - 2) % SLOTS), align_bytes=64)
         for c in range(CHUNKS):
-            staffed_last(last, c)
-        def quantise_chunk(c):
-            quantise_z(1, slice(c * BANK, (c + 1) * BANK), z_grouped[1, c].rearrange("p j t -> p (j t)"))
-
-        interleave(1, 0, nc.scalar.copy)
-        interleave(1, 1, nc.scalar.copy)
-        for u in range(2):
-            quantise_z(0, slice(2 * u * BANK, 2 * (u + 1) * BANK), halves[u][:].rearrange("p c j t -> p (c j t)"))
-        interleave(1, 3, nc.vector.tensor_copy)
-        quantise_chunk(0)
-        interleave(1, 2, nc.vector.tensor_copy)
-        quantise_chunk(3)
-        quantise_chunk(2)
-        quantise_chunk(1)
-        for c in (0, 3, 2, 1):
+            cols = slice(c * BANK, (c + 1) * BANK)
+            nc.scalar.activation(
+                loaded_last[:, cols], pages[last % 2][:, cols], ACT.Identity, bias=load_sb[:, PASSES - 1, PACK - 1 : PACK]
+            )
+        quantise_z(0, 0)
+        for c in range(CHUNKS):
+            cols = slice(c * BANK, (c + 1) * BANK)
+            nc.vector.tensor_tensor(z_pairs[1][:, c, 1, :, 1], loaded_last[:, cols], staff_sb[last][:, cols], ALU.mult)
+        for c in range(CHUNKS):
+            interleave(1, c)
+        for c in range(CHUNKS):
+            if c > 0:
+                quantise_z(0, c)
+            quantise_z(1, c)
             features(0, c)
 
         floored = {}
 
         def pick(n):
-            picked = held.tile([P, PK], F32, name="picked", tag="slot%d" % (1 + n % 2), align_bytes=64)
+            picked = held.tile([P, PK], F32, name="picked", tag="slot%d" % (2 - n % 2), align_bytes=64)
             nc.vector.tensor_tensor(picked[:], y_sb[n][:].indirect(list3[:]), delay_sb[n][:], ALU.add)
             return picked
 
@@ -286,12 +280,12 @@ def tile_list_theatre_turnover_slots_kernel(
             nc.vector.tensor_tensor(crew[n % 2][:].indirect(list4[:]), floored[n][:], wgo_sb[:], ALU.mult)
             nc.sync.dma_start(out[n * P : (n + 1) * P, :], crew[n % 2][:])
 
-        crew = [tail.tile([P, T2], F32, name="crew", tag="chunk1", align_bytes=64), crew_odd]
+        crew = [tail.tile([P, T2], F32, name="crew", tag="chunk3", align_bytes=64), crew_odd]
         nc.vector.memset(crew[0][:], 0.0)
         picked = {0: pick(0)}
         for n in range(OUT_TILES):
             if n + 1 < OUT_TILES:
-                for c in (0, 3, 2, 1):
+                for c in range(CHUNKS):
                     features(n + 1, c)
                 picked[n + 1] = pick(n + 1)
             if n > 0:

@@ -23,7 +23,7 @@ PASSES = H // (P * PACK)
 ROW_TILES = PASSES * PACK
 CHUNKS = T2 // BANK
 OUT_TILES = N // P
-SLOTS = 4
+SLOTS = 2
 
 
 def tile_list_theatre_turnover_slots_kernel(
@@ -34,6 +34,7 @@ def tile_list_theatre_turnover_slots_kernel(
     with ExitStack() as ctx:
         held = ctx.enter_context(tc.tile_pool(name="held", bufs=1))
         ring = ctx.enter_context(tc.tile_pool(name="ring", bufs=2))
+        zeroed = ctx.enter_context(tc.tile_pool(name="zeroed", bufs=1))
         psum = ctx.enter_context(tc.psum_pool(name="psum", bufs=8))
 
         def load_list(source, name):
@@ -45,11 +46,11 @@ def tile_list_theatre_turnover_slots_kernel(
             for r in range(4):
                 nc.sync.dma_start(plane[r:P:32].bitcast(I32), rows[r:16:4].bitcast(I32))
 
-        v_words = held.tile([P, S], U32, align_bytes=64)
+        v_words = []
         v_scales = held.tile([P, S], U8, align_bytes=64)
         w1_codes = [held.tile([P, BANK], U32, name="w1_codes%d" % b, align_bytes=64) for b in range(PASSES)]
         w1_planes = [held.tile([P, BANK], U8, name="w1_planes%d" % b, align_bytes=64) for b in range(PASSES)]
-        pages = [held.tile([P, T2], F32, name="page%d" % u) for u in range(2)]
+        pages = [held.tile([P, T2], F32, name="page0")]
         w2_codes = held.tile([P, 2 * H], U8, align_bytes=64)
         w2_planes = held.tile([P, H], U8, align_bytes=64)
         staff_rows = staff.rearrange("(b p t) c -> b t p c", p=P, t=PACK)
@@ -69,60 +70,86 @@ def tile_list_theatre_turnover_slots_kernel(
             nc.sync.dma_start(staff_sb[i][:], staff_rows[i // PACK, i % PACK])
 
         tab_s = ring.tile([P, T], U8, name="tab_s", tag="wide", bufs=3, align_bytes=64)
-        w1_grouped = [
-            held.tile([P, PACK * BANK], BF16, name="w1_grouped", tag="grouped0", align_bytes=64),
-            ring.tile([P, PACK * BANK], BF16, name="w1_grouped", tag="wide", bufs=3, align_bytes=64),
-        ]
         w2_s_raw = ring.tile([P, H], U8, name="w2_s_raw", tag="wide", bufs=3, align_bytes=64)
+        w1_raw = [
+            held.tile([P, PACK, BANK], F32, name="w1_raw", tag="z_codes1", align_bytes=64),
+            held.tile([P, PACK, BANK], F32, name="w1_raw", tag="z_codes0", align_bytes=64),
+        ]
+        w1_grouped = {
+            (0, 0): held.tile([P, 2 * BANK], BF16, name="w1_grouped", tag="v_words1", align_bytes=64),
+            (0, 2): held.tile([P, 2 * BANK], BF16, name="w1_grouped", tag="grouped0", align_bytes=64),
+            (1, 0): held.tile([P, PACK * BANK], BF16, name="w1_grouped", tag="grouped1", align_bytes=64),
+        }
 
-        def load_w1(b):
-            raw = held.tile([P, PACK, BANK], F32, name="w1_raw", tag="gains%d" % b)
-            nc.sync.dma_start(raw[:], w1[:, b * BANK : (b + 1) * BANK].rearrange("(p j) c -> p j c", j=PACK))
-            nc.scalar.copy(
-                w1_grouped[b][:].rearrange("p (t m j) -> p m t j", t=PACK, j=PACK),
-                raw[:].rearrange("p j (m t) -> p m t j", t=PACK),
+        def load_w1(b, quarters):
+            cols = slice(quarters.start * P, quarters.stop * P)
+            nc.sync.dma_start(
+                w1_raw[b][:, :, cols], w1[:, b * BANK : (b + 1) * BANK].rearrange("(p j) c -> p j c", j=PACK)[:, :, cols]
             )
 
-        def quantise_w1(b):
-            nc.vector.quantize_mx(out=w1_codes[b][:].bitcast(FP8X4), scales=w1_planes[b][:], in_=w1_grouped[b][:])
+        def round_w1(b, ts, quarters, engine_copy):
+            ms = slice(quarters.start * 32, quarters.stop * 32)
+            engine_copy(
+                w1_grouped[b, ts.start][:].rearrange("p (t m j) -> p m t j", m=P, j=PACK)[:, ms],
+                w1_raw[b][:].rearrange("p j (m t) -> p m t j", t=PACK)[:, ms, ts],
+            )
 
+        def quantise_w1(b, ts):
+            cols = slice(ts.start * P, ts.stop * P)
+            nc.vector.quantize_mx(
+                out=w1_codes[b][:, cols].bitcast(FP8X4), scales=w1_planes[b][:, cols], in_=w1_grouped[b, ts.start][:],
+            )
+
+        def order_w2(b, ts):
+            nc.vector.tensor_copy(
+                w2_planes[:, b * BANK : (b + 1) * BANK].rearrange("p (t m) -> p t m", t=PACK)[:, ts],
+                w2_s_raw[:, b * BANK : (b + 1) * BANK].rearrange("p (m t) -> p t m", t=PACK)[:, ts],
+            )
+
+        FIRST, SECOND, ALL = slice(0, 2), slice(2, 4), slice(0, 4)
         with tc.tile_pool(name="head", bufs=1) as head:
-            w2_raw = head.tile([P, 2 * H], U8)
+            w2_raw = zeroed.tile([P, 2 * H], U8, name="w2_raw", offset=4 * T2 - H)
             tab_w = head.tile([P, T], U32)
-            nc.vector.memset(tab_s[:].bitcast(I32), 0)
+            nc.vector.memset(tab_s[:, : T // 2].bitcast(I32), 0)
+            nc.gpsimd.memset(tab_s[:, T // 2 :].bitcast(I32), 0)
             nc.gpsimd.memset(w2_s_raw[:].bitcast(I32), 0)
-            load_w1(0)
-            load_scale_rows(tab_s, tab_scales[0])
+            load_w1(0, FIRST)
             list1 = load_list(offs, "list1")
             nc.sync.dma_start(w2_raw[:].bitcast(I32), w2_words[0].bitcast(I32))
-            load_w1(1)
-            load_scale_rows(w2_s_raw, w2_scales[0])
+            load_scale_rows(tab_s, tab_scales[0])
             nc.sync.dma_start(tab_w[:].bitcast(I32), tab_words[0].rearrange("p t i -> p (t i)").bitcast(I32))
+            load_scale_rows(w2_s_raw, w2_scales[0])
+            load_w1(0, SECOND)
+            nc.vector.memset(pages[0][:], 0.0)
             nc.vector.tensor_copy(
                 w2_codes[:].bitcast(U16).rearrange("p (b t m) -> p b t m", b=PASSES, t=PACK),
                 w2_raw[:].bitcast(U16).rearrange("p (b m t) -> p b t m", b=PASSES, t=PACK),
             )
+            crew_odd = held.tile([P, T2], F32, name="crew_odd")
+            nc.vector.memset(crew_odd[:], 0.0)
+            pages.append(zeroed.tile([P, T2], F32, name="page1", offset=0))
+            nc.gpsimd.memset(pages[1][:], 0.0)
+            crew_even = zeroed.tile([P, T2], F32, name="crew_even", offset=4 * T2)
+            nc.gpsimd.memset(crew_even[:], 0.0)
+            nc.vector.tensor_copy(v_scales[:], tab_s[:].indirect(list1[:]))
+            round_w1(0, FIRST, FIRST, nc.scalar.copy)
+            round_w1(0, SECOND, FIRST, nc.scalar.copy)
 
-            def order_w2(b):
-                nc.vector.tensor_copy(
-                    w2_planes[:, b * BANK : (b + 1) * BANK].rearrange("p (t m) -> p t m", t=PACK),
-                    w2_s_raw[:, b * BANK : (b + 1) * BANK].rearrange("p (m t) -> p t m", t=PACK),
-                )
+            def gather_words(half):
+                v_words.append(held.tile([P, BANK], U32, name="v_words%d" % half, align_bytes=64))
+                nc.vector.tensor_copy(v_words[half][:], tab_w[:].indirect(list1[:, half * 32 : (half + 1) * 32]))
 
-            for half in range(S // BANK):
-                cols = slice(half * BANK, (half + 1) * BANK)
-                part = list1[:, half * 32 : (half + 1) * 32]
-                nc.vector.tensor_copy(v_words[:, cols], tab_w[:].indirect(part))
-                nc.vector.tensor_copy(v_scales[:, cols], tab_s[:].indirect(part))
-                order_w2(half)
-                quantise_w1(half)
-            for page in pages:
-                nc.vector.memset(page[:], 0.0)
+            gather_words(0)
+            order_w2(0, FIRST)
+            round_w1(0, FIRST, SECOND, nc.vector.tensor_copy)
+            quantise_w1(0, FIRST)
+            gather_words(1)
             load_gains(0, 1, "gains_first")
             list2 = load_list(offs2, "list2")
+            load_gains(1, 1, "gains0")
             load_sb = held.tile([P, PASSES, PACK], F32)
             nc.sync.dma_start(load_sb[:], load.rearrange("(b p t) -> p b t", p=P, t=PACK))
-            load_gains(1, 1, "gains0")
+            load_w1(1, ALL)
             load_staff(0)
             load_gains(2, 2, "gains1")
             load_staff(1)
@@ -141,7 +168,6 @@ def tile_list_theatre_turnover_slots_kernel(
         list4 = load_list(offs4, "list4")
         with nc.allow_non_contiguous_dma(reason="one value a partition"):
             nc.sync.dma_start(low_sb[:], low.rearrange("(n p) -> p n", p=P))
-        nc.scalar.activation(neg_low[:], low_sb[:], ACT.Copy, scale=-1.0)
         nc.sync.dma_start(wgo_sb[:], wgo)
         delay_sb = [tail.tile([P, PK], F32, name="delay%d" % n) for n in range(OUT_TILES)]
         for n in range(OUT_TILES):
@@ -150,42 +176,50 @@ def tile_list_theatre_turnover_slots_kernel(
         z_pairs = [ring.tile([P, CHUNKS, 2, BANK, 2], BF16, name="z_pairs", tag="z_pairs", align_bytes=64) for b in range(PASSES)]
         z_codes = [held.tile([P, T2], U32, name="z_codes", tag="z_codes%d" % b, align_bytes=64) for b in range(PASSES)]
         weighted = {}
+        largers = {}
         z_grouped = {}
         z_planes = {}
 
         def scores(i):
             cols = slice(i * P, (i + 1) * P)
             b, t = divmod(i, PACK)
-            larger = held.tile([P, S], F32, name="larger", tag="slot%d" % ((i - 2) % SLOTS) if i != 1 else "crew1", align_bytes=64)
-            weighted[i] = held.tile([P, S], F32, name="weighted", tag="slot%d" % (i % SLOTS), align_bytes=64)
+            larger = held.tile([P, S], F32, name="larger", tag="larger%d" % (i % 2), align_bytes=64)
+            largers[i] = larger
+            if i < 2:
+                weighted[i] = held.tile([P, S], F32, name="weighted", tag="slot%d" % (i % SLOTS), align_bytes=64)
             for half in range(S // BANK):
                 js = slice(half * BANK, (half + 1) * BANK)
                 team = psum.tile([P, BANK], F32, name="team", tag="bank")
                 nc.tensor.matmul_mx(
                     out=team[:], lhsT=w2_codes[:, 2 * i * P : 2 * (i + 1) * P].bitcast(FP4X4), lhsT_scale=w2_planes[:, cols],
-                    rhs=v_words[:, js].bitcast(FP8X4), rhs_scale=v_scales[:, js], start=True, stop=True,
+                    rhs=v_words[half][:].bitcast(FP8X4), rhs_scale=v_scales[:, js], start=True, stop=True,
                 )
                 room = psum.tile([P, BANK], F32, name="room", tag="bank")
                 nc.tensor.matmul_mx(
                     out=room[:], lhsT=w1_codes[b][:, t * P : (t + 1) * P].bitcast(FP8X4),
                     lhsT_scale=w1_planes[b][:, t * P : (t + 1) * P],
-                    rhs=v_words[:, js].bitcast(FP8X4), rhs_scale=v_scales[:, js], start=True, stop=True,
+                    rhs=v_words[half][:].bitcast(FP8X4), rhs_scale=v_scales[:, js], start=True, stop=True,
                 )
-                team_sb = ring.tile([P, BANK], F32, name="team_sb", tag="team_sb", bufs=3)
+                team_sb = ring.tile([P, BANK], F32, name="team_sb", tag="team_sb", bufs=4)
                 nc.scalar.copy(team_sb[:], team[:])
                 nc.vector.tensor_tensor(larger[:, js], room[:], team_sb[:], ALU.max)
                 if i == 0:
                     nc.gpsimd.tensor_tensor(weighted[i][:, js], larger[:, js], gains[t][:, js], ALU.mult)
-            if i > 0:
-                nc.gpsimd.tensor_tensor(weighted[i][:], larger[:], gains[t], ALU.mult)
+            if i == 1:
+                weigh(i)
+
+        def weigh(i):
+            if i > 1:
+                weighted[i] = held.tile([P, S], F32, name="weighted", tag="slot%d" % (i % SLOTS), align_bytes=64)
+            nc.gpsimd.tensor_tensor(weighted[i][:], largers[i][:], gains[i % PACK], ALU.mult)
 
         def place(i):
             nc.vector.tensor_copy(pages[i % 2][:].indirect(list2[:]), weighted[i][:])
 
         def staffed(i):
             b, t = divmod(i, PACK)
-            loaded = held.tile([P, T2], F32, name="loaded", tag="slot%d" % ((i - 1) % SLOTS), align_bytes=64)
-            parts = 2 if i == ROW_TILES - 2 else 1
+            loaded = held.tile([P, T2], F32, name="loaded", tag="slot%d" % (i % SLOTS), align_bytes=64)
+            parts = 1 if i == 1 else 2
             for u in range(parts):
                 cols = slice(u * T2 // parts, (u + 1) * T2 // parts)
                 nc.scalar.activation(loaded[:, cols], pages[i % 2][:, cols], ACT.Identity, bias=load_sb[:, b, t : t + 1])
@@ -216,17 +250,23 @@ def tile_list_theatre_turnover_slots_kernel(
             z_grouped[0, c] = halves[c // 2][:, c % 2]
         scores(0)
         scores(1)
-        crew_odd = held.tile([P, T2], F32, name="crew_odd", tag="crew1", align_bytes=64)
-        nc.gpsimd.memset(crew_odd[:], 0.0)
+        round_w1(0, SECOND, SECOND, nc.scalar.copy)
+        round_w1(1, ALL, ALL, nc.scalar.copy)
+        order_w2(0, SECOND)
+        order_w2(1, ALL)
+        quantise_w1(0, SECOND)
         for i in range(ROW_TILES):
             place(i)
-            if i + 2 <= last:
-                scores(i + 2)
             if i < last:
                 staffed(i)
+            if i + 2 <= last:
+                if i + 2 == PACK:
+                    quantise_w1(1, ALL)
+                scores(i + 2)
+                weigh(i + 2)
             if i + 3 <= last:
                 load_staff(i + 3)
-            for c in {4: (0, 1), 5: (2,), 6: (3,)}.get(i, ()):
+            for c in {4: (0, 1), 5: (2, 3)}.get(i, ()):
                 interleave(0, c)
         for c in range(CHUNKS):
             z_grouped[1, c] = tail.tile([P, BANK, PACK], BF16, name="z_chunk", tag="chunk%d" % c, align_bytes=64)[:]
@@ -245,7 +285,7 @@ def tile_list_theatre_turnover_slots_kernel(
                 )
             nc.scalar.copy(y_sb[n][:, cols], acc[:])
 
-        loaded_last = held.tile([P, T2], F32, name="loaded", tag="slot%d" % ((last - 2) % SLOTS), align_bytes=64)
+        loaded_last = held.tile([P, T2], F32, name="loaded", tag="slot%d" % ((last - 1) % SLOTS), align_bytes=64)
         for c in range(CHUNKS):
             cols = slice(c * BANK, (c + 1) * BANK)
             nc.scalar.activation(
@@ -263,15 +303,16 @@ def tile_list_theatre_turnover_slots_kernel(
             quantise_z(1, c)
             features(0, c)
 
+        nc.scalar.activation(neg_low[:], low_sb[:], ACT.Copy, scale=-1.0)
         floored = {}
 
         def pick(n):
-            picked = held.tile([P, PK], F32, name="picked", tag="slot%d" % (2 - n % 2), align_bytes=64)
+            picked = held.tile([P, PK], F32, name="picked", tag="larger%d" % (n % 2), align_bytes=64)
             nc.vector.tensor_tensor(picked[:], y_sb[n][:].indirect(list3[:]), delay_sb[n][:], ALU.add)
             return picked
 
         def floor(n, picked):
-            above = held.tile([P, PK], F32, name="above", tag="slot0", align_bytes=64)
+            above = held.tile([P, PK], F32, name="above", tag="page0")
             nc.scalar.activation(above[:], picked[:], ACT.Relu, bias=neg_low[:, n : n + 1])
             floored[n] = held.tile([P, PK], F32, name="floored", tag="grouped%d" % (n % 2), align_bytes=64)
             nc.scalar.activation(floored[n][:], above[:], ACT.Identity, bias=low_sb[:, n : n + 1])
@@ -280,8 +321,7 @@ def tile_list_theatre_turnover_slots_kernel(
             nc.vector.tensor_tensor(crew[n % 2][:].indirect(list4[:]), floored[n][:], wgo_sb[:], ALU.mult)
             nc.sync.dma_start(out[n * P : (n + 1) * P, :], crew[n % 2][:])
 
-        crew = [tail.tile([P, T2], F32, name="crew", tag="chunk3", align_bytes=64), crew_odd]
-        nc.vector.memset(crew[0][:], 0.0)
+        crew = [crew_even, crew_odd]
         picked = {0: pick(0)}
         for n in range(OUT_TILES):
             if n + 1 < OUT_TILES:

@@ -65,9 +65,13 @@ def tile_list_theatre_turnover_slots_kernel(
                 nc.sync.dma_start(rows[32 * g : 32 * (g + 1)], wgs_rows[:, first : first + count])
             gains.extend([rows[:, u] for u in range(count)])
 
+        def pass_and_byte(i):
+            b, s = divmod(i, PACK)
+            return b, (s if b == 0 else (0, 2, 1, 3)[s])
+
         def load_staff(i):
             staff_sb[i] = ring.tile([P, T2], F32, name="staff", tag="wide", bufs=3, align_bytes=64)
-            nc.sync.dma_start(staff_sb[i][:], staff_rows[i // PACK, i % PACK])
+            nc.sync.dma_start(staff_sb[i][:], staff_rows[pass_and_byte(i)])
 
         tab_s = ring.tile([P, T], U8, name="tab_s", tag="wide", bufs=3, align_bytes=64)
         w2_s_raw = ring.tile([P, H], U8, name="w2_s_raw", tag="wide", bufs=3, align_bytes=64)
@@ -181,8 +185,8 @@ def tile_list_theatre_turnover_slots_kernel(
         z_planes = {}
 
         def scores(i):
-            cols = slice(i * P, (i + 1) * P)
-            b, t = divmod(i, PACK)
+            b, t = pass_and_byte(i)
+            cols = slice((b * PACK + t) * P, (b * PACK + t + 1) * P)
             larger = held.tile([P, S], F32, name="larger", tag="larger%d" % (i % 2), align_bytes=64)
             largers[i] = larger
             if i < 2:
@@ -191,7 +195,7 @@ def tile_list_theatre_turnover_slots_kernel(
                 js = slice(half * BANK, (half + 1) * BANK)
                 team = psum.tile([P, BANK], F32, name="team", tag="bank")
                 nc.tensor.matmul_mx(
-                    out=team[:], lhsT=w2_codes[:, 2 * i * P : 2 * (i + 1) * P].bitcast(FP4X4), lhsT_scale=w2_planes[:, cols],
+                    out=team[:], lhsT=w2_codes[:, 2 * cols.start : 2 * cols.stop].bitcast(FP4X4), lhsT_scale=w2_planes[:, cols],
                     rhs=v_words[half][:].bitcast(FP8X4), rhs_scale=v_scales[:, js], start=True, stop=True,
                 )
                 room = psum.tile([P, BANK], F32, name="room", tag="bank")
@@ -211,13 +215,13 @@ def tile_list_theatre_turnover_slots_kernel(
         def weigh(i):
             if i > 1:
                 weighted[i] = held.tile([P, S], F32, name="weighted", tag="slot%d" % (i % SLOTS), align_bytes=64)
-            nc.gpsimd.tensor_tensor(weighted[i][:], largers[i][:], gains[i % PACK], ALU.mult)
+            nc.gpsimd.tensor_tensor(weighted[i][:], largers[i][:], gains[pass_and_byte(i)[1]], ALU.mult)
 
         def place(i):
             nc.vector.tensor_copy(pages[i % 2][:].indirect(list2[:]), weighted[i][:])
 
         def staffed(i):
-            b, t = divmod(i, PACK)
+            b, t = pass_and_byte(i)
             loaded = held.tile([P, T2], F32, name="loaded", tag="slot%d" % (i % SLOTS), align_bytes=64)
             parts = 1 if i == 1 else 2
             for u in range(parts):
@@ -285,50 +289,63 @@ def tile_list_theatre_turnover_slots_kernel(
                 )
             nc.scalar.copy(y_sb[n][:, cols], acc[:])
 
-        loaded_last = held.tile([P, T2], F32, name="loaded", tag="slot%d" % ((last - 1) % SLOTS), align_bytes=64)
         for c in range(CHUNKS):
             cols = slice(c * BANK, (c + 1) * BANK)
-            nc.scalar.activation(
-                loaded_last[:, cols], pages[last % 2][:, cols], ACT.Identity, bias=load_sb[:, PASSES - 1, PACK - 1 : PACK]
+            nc.vector.scalar_tensor_tensor(
+                z_pairs[1][:, c, 1, :, 1], pages[last % 2][:, cols], load_sb[:, PASSES - 1, PACK - 1 : PACK],
+                staff_sb[last][:, cols], ALU.add, ALU.mult,
             )
-        quantise_z(0, 0)
-        for c in range(CHUNKS):
-            cols = slice(c * BANK, (c + 1) * BANK)
-            nc.vector.tensor_tensor(z_pairs[1][:, c, 1, :, 1], loaded_last[:, cols], staff_sb[last][:, cols], ALU.mult)
         for c in range(CHUNKS):
             interleave(1, c)
         for c in range(CHUNKS):
-            if c > 0:
-                quantise_z(0, c)
+            quantise_z(0, c)
             quantise_z(1, c)
             features(0, c)
+            features(1, c)
 
         nc.scalar.activation(neg_low[:], low_sb[:], ACT.Copy, scale=-1.0)
-        floored = {}
+        picked_tags = ("larger0", "larger1", "gains0")
+        swap_tags = ("gains1", "gains_first")
+        HALVES = [slice(u * BANK, (u + 1) * BANK) for u in range(2)]
+        picked, final = {}, {}
 
-        def pick(n):
-            picked = held.tile([P, PK], F32, name="picked", tag="larger%d" % (n % 2), align_bytes=64)
-            nc.vector.tensor_tensor(picked[:], y_sb[n][:].indirect(list3[:]), delay_sb[n][:], ALU.add)
-            return picked
+        def pick(n, parts):
+            picked[n] = held.tile([P, PK], F32, name="picked", tag=picked_tags[n], align_bytes=64 if n < 2 else 32)
+            width = PK // parts
+            for u in range(parts):
+                nc.vector.tensor_copy(
+                    picked[n][:, u * width : (u + 1) * width],
+                    y_sb[n][:].indirect(list3[:, u * width // 16 : (u + 1) * width // 16]),
+                )
 
-        def floor(n, picked):
+        def finish(n):
+            summed = held.tile([P, PK], F32, name="summed", tag=swap_tags[n % 2])
             above = held.tile([P, PK], F32, name="above", tag="page0")
-            nc.scalar.activation(above[:], picked[:], ACT.Relu, bias=neg_low[:, n : n + 1])
-            floored[n] = held.tile([P, PK], F32, name="floored", tag="grouped%d" % (n % 2), align_bytes=64)
-            nc.scalar.activation(floored[n][:], above[:], ACT.Identity, bias=low_sb[:, n : n + 1])
+            floored = held.tile([P, PK], F32, name="floored", tag=swap_tags[(n + 1) % 2])
+            final[n] = held.tile([P, PK], F32, name="final", tag="grouped%d" % (n % 2), align_bytes=64)
+            for js in HALVES:
+                nc.gpsimd.tensor_tensor(summed[:, js], picked[n][:, js], delay_sb[n][:, js], ALU.add)
+            for js in HALVES:
+                nc.scalar.activation(above[:, js], summed[:, js], ACT.Relu, bias=neg_low[:, n : n + 1])
+                nc.scalar.activation(floored[:, js], above[:, js], ACT.Identity, bias=low_sb[:, n : n + 1])
+            for js in HALVES:
+                nc.gpsimd.tensor_tensor(final[n][:, js], floored[:, js], wgo_sb[:, js], ALU.mult)
 
-        def hand_over(n):
-            nc.vector.tensor_tensor(crew[n % 2][:].indirect(list4[:]), floored[n][:], wgo_sb[:], ALU.mult)
+        def hand_over(n, parts):
+            width = PK // parts
+            for u in range(parts):
+                nc.vector.tensor_copy(
+                    crew[n % 2][:].indirect(list4[:, u * width // 16 : (u + 1) * width // 16]),
+                    final[n][:, u * width : (u + 1) * width],
+                )
             nc.sync.dma_start(out[n * P : (n + 1) * P, :], crew[n % 2][:])
 
         crew = [crew_even, crew_odd]
-        picked = {0: pick(0)}
+        pick(0, 2)
+        pick(1, 1)
+        for c in range(CHUNKS):
+            features(2, c)
+        pick(2, 1)
         for n in range(OUT_TILES):
-            if n + 1 < OUT_TILES:
-                for c in range(CHUNKS):
-                    features(n + 1, c)
-                picked[n + 1] = pick(n + 1)
-            if n > 0:
-                hand_over(n - 1)
-            floor(n, picked[n])
-        hand_over(OUT_TILES - 1)
+            finish(n)
+            hand_over(n, 1)

@@ -24,6 +24,7 @@ ROW_TILES = PASSES * PACK
 CHUNKS = T2 // BANK
 OUT_TILES = N // P
 SLOTS = 2
+RESULT_BANKS = 4
 
 
 def tile_list_theatre_turnover_slots_kernel(
@@ -35,7 +36,7 @@ def tile_list_theatre_turnover_slots_kernel(
         held = ctx.enter_context(tc.tile_pool(name="held", bufs=1))
         ring = ctx.enter_context(tc.tile_pool(name="ring", bufs=2))
         zeroed = ctx.enter_context(tc.tile_pool(name="zeroed", bufs=1))
-        psum = ctx.enter_context(tc.psum_pool(name="psum", bufs=8))
+        psum = ctx.enter_context(tc.psum_pool(name="psum", bufs=1))
 
         def load_list(source, name):
             tile = held.tile([P, S // 16], U16, name=name)
@@ -193,12 +194,12 @@ def tile_list_theatre_turnover_slots_kernel(
                 weighted[i] = held.tile([P, S], F32, name="weighted", tag="slot%d" % (i % SLOTS), align_bytes=64)
             for half in range(S // BANK):
                 js = slice(half * BANK, (half + 1) * BANK)
-                team = psum.tile([P, BANK], F32, name="team", tag="bank")
+                team = psum.tile([P, BANK], F32, name="team", tag="bank%d" % (4 * (i % 2) + 2 * half))
                 nc.tensor.matmul_mx(
                     out=team[:], lhsT=w2_codes[:, 2 * cols.start : 2 * cols.stop].bitcast(FP4X4), lhsT_scale=w2_planes[:, cols],
                     rhs=v_words[half][:].bitcast(FP8X4), rhs_scale=v_scales[:, js], start=True, stop=True,
                 )
-                room = psum.tile([P, BANK], F32, name="room", tag="bank")
+                room = psum.tile([P, BANK], F32, name="room", tag="bank%d" % (4 * (i % 2) + 2 * half + 1))
                 nc.tensor.matmul_mx(
                     out=room[:], lhsT=w1_codes[b][:, t * P : (t + 1) * P].bitcast(FP8X4),
                     lhsT_scale=w1_planes[b][:, t * P : (t + 1) * P],
@@ -239,11 +240,12 @@ def tile_list_theatre_turnover_slots_kernel(
                 z_pairs[b][:, c].rearrange("p u j e -> p u (j e)").bitcast(U32).rearrange("p u j -> p j u"),
             )
 
-        def quantise_z(b, c):
-            cols = slice(c * BANK, (c + 1) * BANK)
+        def quantise_z(b, first, width):
+            cols = slice(first, first + width)
+            c, j = divmod(first, BANK)
             nc.vector.quantize_mx(
                 out=z_codes[b][:, cols].bitcast(FP8X4), scales=z_planes[b][:, cols],
-                in_=z_grouped[b, c].rearrange("p j t -> p (j t)"),
+                in_=z_grouped[b, c][:, j : j + width].rearrange("p j t -> p (j t)"),
             )
 
         last = ROW_TILES - 1
@@ -274,20 +276,24 @@ def tile_list_theatre_turnover_slots_kernel(
                 interleave(0, c)
         for c in range(CHUNKS):
             z_grouped[1, c] = tail.tile([P, BANK, PACK], BF16, name="z_chunk", tag="chunk%d" % c, align_bytes=64)[:]
-        z_planes[0] = held.tile([P, T2], U8, name="z_planes0", tag="slot%d" % (last % SLOTS), align_bytes=64)
+        z_planes[0] = held.tile([P, T2], U8, name="z_planes0", tag="larger%d" % (last % 2), align_bytes=64)
         z_planes[1] = held.tile([P, T2], U8, name="z_planes1", align_bytes=64)
 
         y_sb = [ring.tile([P, T2], F32, name="y", tag="wide", bufs=3, align_bytes=64) for n in range(OUT_TILES)]
 
-        def features(n, c):
-            cols = slice(c * BANK, (c + 1) * BANK)
-            acc = psum.tile([P, BANK], F32, name="acc", tag="bank")
+        sums = []
+
+        def features(n, first, width, engine_copy):
+            cols = slice(first, first + width)
+            acc = psum.tile([P, BANK], F32, name="acc", tag="bank%d" % (len(sums) % RESULT_BANKS))
+            sums.append(acc)
             for b in range(PASSES):
                 nc.tensor.matmul_mx(
-                    out=acc[:], lhsT=w3_codes[:, b, n * P : (n + 1) * P].bitcast(FP8X4), lhsT_scale=w3_planes[:, b, n * P : (n + 1) * P],
+                    out=acc[:, :width], lhsT=w3_codes[:, b, n * P : (n + 1) * P].bitcast(FP8X4),
+                    lhsT_scale=w3_planes[:, b, n * P : (n + 1) * P],
                     rhs=z_codes[b][:, cols].bitcast(FP8X4), rhs_scale=z_planes[b][:, cols], start=(b == 0), stop=(b == PASSES - 1),
                 )
-            nc.scalar.copy(y_sb[n][:, cols], acc[:])
+            engine_copy(y_sb[n][:, cols], acc[:, :width])
 
         for c in range(CHUNKS):
             cols = slice(c * BANK, (c + 1) * BANK)
@@ -298,54 +304,44 @@ def tile_list_theatre_turnover_slots_kernel(
         for c in range(CHUNKS):
             interleave(1, c)
         for c in range(CHUNKS):
-            quantise_z(0, c)
-            quantise_z(1, c)
-            features(0, c)
-            features(1, c)
+            quantise_z(0, c * BANK, BANK)
+            if c < CHUNKS - 1:
+                quantise_z(1, c * BANK, BANK)
+                features(0, c * BANK, BANK, nc.scalar.copy)
+            if c == 1:
+                features(1, 0, BANK, nc.scalar.copy)
+        pieces = ((T2 - BANK, 256, nc.scalar.copy), (T2 - 256, P, nc.vector.tensor_copy), (T2 - P, P, nc.vector.tensor_copy))
+        for first, width, engine_copy in pieces:
+            quantise_z(1, first, width)
+        for first, width, engine_copy in pieces:
+            features(0, first, width, engine_copy)
 
         nc.scalar.activation(neg_low[:], low_sb[:], ACT.Copy, scale=-1.0)
-        picked_tags = ("larger0", "larger1", "gains0")
-        swap_tags = ("gains1", "gains_first")
-        HALVES = [slice(u * BANK, (u + 1) * BANK) for u in range(2)]
-        picked, final = {}, {}
+        floored = {}
 
-        def pick(n, parts):
-            picked[n] = held.tile([P, PK], F32, name="picked", tag=picked_tags[n], align_bytes=64 if n < 2 else 32)
-            width = PK // parts
-            for u in range(parts):
-                nc.vector.tensor_copy(
-                    picked[n][:, u * width : (u + 1) * width],
-                    y_sb[n][:].indirect(list3[:, u * width // 16 : (u + 1) * width // 16]),
-                )
+        def pick(n):
+            picked = held.tile([P, PK], F32, name="picked", tag="slot%d" % (n % 2), align_bytes=64)
+            nc.vector.tensor_tensor(picked[:], y_sb[n][:].indirect(list3[:]), delay_sb[n][:], ALU.add)
+            return picked
 
-        def finish(n):
-            summed = held.tile([P, PK], F32, name="summed", tag=swap_tags[n % 2])
+        def floor(n, picked):
             above = held.tile([P, PK], F32, name="above", tag="page0")
-            floored = held.tile([P, PK], F32, name="floored", tag=swap_tags[(n + 1) % 2])
-            final[n] = held.tile([P, PK], F32, name="final", tag="grouped%d" % (n % 2), align_bytes=64)
-            for js in HALVES:
-                nc.gpsimd.tensor_tensor(summed[:, js], picked[n][:, js], delay_sb[n][:, js], ALU.add)
-            for js in HALVES:
-                nc.scalar.activation(above[:, js], summed[:, js], ACT.Relu, bias=neg_low[:, n : n + 1])
-                nc.scalar.activation(floored[:, js], above[:, js], ACT.Identity, bias=low_sb[:, n : n + 1])
-            for js in HALVES:
-                nc.gpsimd.tensor_tensor(final[n][:, js], floored[:, js], wgo_sb[:, js], ALU.mult)
+            nc.scalar.activation(above[:], picked[:], ACT.Relu, bias=neg_low[:, n : n + 1])
+            floored[n] = held.tile([P, PK], F32, name="floored", tag="grouped%d" % (n % 2), align_bytes=64)
+            nc.scalar.activation(floored[n][:], above[:], ACT.Identity, bias=low_sb[:, n : n + 1])
 
-        def hand_over(n, parts):
-            width = PK // parts
-            for u in range(parts):
-                nc.vector.tensor_copy(
-                    crew[n % 2][:].indirect(list4[:, u * width // 16 : (u + 1) * width // 16]),
-                    final[n][:, u * width : (u + 1) * width],
-                )
+        def hand_over(n):
+            nc.vector.tensor_tensor(crew[n % 2][:].indirect(list4[:]), floored[n][:], wgo_sb[:], ALU.mult)
             nc.sync.dma_start(out[n * P : (n + 1) * P, :], crew[n % 2][:])
 
         crew = [crew_even, crew_odd]
-        pick(0, 2)
-        pick(1, 1)
-        for c in range(CHUNKS):
-            features(2, c)
-        pick(2, 1)
+        picked = {0: pick(0)}
         for n in range(OUT_TILES):
-            finish(n)
-            hand_over(n, 1)
+            if n + 1 < OUT_TILES:
+                for c in range(1 if n == 0 else 0, CHUNKS):
+                    features(n + 1, c * BANK, BANK, nc.scalar.copy)
+                picked[n + 1] = pick(n + 1)
+            if n > 0:
+                hand_over(n - 1)
+            floor(n, picked[n])
+        hand_over(OUT_TILES - 1)

@@ -276,7 +276,7 @@ def tile_list_theatre_turnover_slots_kernel(
                 interleave(0, c)
         for c in range(CHUNKS):
             z_grouped[1, c] = tail.tile([P, BANK, PACK], BF16, name="z_chunk", tag="chunk%d" % c, align_bytes=64)[:]
-        z_planes[0] = held.tile([P, T2], U8, name="z_planes0", tag="larger%d" % (last % 2), align_bytes=64)
+        z_planes[0] = held.tile([P, T2], U8, name="z_planes0", tag="slot%d" % (last % SLOTS), align_bytes=64)
         z_planes[1] = held.tile([P, T2], U8, name="z_planes1", align_bytes=64)
 
         y_sb = [ring.tile([P, T2], F32, name="y", tag="wide", bufs=3, align_bytes=64) for n in range(OUT_TILES)]
@@ -320,7 +320,7 @@ def tile_list_theatre_turnover_slots_kernel(
         floored = {}
 
         def pick(n):
-            picked = held.tile([P, PK], F32, name="picked", tag="slot%d" % (n % 2), align_bytes=64)
+            picked = held.tile([P, PK], F32, name="picked", tag="larger%d" % (n % 2), align_bytes=64)
             nc.vector.tensor_tensor(picked[:], y_sb[n][:].indirect(list3[:]), delay_sb[n][:], ALU.add)
             return picked
 

@@ -23,7 +23,7 @@ PASSES = H // (P * PACK)
 ROW_TILES = PASSES * PACK
 CHUNKS = T2 // BANK
 OUT_TILES = N // P
-SLOTS = 2
+SLOTS = 3
 RESULT_BANKS = 4
 
 
@@ -68,7 +68,7 @@ def tile_list_theatre_turnover_slots_kernel(
 
         def pass_and_byte(i):
             b, s = divmod(i, PACK)
-            return b, (s if b == 0 else (0, 2, 1, 3)[s])
+            return b, (s if b == 0 else (2, 0, 1, 3)[s])
 
         def load_staff(i):
             staff_sb[i] = ring.tile([P, T2], F32, name="staff", tag="wide", bufs=3, align_bytes=64)
@@ -151,23 +151,26 @@ def tile_list_theatre_turnover_slots_kernel(
             gather_words(1)
             load_gains(0, 1, "gains_first")
             list2 = load_list(offs2, "list2")
-            load_gains(1, 1, "gains0")
+            load_gains(1, 2, "gains0")
             load_sb = held.tile([P, PASSES, PACK], F32)
             nc.sync.dma_start(load_sb[:], load.rearrange("(b p t) -> p b t", p=P, t=PACK))
             load_w1(1, ALL)
             load_staff(0)
-            load_gains(2, 2, "gains1")
+            load_gains(3, 1, "gains1")
             load_staff(1)
             load_staff(2)
 
         tail = ctx.enter_context(tc.tile_pool(name="tail", bufs=1))
-        w3_codes = tail.tile([P, PASSES, N], U32, align_bytes=64)
+        w3_codes = [tail.tile([P, PASSES, P], U32, name="w3_codes%d" % n, align_bytes=64) for n in range(OUT_TILES)]
         w3_planes = tail.tile([P, PASSES, N], U8, align_bytes=64)
         low_sb = tail.tile([P, OUT_TILES], F32)
         neg_low = tail.tile([P, OUT_TILES], F32)
         wgo_sb = tail.tile([P, PK], F32)
         nc.gpsimd.memset(w3_planes[:].bitcast(I32), 0)
-        nc.sync.dma_start(w3_codes[:].bitcast(I32), w3_words.rearrange("a p c i -> p a (c i)").bitcast(I32))
+        for n in range(OUT_TILES):
+            nc.sync.dma_start(
+                w3_codes[n][:].bitcast(I32), w3_words[:, :, n * P : (n + 1) * P].rearrange("a p c i -> p a (c i)").bitcast(I32)
+            )
         load_scale_rows(w3_planes, w3_scales.rearrange("a q c -> q a c"))
         list3 = load_list(offs3, "list3")
         list4 = load_list(offs4, "list4")
@@ -188,9 +191,9 @@ def tile_list_theatre_turnover_slots_kernel(
         def scores(i):
             b, t = pass_and_byte(i)
             cols = slice((b * PACK + t) * P, (b * PACK + t + 1) * P)
-            larger = held.tile([P, S], F32, name="larger", tag="larger%d" % (i % 2), align_bytes=64)
+            larger = held.tile([P, S], F32, name="larger", tag="larger%d" % (i % SLOTS), align_bytes=64)
             largers[i] = larger
-            if i < 2:
+            if i == 0:
                 weighted[i] = held.tile([P, S], F32, name="weighted", tag="slot%d" % (i % SLOTS), align_bytes=64)
             for half in range(S // BANK):
                 js = slice(half * BANK, (half + 1) * BANK)
@@ -210,12 +213,9 @@ def tile_list_theatre_turnover_slots_kernel(
                 nc.vector.tensor_tensor(larger[:, js], room[:], team_sb[:], ALU.max)
                 if i == 0:
                     nc.gpsimd.tensor_tensor(weighted[i][:, js], larger[:, js], gains[t][:, js], ALU.mult)
-            if i == 1:
-                weigh(i)
 
         def weigh(i):
-            if i > 1:
-                weighted[i] = held.tile([P, S], F32, name="weighted", tag="slot%d" % (i % SLOTS), align_bytes=64)
+            weighted[i] = held.tile([P, S], F32, name="weighted", tag="slot%d" % (i % SLOTS), align_bytes=64)
             nc.gpsimd.tensor_tensor(weighted[i][:], largers[i][:], gains[pass_and_byte(i)[1]], ALU.mult)
 
         def place(i):
@@ -256,20 +256,23 @@ def tile_list_theatre_turnover_slots_kernel(
             z_grouped[0, c] = halves[c // 2][:, c % 2]
         scores(0)
         scores(1)
+        weigh(1)
         round_w1(0, SECOND, SECOND, nc.scalar.copy)
         round_w1(1, ALL, ALL, nc.scalar.copy)
         order_w2(0, SECOND)
         order_w2(1, ALL)
         quantise_w1(0, SECOND)
+        scores(2)
+        weigh(2)
         for i in range(ROW_TILES):
             place(i)
             if i < last:
                 staffed(i)
-            if i + 2 <= last:
-                if i + 2 == PACK:
+            if i + SLOTS <= last:
+                if i + SLOTS == PACK:
                     quantise_w1(1, ALL)
-                scores(i + 2)
-                weigh(i + 2)
+                scores(i + SLOTS)
+                weigh(i + SLOTS)
             if i + 3 <= last:
                 load_staff(i + 3)
             for c in {4: (0, 1), 5: (2, 3)}.get(i, ()):
@@ -289,7 +292,7 @@ def tile_list_theatre_turnover_slots_kernel(
             sums.append(acc)
             for b in range(PASSES):
                 nc.tensor.matmul_mx(
-                    out=acc[:, :width], lhsT=w3_codes[:, b, n * P : (n + 1) * P].bitcast(FP8X4),
+                    out=acc[:, :width], lhsT=w3_codes[n][:, b].bitcast(FP8X4),
                     lhsT_scale=w3_planes[:, b, n * P : (n + 1) * P],
                     rhs=z_codes[b][:, cols].bitcast(FP8X4), rhs_scale=z_planes[b][:, cols], start=(b == 0), stop=(b == PASSES - 1),
                 )
@@ -325,7 +328,10 @@ def tile_list_theatre_turnover_slots_kernel(
             return picked
 
         def floor(n, picked):
-            above = held.tile([P, PK], F32, name="above", tag="page0")
+            if n == 0:
+                above = tail.tile([P, PK], F32, name="above", tag="w3_codes1", align_bytes=64)
+            else:
+                above = held.tile([P, PK], F32, name="above", tag="page0")
             nc.scalar.activation(above[:], picked[:], ACT.Relu, bias=neg_low[:, n : n + 1])
             floored[n] = held.tile([P, PK], F32, name="floored", tag="grouped%d" % (n % 2), align_bytes=64)
             nc.scalar.activation(floored[n][:], above[:], ACT.Identity, bias=low_sb[:, n : n + 1])

@@ -75,16 +75,15 @@ def tile_list_theatre_turnover_slots_kernel(
             nc.sync.dma_start(staff_sb[i][:], staff_rows[pass_and_byte(i)])
 
         tab_s = ring.tile([P, T], U8, name="tab_s", tag="wide", bufs=3, align_bytes=64)
-        w2_s_raw = ring.tile([P, H], U8, name="w2_s_raw", tag="wide", bufs=3, align_bytes=64)
+        w2_s_raw = held.tile([P, H], U8, name="w2_s_raw", tag="larger0", align_bytes=64)
         w1_raw = [
             held.tile([P, PACK, BANK], F32, name="w1_raw", tag="z_codes1", align_bytes=64),
             held.tile([P, PACK, BANK], F32, name="w1_raw", tag="z_codes0", align_bytes=64),
         ]
-        w1_grouped = {
-            (0, 0): held.tile([P, 2 * BANK], BF16, name="w1_grouped", tag="v_words1", align_bytes=64),
-            (0, 2): held.tile([P, 2 * BANK], BF16, name="w1_grouped", tag="grouped0", align_bytes=64),
-            (1, 0): held.tile([P, PACK * BANK], BF16, name="w1_grouped", tag="grouped1", align_bytes=64),
-        }
+        w1_grouped = [
+            held.tile([P, PACK * BANK], BF16, name="w1_grouped", tag="v_words1", align_bytes=64),
+            held.tile([P, PACK * BANK], BF16, name="w1_grouped", tag="grouped1", align_bytes=64),
+        ]
 
         def load_w1(b, quarters):
             cols = slice(quarters.start * P, quarters.stop * P)
@@ -95,15 +94,12 @@ def tile_list_theatre_turnover_slots_kernel(
         def round_w1(b, ts, quarters, engine_copy):
             ms = slice(quarters.start * 32, quarters.stop * 32)
             engine_copy(
-                w1_grouped[b, ts.start][:].rearrange("p (t m j) -> p m t j", m=P, j=PACK)[:, ms],
+                w1_grouped[b][:].rearrange("p (t m j) -> p m t j", m=P, j=PACK)[:, ms, ts],
                 w1_raw[b][:].rearrange("p j (m t) -> p m t j", t=PACK)[:, ms, ts],
             )
 
-        def quantise_w1(b, ts):
-            cols = slice(ts.start * P, ts.stop * P)
-            nc.vector.quantize_mx(
-                out=w1_codes[b][:, cols].bitcast(FP8X4), scales=w1_planes[b][:, cols], in_=w1_grouped[b, ts.start][:],
-            )
+        def quantise_w1(b):
+            nc.vector.quantize_mx(out=w1_codes[b][:].bitcast(FP8X4), scales=w1_planes[b][:], in_=w1_grouped[b][:])
 
         def order_w2(b, ts):
             nc.vector.tensor_copy(
@@ -137,8 +133,8 @@ def tile_list_theatre_turnover_slots_kernel(
             crew_even = zeroed.tile([P, T2], F32, name="crew_even", offset=4 * T2)
             nc.gpsimd.memset(crew_even[:], 0.0)
             nc.vector.tensor_copy(v_scales[:], tab_s[:].indirect(list1[:]))
-            round_w1(0, FIRST, FIRST, nc.scalar.copy)
-            round_w1(0, SECOND, FIRST, nc.scalar.copy)
+            round_w1(0, ALL, FIRST, nc.scalar.copy)
+            round_w1(0, SECOND, SECOND, nc.scalar.copy)
 
             def gather_words(half):
                 v_words.append(held.tile([P, BANK], U32, name="v_words%d" % half, align_bytes=64))
@@ -146,8 +142,10 @@ def tile_list_theatre_turnover_slots_kernel(
 
             gather_words(0)
             order_w2(0, FIRST)
+            order_w2(0, SECOND)
+            order_w2(1, ALL)
             round_w1(0, FIRST, SECOND, nc.vector.tensor_copy)
-            quantise_w1(0, FIRST)
+            quantise_w1(0)
             gather_words(1)
             load_gains(0, 1, "gains_first")
             list2 = load_list(offs2, "list2")
@@ -224,7 +222,7 @@ def tile_list_theatre_turnover_slots_kernel(
         def staffed(i):
             b, t = pass_and_byte(i)
             loaded = held.tile([P, T2], F32, name="loaded", tag="slot%d" % (i % SLOTS), align_bytes=64)
-            parts = 1 if i == 1 else 2
+            parts = 2
             for u in range(parts):
                 cols = slice(u * T2 // parts, (u + 1) * T2 // parts)
                 nc.scalar.activation(loaded[:, cols], pages[i % 2][:, cols], ACT.Identity, bias=load_sb[:, b, t : t + 1])
@@ -257,11 +255,7 @@ def tile_list_theatre_turnover_slots_kernel(
         scores(0)
         scores(1)
         weigh(1)
-        round_w1(0, SECOND, SECOND, nc.scalar.copy)
         round_w1(1, ALL, ALL, nc.scalar.copy)
-        order_w2(0, SECOND)
-        order_w2(1, ALL)
-        quantise_w1(0, SECOND)
         scores(2)
         weigh(2)
         for i in range(ROW_TILES):
@@ -270,7 +264,7 @@ def tile_list_theatre_turnover_slots_kernel(
                 staffed(i)
             if i + SLOTS <= last:
                 if i + SLOTS == PACK:
-                    quantise_w1(1, ALL)
+                    quantise_w1(1)
                 scores(i + SLOTS)
                 weigh(i + SLOTS)
             if i + 3 <= last:
@@ -298,12 +292,15 @@ def tile_list_theatre_turnover_slots_kernel(
                 )
             engine_copy(y_sb[n][:, cols], acc[:, :width])
 
-        for c in range(CHUNKS):
+        load_last = load_sb[:, PASSES - 1, PACK - 1 : PACK]
+        loaded_last = held.tile([P, T2], F32, name="loaded", tag="slot%d" % ((last - 2) % SLOTS), align_bytes=64)
+        nc.vector.scalar_tensor_tensor(
+            z_pairs[1][:, 0, 1, :, 1], pages[last % 2][:, :BANK], load_last, staff_sb[last][:, :BANK], ALU.add, ALU.mult
+        )
+        for c in range(1, CHUNKS):
             cols = slice(c * BANK, (c + 1) * BANK)
-            nc.vector.scalar_tensor_tensor(
-                z_pairs[1][:, c, 1, :, 1], pages[last % 2][:, cols], load_sb[:, PASSES - 1, PACK - 1 : PACK],
-                staff_sb[last][:, cols], ALU.add, ALU.mult,
-            )
+            nc.scalar.activation(loaded_last[:, cols], pages[last % 2][:, cols], ACT.Identity, bias=load_last)
+            nc.vector.tensor_tensor(z_pairs[1][:, c, 1, :, 1], loaded_last[:, cols], staff_sb[last][:, cols], ALU.mult)
         for c in range(CHUNKS):
             interleave(1, c)
         for c in range(CHUNKS):

@@ -1,6 +1,7 @@
 from contextlib import ExitStack
 
 import concourse.mybir as mybir
+from concourse.masks import make_identity
 
 K, H, N, T, S, T2, PK = 512, 1024, 384, 4096, 1024, 2048, 1024
 FLOPS = 2 * 2 * K * H * S + 2 * H * N * T2
@@ -114,6 +115,8 @@ def tile_list_theatre_turnover_slots_kernel(
             nc.vector.memset(tab_s[:, : T // 2].bitcast(I32), 0)
             nc.gpsimd.memset(tab_s[:, T // 2 :].bitcast(I32), 0)
             nc.gpsimd.memset(w2_s_raw[:].bitcast(I32), 0)
+            identity = held.tile([P, P], F32)
+            make_identity(nc, identity[:])
             load_w1(0, FIRST)
             list1 = load_list(offs, "list1")
             nc.sync.dma_start(w2_raw[:].bitcast(I32), w2_words[0].bitcast(I32))
@@ -184,7 +187,6 @@ def tile_list_theatre_turnover_slots_kernel(
         weighted = {}
         largers = {}
         z_grouped = {}
-        z_planes = {}
 
         def scores(i):
             b, t = pass_and_byte(i)
@@ -222,12 +224,12 @@ def tile_list_theatre_turnover_slots_kernel(
         def staffed(i):
             b, t = pass_and_byte(i)
             loaded = held.tile([P, T2], F32, name="loaded", tag="slot%d" % (i % SLOTS), align_bytes=64)
-            parts = 2
-            for u in range(parts):
-                cols = slice(u * T2 // parts, (u + 1) * T2 // parts)
+            split = 1 if i == ROW_TILES - 2 else 2
+            for chunks in (slice(0, split), slice(split, CHUNKS)):
+                cols = slice(chunks.start * BANK, chunks.stop * BANK)
                 nc.scalar.activation(loaded[:, cols], pages[i % 2][:, cols], ACT.Identity, bias=load_sb[:, b, t : t + 1])
                 nc.gpsimd.tensor_tensor(
-                    z_pairs[b][:, u * CHUNKS // parts : (u + 1) * CHUNKS // parts, t // 2, :, t % 2],
+                    z_pairs[b][:, chunks, t // 2, :, t % 2],
                     loaded[:, cols].rearrange("p (c j) -> p c j", j=BANK),
                     staff_sb[i][:, cols].rearrange("p (c j) -> p c j", j=BANK), ALU.mult,
                 )
@@ -242,7 +244,7 @@ def tile_list_theatre_turnover_slots_kernel(
             cols = slice(first, first + width)
             c, j = divmod(first, BANK)
             nc.vector.quantize_mx(
-                out=z_codes[b][:, cols].bitcast(FP8X4), scales=z_planes[b][:, cols],
+                out=z_codes[b][:, cols].bitcast(FP8X4), scales=z_planes[:, b, cols],
                 in_=z_grouped[b, c][:, j : j + width].rearrange("p j t -> p (j t)"),
             )
 
@@ -271,10 +273,21 @@ def tile_list_theatre_turnover_slots_kernel(
                 load_staff(i + 3)
             for c in {4: (0, 1), 5: (2, 3)}.get(i, ()):
                 interleave(0, c)
+        def turn(bank, rows):
+            turned = psum.tile([P, BANK], F32, name="turned", tag="bank%d" % bank)
+            for q in range(BANK // P):
+                nc.tensor.transpose(turned[:, q * P : (q + 1) * P], rows[:, q * P : (q + 1) * P], identity[:])
+            return turned
+
+        turned_early = tail.tile([P, CHUNKS - 2, BANK], F32, name="turned_early", tag="woven", align_bytes=64)
+        turned_late = held.tile([P, BANK], F32, name="turned_late", tag="larger2", align_bytes=64)
+        turned_sb = [turned_early[:, c] for c in range(CHUNKS - 2)] + [turned_late[:]]
+        for c in range(CHUNKS - 1):
+            nc.scalar.copy(turned_sb[c], turn(c, staff_sb[last][:, c * BANK : (c + 1) * BANK])[:])
+        staff_banks = [turn(RESULT_BANKS + c, turned_sb[c]) for c in range(CHUNKS - 1)]
+        woven = tail.tile([P, CHUNKS, BANK, PACK], BF16, name="woven", align_bytes=64)
         for c in range(CHUNKS):
-            z_grouped[1, c] = tail.tile([P, BANK, PACK], BF16, name="z_chunk", tag="chunk%d" % c, align_bytes=64)[:]
-        z_planes[0] = held.tile([P, T2], U8, name="z_planes0", tag="slot%d" % (last % SLOTS), align_bytes=64)
-        z_planes[1] = held.tile([P, T2], U8, name="z_planes1", align_bytes=64)
+            z_grouped[1, c] = woven[:, c]
 
         y_sb = [ring.tile([P, T2], F32, name="y", tag="wide", bufs=3, align_bytes=64) for n in range(OUT_TILES)]
 
@@ -288,19 +301,20 @@ def tile_list_theatre_turnover_slots_kernel(
                 nc.tensor.matmul_mx(
                     out=acc[:, :width], lhsT=w3_codes[n][:, b].bitcast(FP8X4),
                     lhsT_scale=w3_planes[:, b, n * P : (n + 1) * P],
-                    rhs=z_codes[b][:, cols].bitcast(FP8X4), rhs_scale=z_planes[b][:, cols], start=(b == 0), stop=(b == PASSES - 1),
+                    rhs=z_codes[b][:, cols].bitcast(FP8X4), rhs_scale=z_planes[:, b, cols], start=(b == 0), stop=(b == PASSES - 1),
                 )
             engine_copy(y_sb[n][:, cols], acc[:, :width])
 
         load_last = load_sb[:, PASSES - 1, PACK - 1 : PACK]
-        loaded_last = held.tile([P, T2], F32, name="loaded", tag="slot%d" % ((last - 2) % SLOTS), align_bytes=64)
-        nc.vector.scalar_tensor_tensor(
-            z_pairs[1][:, 0, 1, :, 1], pages[last % 2][:, :BANK], load_last, staff_sb[last][:, :BANK], ALU.add, ALU.mult
-        )
-        for c in range(1, CHUNKS):
-            cols = slice(c * BANK, (c + 1) * BANK)
-            nc.scalar.activation(loaded_last[:, cols], pages[last % 2][:, cols], ACT.Identity, bias=load_last)
-            nc.vector.tensor_tensor(z_pairs[1][:, c, 1, :, 1], loaded_last[:, cols], staff_sb[last][:, cols], ALU.mult)
+        for c in range(CHUNKS - 1):
+            nc.vector.scalar_tensor_tensor(
+                z_pairs[1][:, c, 1, :, 1], pages[last % 2][:, c * BANK : (c + 1) * BANK], load_last, staff_banks[c][:],
+                ALU.add, ALU.mult,
+            )
+        loaded_last = held.tile([P, BANK], F32, name="loaded", tag="slot%d" % ((last - 1) % SLOTS), align_bytes=64)
+        nc.gpsimd.tensor_scalar(loaded_last[:], pages[last % 2][:, T2 - BANK :], 1.0, load_last, ALU.mult, ALU.add)
+        nc.gpsimd.tensor_tensor(z_pairs[1][:, CHUNKS - 1, 1, :, 1], loaded_last[:], staff_sb[last][:, T2 - BANK :], ALU.mult)
+        z_planes = held.tile([P, PASSES, T2], U8, name="z_planes", tag="larger2", align_bytes=64)
         for c in range(CHUNKS):
             interleave(1, c)
         for c in range(CHUNKS):
@@ -325,8 +339,8 @@ def tile_list_theatre_turnover_slots_kernel(
             return picked
 
         def floor(n, picked):
-            if n == 0:
-                above = tail.tile([P, PK], F32, name="above", tag="w3_codes1", align_bytes=64)
+            if n + 1 < OUT_TILES:
+                above = tail.tile([P, PK], F32, name="above", tag="w3_codes%d" % (n + 1), align_bytes=64)
             else:
                 above = held.tile([P, PK], F32, name="above", tag="page0")
             nc.scalar.activation(above[:], picked[:], ACT.Relu, bias=neg_low[:, n : n + 1])

@@ -152,12 +152,12 @@ def tile_list_theatre_turnover_slots_kernel(
             gather_words(1)
             load_gains(0, 1, "gains_first")
             list2 = load_list(offs2, "list2")
-            load_gains(1, 2, "gains0")
+            load_gains(1, 1, "gains0")
+            load_w1(1, ALL)
             load_sb = held.tile([P, PASSES, PACK], F32)
             nc.sync.dma_start(load_sb[:], load.rearrange("(b p t) -> p b t", p=P, t=PACK))
-            load_w1(1, ALL)
+            load_gains(2, 2, "gains1")
             load_staff(0)
-            load_gains(3, 1, "gains1")
             load_staff(1)
             load_staff(2)
 
@@ -183,39 +183,77 @@ def tile_list_theatre_turnover_slots_kernel(
             nc.sync.dma_start(delay_sb[n][:], delay[n * P : (n + 1) * P, :])
 
         z_pairs = [ring.tile([P, CHUNKS, 2, BANK, 2], BF16, name="z_pairs", tag="z_pairs", align_bytes=64) for b in range(PASSES)]
-        z_codes = [held.tile([P, T2], U32, name="z_codes", tag="z_codes%d" % b, align_bytes=64) for b in range(PASSES)]
         weighted = {}
         largers = {}
         z_grouped = {}
 
-        def scores(i):
+        def products(i, half):
             b, t = pass_and_byte(i)
             cols = slice((b * PACK + t) * P, (b * PACK + t + 1) * P)
+            js = slice(half * BANK, (half + 1) * BANK)
+            team = psum.tile([P, BANK], F32, name="team", tag="bank%d" % (4 * (i % 2) + 2 * half))
+            nc.tensor.matmul_mx(
+                out=team[:], lhsT=w2_codes[:, 2 * cols.start : 2 * cols.stop].bitcast(FP4X4), lhsT_scale=w2_planes[:, cols],
+                rhs=v_words[half][:].bitcast(FP8X4), rhs_scale=v_scales[:, js], start=True, stop=True,
+            )
+            room = psum.tile([P, BANK], F32, name="room", tag="bank%d" % (4 * (i % 2) + 2 * half + 1))
+            nc.tensor.matmul_mx(
+                out=room[:], lhsT=w1_codes[b][:, t * P : (t + 1) * P].bitcast(FP8X4),
+                lhsT_scale=w1_planes[b][:, t * P : (t + 1) * P],
+                rhs=v_words[half][:].bitcast(FP8X4), rhs_scale=v_scales[:, js], start=True, stop=True,
+            )
+            return team, room
+
+        def turn(bank, *terms):
+            turned = psum.tile([P, BANK], F32, name="turned", tag="bank%d" % bank)
+            for q in range(BANK // P):
+                for u, rows in enumerate(terms):
+                    nc.tensor.matmul(
+                        turned[:, q * P : (q + 1) * P], rows[:, q * P : (q + 1) * P], identity[:],
+                        start=(u == 0), stop=(u == len(terms) - 1), is_transpose=True,
+                    )
+            return turned
+
+        side, pending = {}, {}
+
+        def excess_begin(i, tag):
+            side[i] = held.tile([P, 2, 2, BANK], F32, name="side", tag=tag, align_bytes=64)
+            for half in range(2):
+                work = side[i][:, half]
+                bank = 4 * (i % 2) + 2 * half
+                team, room = products(i, half)
+                nc.scalar.copy(work[:, 0], room[:])
+                nc.scalar.activation(work[:, 1], team[:], ACT.Copy, scale=-1.0)
+                pending[i, half] = (turn(bank, work[:, 0], work[:, 1]), turn(bank + 1, work[:, 1]))
+
+        def excess_clip(i):
+            for half in range(2):
+                work = side[i][:, half]
+                difference, negated = pending[i, half]
+                nc.scalar.activation(work[:, 0], difference[:], ACT.Relu)
+                nc.scalar.activation(work[:, 1], negated[:], ACT.Copy, scale=-1.0)
+                pending[i, half] = turn(4 * (i % 2) + 2 * half, work[:, 0], work[:, 1])
+
+        def scores(i):
             larger = held.tile([P, S], F32, name="larger", tag="larger%d" % (i % SLOTS), align_bytes=64)
             largers[i] = larger
             if i == 0:
                 weighted[i] = held.tile([P, S], F32, name="weighted", tag="slot%d" % (i % SLOTS), align_bytes=64)
             for half in range(S // BANK):
                 js = slice(half * BANK, (half + 1) * BANK)
-                team = psum.tile([P, BANK], F32, name="team", tag="bank%d" % (4 * (i % 2) + 2 * half))
-                nc.tensor.matmul_mx(
-                    out=team[:], lhsT=w2_codes[:, 2 * cols.start : 2 * cols.stop].bitcast(FP4X4), lhsT_scale=w2_planes[:, cols],
-                    rhs=v_words[half][:].bitcast(FP8X4), rhs_scale=v_scales[:, js], start=True, stop=True,
-                )
-                room = psum.tile([P, BANK], F32, name="room", tag="bank%d" % (4 * (i % 2) + 2 * half + 1))
-                nc.tensor.matmul_mx(
-                    out=room[:], lhsT=w1_codes[b][:, t * P : (t + 1) * P].bitcast(FP8X4),
-                    lhsT_scale=w1_planes[b][:, t * P : (t + 1) * P],
-                    rhs=v_words[half][:].bitcast(FP8X4), rhs_scale=v_scales[:, js], start=True, stop=True,
-                )
+                if i in side:
+                    nc.scalar.copy(larger[:, js], pending[i, half][:])
+                    continue
+                team, room = products(i, half)
                 team_sb = ring.tile([P, BANK], F32, name="team_sb", tag="team_sb", bufs=4)
                 nc.scalar.copy(team_sb[:], team[:])
                 nc.vector.tensor_tensor(larger[:, js], room[:], team_sb[:], ALU.max)
                 if i == 0:
-                    nc.gpsimd.tensor_tensor(weighted[i][:, js], larger[:, js], gains[t][:, js], ALU.mult)
+                    nc.gpsimd.tensor_tensor(weighted[i][:, js], larger[:, js], gains[0][:, js], ALU.mult)
 
         def weigh(i):
-            weighted[i] = held.tile([P, S], F32, name="weighted", tag="slot%d" % (i % SLOTS), align_bytes=64)
+            tag = "grouped0" if i == SLOTS else "slot%d" % (i % SLOTS)
+            weighted[i] = held.tile([P, S], F32, name="weighted", tag=tag, align_bytes=64)
             nc.gpsimd.tensor_tensor(weighted[i][:], largers[i][:], gains[pass_and_byte(i)[1]], ALU.mult)
 
         def place(i):
@@ -249,36 +287,42 @@ def tile_list_theatre_turnover_slots_kernel(
             )
 
         last = ROW_TILES - 1
+        scores(0)
+        scores(1)
+        weigh(1)
+        scores(2)
+        weigh(2)
+        excess_begin(3, "z_codes1")
+        excess_clip(3)
+        scores(3)
+        weigh(3)
         halves = [
             held.tile([P, 2, BANK, PACK], BF16, name="z_half", tag="grouped%d" % u, align_bytes=64) for u in range(2)
         ]
         for c in range(CHUNKS):
             z_grouped[0, c] = halves[c // 2][:, c % 2]
-        scores(0)
-        scores(1)
-        weigh(1)
-        round_w1(1, ALL, ALL, nc.scalar.copy)
-        scores(2)
-        weigh(2)
         for i in range(ROW_TILES):
             place(i)
             if i < last:
                 staffed(i)
-            if i + SLOTS <= last:
+            if i == 0:
+                round_w1(1, ALL, ALL, nc.scalar.copy)
+            elif i + SLOTS <= last:
                 if i + SLOTS == PACK:
                     quantise_w1(1)
                 scores(i + SLOTS)
                 weigh(i + SLOTS)
+            if i == 2:
+                excess_begin(6, "z_codes0")
+                excess_begin(7, "z_codes1")
+                excess_clip(6)
+            if i == 3:
+                excess_clip(7)
             if i + 3 <= last:
                 load_staff(i + 3)
             for c in {4: (0, 1), 5: (2, 3)}.get(i, ()):
                 interleave(0, c)
-        def turn(bank, rows):
-            turned = psum.tile([P, BANK], F32, name="turned", tag="bank%d" % bank)
-            for q in range(BANK // P):
-                nc.tensor.transpose(turned[:, q * P : (q + 1) * P], rows[:, q * P : (q + 1) * P], identity[:])
-            return turned
-
+        z_codes = [held.tile([P, T2], U32, name="z_codes", tag="z_codes%d" % b, align_bytes=64) for b in range(PASSES)]
         turned_early = tail.tile([P, CHUNKS - 2, BANK], F32, name="turned_early", tag="woven", align_bytes=64)
         turned_late = held.tile([P, BANK], F32, name="turned_late", tag="larger2", align_bytes=64)
         turned_sb = [turned_early[:, c] for c in range(CHUNKS - 2)] + [turned_late[:]]

@@ -137,17 +137,15 @@ def tile_list_theatre_turnover_slots_kernel(
             nc.gpsimd.memset(crew_even[:], 0.0)
             nc.vector.tensor_copy(v_scales[:], tab_s[:].indirect(list1[:]))
             round_w1(0, ALL, FIRST, nc.scalar.copy)
-            round_w1(0, SECOND, SECOND, nc.scalar.copy)
 
             def gather_words(half):
                 v_words.append(held.tile([P, BANK], U32, name="v_words%d" % half, align_bytes=64))
                 nc.vector.tensor_copy(v_words[half][:], tab_w[:].indirect(list1[:, half * 32 : (half + 1) * 32]))
 
             gather_words(0)
-            order_w2(0, FIRST)
-            order_w2(0, SECOND)
+            order_w2(0, ALL)
             order_w2(1, ALL)
-            round_w1(0, FIRST, SECOND, nc.vector.tensor_copy)
+            round_w1(0, ALL, SECOND, nc.vector.tensor_copy)
             quantise_w1(0)
             gather_words(1)
             load_gains(0, 1, "gains_first")
@@ -312,6 +310,9 @@ def tile_list_theatre_turnover_slots_kernel(
                     quantise_w1(1)
                 scores(i + SLOTS)
                 weigh(i + SLOTS)
+            if i == 1:
+                excess_begin(5, "z_codes1")
+                excess_clip(5)
             if i == 2:
                 excess_begin(6, "z_codes0")
                 excess_begin(7, "z_codes1")

@@ -24,8 +24,18 @@ PASSES = H // (P * PACK)
 ROW_TILES = PASSES * PACK
 CHUNKS = T2 // BANK
 OUT_TILES = N // P
-SLOTS = 3
+STAFF_SLOTS = 5
 RESULT_BANKS = 4
+FROM_BANK = ()
+
+KB = 1024
+AREAS = (
+    ("small", 1), ("v_words", 4), ("v_scales", 1), ("w1_early", 4), ("w1_codes", 4), ("w1_planes", 1),
+    ("w2_codes", 2), ("w2_planes", 1), ("gains", 16), ("pages", 16), ("staff", 8 * STAFF_SLOTS), ("loaded0", 8),
+    ("z_codes", 16), ("loaded1", 8.25), ("work", 16), ("pairs1", 16), ("pairs0", 16), ("woven", 16), ("larger", 16), ("weighted", 20),
+    ("w3", 10), ("wgo", 4),
+)
+AT = {name: int(KB * sum(size for other, size in AREAS[:u])) for u, (name, size) in enumerate(AREAS)}
 
 
 def tile_list_theatre_turnover_slots_kernel(
@@ -34,13 +44,19 @@ def tile_list_theatre_turnover_slots_kernel(
 ):
     nc = tc.nc
     with ExitStack() as ctx:
-        held = ctx.enter_context(tc.tile_pool(name="held", bufs=1))
-        ring = ctx.enter_context(tc.tile_pool(name="ring", bufs=2))
-        zeroed = ctx.enter_context(tc.tile_pool(name="zeroed", bufs=1))
+        lists = ctx.enter_context(tc.tile_pool(name="lists", bufs=1))
+        sbuf = ctx.enter_context(tc.tile_pool(name="sbuf", bufs=1))
         psum = ctx.enter_context(tc.psum_pool(name="psum", bufs=1))
 
+        def at(name, shape, dtype, area, kb=0):
+            start = AT[area] + int(kb * KB)
+            return sbuf.tile([P] + shape, dtype, name=name, tag="%s%d" % (name, start), offset=start, align_bytes=64)
+
+        def bank(u):
+            return psum.tile([P, BANK], F32, name="bank", tag="bank%d" % u)
+
         def load_list(source, name):
-            tile = held.tile([P, S // 16], U16, name=name)
+            tile = lists.tile([P, S // 16], U16, name=name)
             nc.sync.dma_start(tile[:], source)
             return tile
 
@@ -48,123 +64,74 @@ def tile_list_theatre_turnover_slots_kernel(
             for r in range(4):
                 nc.sync.dma_start(plane[r:P:32].bitcast(I32), rows[r:16:4].bitcast(I32))
 
-        v_words = []
-        v_scales = held.tile([P, S], U8, align_bytes=64)
-        w1_codes = [held.tile([P, BANK], U32, name="w1_codes%d" % b, align_bytes=64) for b in range(PASSES)]
-        w1_planes = [held.tile([P, BANK], U8, name="w1_planes%d" % b, align_bytes=64) for b in range(PASSES)]
-        pages = [held.tile([P, T2], F32, name="page0")]
-        w2_codes = held.tile([P, 2 * H], U8, align_bytes=64)
-        w2_planes = held.tile([P, H], U8, align_bytes=64)
-        staff_rows = staff.rearrange("(b p t) c -> b t p c", p=P, t=PACK)
-        wgs_rows = wgs.rearrange("(q t) j -> q t j", t=PACK)
-        staff_sb = {}
-
-        gains = []
-
-        def load_gains(first, count, tag):
-            rows = held.tile([P, count, S], F32, name="gains", tag=tag)
-            for g in (0, 2, 1, 3):
-                nc.sync.dma_start(rows[32 * g : 32 * (g + 1)], wgs_rows[:, first : first + count])
-            gains.extend([rows[:, u] for u in range(count)])
-
         def pass_and_byte(i):
             b, s = divmod(i, PACK)
             return b, (s if b == 0 else (2, 0, 1, 3)[s])
 
+        tab_s = at("tab_s", [T], U8, "work")
+        tab_w = at("tab_w", [T], U32, "pairs0")
+        w2_raw = at("w2_raw", [2 * H], U8, "woven", 8)
+        w2_s_raw = at("w2_s_raw", [H], U8, "pages", 8)
+        w2_codes = at("w2_codes", [2 * H], U8, "w2_codes")
+        w2_planes = at("w2_planes", [H], U8, "w2_planes")
+        w1_codes = [at("w1_codes%d" % b, [BANK], U32, "w1_codes", 2 * b) for b in range(PASSES)]
+        w1_planes = [at("w1_planes%d" % b, [BANK], U8, "w1_planes", b / 2) for b in range(PASSES)]
+        w1_raw = [at("w1_raw%d" % u, [PACK, BANK // 2], F32, ("pairs1", "loaded0", "pairs1", "pairs1")[u], (0, 0, 4, 8)[u]) for u in range(4)]
+        w1_grouped = {
+            (0, 0): at("w1_grouped00", [2, P, PACK], BF16, "w1_early"),
+            (0, 1): at("w1_grouped01", [2, P, PACK], BF16, "w1_early", 2),
+            (1, 0): at("w1_grouped10", [2, P, PACK], BF16, "weighted", 11),
+            (1, 1): at("w1_grouped11", [2, P, PACK], BF16, "larger", 8),
+        }
+        w1_rows = w1.rearrange("(p j) c -> p j c", j=PACK)
+        v_scales = at("v_scales", [S], U8, "v_scales")
+        identity = at("identity", [P], F32, "small")
+        pages = [at("page0", [T2], F32, "pages")]
+
+        nc.gpsimd.memset(w2_s_raw[:].bitcast(I32), 0)
+        nc.vector.memset(tab_s[:, : T // 2].bitcast(I32), 0)
+        nc.gpsimd.memset(tab_s[:, T // 2 :].bitcast(I32), 0)
+        make_identity(nc, identity[:])
+
+        def load_w1(u):
+            nc.sync.dma_start(w1_raw[u][:], w1_rows[:, :, u * BANK // 2 : (u + 1) * BANK // 2])
+
+        load_w1(0)
+        load_scale_rows(w2_s_raw, w2_scales[0])
+        load_w1(1)
+        nc.sync.dma_start(w2_raw[:].bitcast(I32), w2_words[0].bitcast(I32))
+        list1 = load_list(offs, "list1")
+        load_scale_rows(tab_s, tab_scales[0])
+        nc.sync.dma_start(tab_w[:].bitcast(I32), tab_words[0].rearrange("p t i -> p (t i)").bitcast(I32))
+        for u in range(2, 4):
+            load_w1(u)
+
+        wgs_rows = wgs.rearrange("(q t) j -> q t j", t=PACK)
+        gains = []
+
+        def load_gains(first, count):
+            rows = at("gains%d" % first, [count, S], F32, "gains", 4 * first)
+            for g in (0, 2, 1, 3):
+                nc.sync.dma_start(rows[32 * g : 32 * (g + 1)], wgs_rows[:, first : first + count])
+            gains.extend([rows[:, u] for u in range(count)])
+
+        staff_rows = staff.rearrange("(b p t) c -> b t p c", p=P, t=PACK)
+        staff_sb = {}
+
         def load_staff(i):
-            staff_sb[i] = ring.tile([P, T2], F32, name="staff", tag="wide", bufs=3, align_bytes=64)
+            staff_sb[i] = at("staff%d" % i, [T2], F32, "staff", 8 * (0, 1, 2, 3, 4, 2, 1, 0)[i])
             nc.sync.dma_start(staff_sb[i][:], staff_rows[pass_and_byte(i)])
 
-        tab_s = ring.tile([P, T], U8, name="tab_s", tag="wide", bufs=3, align_bytes=64)
-        w2_s_raw = held.tile([P, H], U8, name="w2_s_raw", tag="larger0", align_bytes=64)
-        w1_raw = [
-            held.tile([P, PACK, BANK], F32, name="w1_raw", tag="z_codes1", align_bytes=64),
-            held.tile([P, PACK, BANK], F32, name="w1_raw", tag="z_codes0", align_bytes=64),
-        ]
-        w1_grouped = [
-            held.tile([P, PACK * BANK], BF16, name="w1_grouped", tag="v_words1", align_bytes=64),
-            held.tile([P, PACK * BANK], BF16, name="w1_grouped", tag="grouped1", align_bytes=64),
-        ]
-
-        def load_w1(b, quarters):
-            cols = slice(quarters.start * P, quarters.stop * P)
-            nc.sync.dma_start(
-                w1_raw[b][:, :, cols], w1[:, b * BANK : (b + 1) * BANK].rearrange("(p j) c -> p j c", j=PACK)[:, :, cols]
-            )
-
-        def round_w1(b, ts, quarters, engine_copy):
-            ms = slice(quarters.start * 32, quarters.stop * 32)
-            engine_copy(
-                w1_grouped[b][:].rearrange("p (t m j) -> p m t j", m=P, j=PACK)[:, ms, ts],
-                w1_raw[b][:].rearrange("p j (m t) -> p m t j", t=PACK)[:, ms, ts],
-            )
-
-        def quantise_w1(b):
-            nc.vector.quantize_mx(out=w1_codes[b][:].bitcast(FP8X4), scales=w1_planes[b][:], in_=w1_grouped[b][:])
-
-        def order_w2(b, ts):
-            nc.vector.tensor_copy(
-                w2_planes[:, b * BANK : (b + 1) * BANK].rearrange("p (t m) -> p t m", t=PACK)[:, ts],
-                w2_s_raw[:, b * BANK : (b + 1) * BANK].rearrange("p (m t) -> p t m", t=PACK)[:, ts],
-            )
-
-        FIRST, SECOND, ALL = slice(0, 2), slice(2, 4), slice(0, 4)
-        with tc.tile_pool(name="head", bufs=1) as head:
-            w2_raw = zeroed.tile([P, 2 * H], U8, name="w2_raw", offset=4 * T2 - H)
-            tab_w = head.tile([P, T], U32)
-            nc.vector.memset(tab_s[:, : T // 2].bitcast(I32), 0)
-            nc.gpsimd.memset(tab_s[:, T // 2 :].bitcast(I32), 0)
-            nc.gpsimd.memset(w2_s_raw[:].bitcast(I32), 0)
-            identity = held.tile([P, P], F32)
-            make_identity(nc, identity[:])
-            load_w1(0, FIRST)
-            list1 = load_list(offs, "list1")
-            nc.sync.dma_start(w2_raw[:].bitcast(I32), w2_words[0].bitcast(I32))
-            load_scale_rows(tab_s, tab_scales[0])
-            nc.sync.dma_start(tab_w[:].bitcast(I32), tab_words[0].rearrange("p t i -> p (t i)").bitcast(I32))
-            load_scale_rows(w2_s_raw, w2_scales[0])
-            load_w1(0, SECOND)
-            nc.vector.memset(pages[0][:], 0.0)
-            nc.vector.tensor_copy(
-                w2_codes[:].bitcast(U16).rearrange("p (b t m) -> p b t m", b=PASSES, t=PACK),
-                w2_raw[:].bitcast(U16).rearrange("p (b m t) -> p b t m", b=PASSES, t=PACK),
-            )
-            crew_odd = held.tile([P, T2], F32, name="crew_odd")
-            nc.vector.memset(crew_odd[:], 0.0)
-            pages.append(zeroed.tile([P, T2], F32, name="page1", offset=0))
-            nc.gpsimd.memset(pages[1][:], 0.0)
-            crew_even = zeroed.tile([P, T2], F32, name="crew_even", offset=4 * T2)
-            nc.gpsimd.memset(crew_even[:], 0.0)
-            nc.vector.tensor_copy(v_scales[:], tab_s[:].indirect(list1[:]))
-            round_w1(0, ALL, FIRST, nc.scalar.copy)
-
-            def gather_words(half):
-                v_words.append(held.tile([P, BANK], U32, name="v_words%d" % half, align_bytes=64))
-                nc.vector.tensor_copy(v_words[half][:], tab_w[:].indirect(list1[:, half * 32 : (half + 1) * 32]))
-
-            gather_words(0)
-            order_w2(0, ALL)
-            order_w2(1, ALL)
-            round_w1(0, ALL, SECOND, nc.vector.tensor_copy)
-            quantise_w1(0)
-            gather_words(1)
-            load_gains(0, 1, "gains_first")
-            list2 = load_list(offs2, "list2")
-            load_gains(1, 1, "gains0")
-            load_w1(1, ALL)
-            load_sb = held.tile([P, PASSES, PACK], F32)
-            nc.sync.dma_start(load_sb[:], load.rearrange("(b p t) -> p b t", p=P, t=PACK))
-            load_gains(2, 2, "gains1")
-            load_staff(0)
-            load_staff(1)
-            load_staff(2)
-
-        tail = ctx.enter_context(tc.tile_pool(name="tail", bufs=1))
-        w3_codes = [tail.tile([P, PASSES, P], U32, name="w3_codes%d" % n, align_bytes=64) for n in range(OUT_TILES)]
-        w3_planes = tail.tile([P, PASSES, N], U8, align_bytes=64)
-        low_sb = tail.tile([P, OUT_TILES], F32)
-        neg_low = tail.tile([P, OUT_TILES], F32)
-        wgo_sb = tail.tile([P, PK], F32)
+        load_gains(0, 1)
+        list2 = load_list(offs2, "list2")
+        load_gains(1, 1)
+        load_sb = at("load_sb", [PASSES, PACK], F32, "small", 0.5)
+        nc.sync.dma_start(load_sb[:], load.rearrange("(b p t) -> p b t", p=P, t=PACK))
+        load_gains(2, 2)
+        for i in range(STAFF_SLOTS):
+            load_staff(i)
+        w3_codes = [at("w3_codes%d" % n, [PASSES, P], U32, "w3", (0, 2, 6)[n]) for n in range(OUT_TILES)]
+        w3_planes = at("w3_planes", [PASSES, N], U8, "w3", 1)
         nc.gpsimd.memset(w3_planes[:].bitcast(I32), 0)
         for n in range(OUT_TILES):
             nc.sync.dma_start(
@@ -173,95 +140,174 @@ def tile_list_theatre_turnover_slots_kernel(
         load_scale_rows(w3_planes, w3_scales.rearrange("a q c -> q a c"))
         list3 = load_list(offs3, "list3")
         list4 = load_list(offs4, "list4")
+        low_sb = at("low_sb", [OUT_TILES], F32, "small", 0.5625)
+        neg_low = at("neg_low", [OUT_TILES], F32, "small", 0.625)
         with nc.allow_non_contiguous_dma(reason="one value a partition"):
             nc.sync.dma_start(low_sb[:], low.rearrange("(n p) -> p n", p=P))
-        nc.sync.dma_start(wgo_sb[:], wgo)
-        delay_sb = [tail.tile([P, PK], F32, name="delay%d" % n) for n in range(OUT_TILES)]
-        for n in range(OUT_TILES):
-            nc.sync.dma_start(delay_sb[n][:], delay[n * P : (n + 1) * P, :])
 
-        z_pairs = [ring.tile([P, CHUNKS, 2, BANK, 2], BF16, name="z_pairs", tag="z_pairs", align_bytes=64) for b in range(PASSES)]
-        weighted = {}
-        largers = {}
-        z_grouped = {}
+        def round_w1(b, u, ms, rows, engine_copy):
+            engine_copy(
+                w1_grouped[b, u][:].rearrange("p t m j -> p m t j")[:, ms],
+                rows[:].rearrange("p j (m t) -> p m t j", t=PACK)[:, :, 2 * u : 2 * u + 2],
+            )
 
-        def products(i, half):
+        def gpsimd_copy(target, source):
+            nc.gpsimd.tensor_scalar(target, source, 1.0, 0.0, ALU.mult, ALU.add)
+
+        def quantise_w1(b, u):
+            cols = slice(u * 2 * P, (u + 1) * 2 * P)
+            nc.vector.quantize_mx(
+                out=w1_codes[b][:, cols].bitcast(FP8X4), scales=w1_planes[b][:, cols],
+                in_=w1_grouped[b, u][:].rearrange("p t m j -> p (t m j)"),
+            )
+
+        def order_w2_scales(b):
+            nc.vector.tensor_copy(
+                w2_planes[:, b * BANK : (b + 1) * BANK].rearrange("p (t m) -> p t m", t=PACK),
+                w2_s_raw[:, b * BANK : (b + 1) * BANK].rearrange("p (m t) -> p t m", t=PACK),
+            )
+
+        v_words = []
+
+        def gather_words(half):
+            v_words.append(at("v_words%d" % half, [BANK], U32, "v_words", 2 * half))
+            nc.vector.tensor_copy(v_words[half][:], tab_w[:].indirect(list1[:, half * 32 : (half + 1) * 32]))
+
+        nc.vector.memset(pages[0][:], 0.0)
+        nc.vector.tensor_copy(
+            w2_codes[:].bitcast(U16).rearrange("p (b t m) -> p b t m", b=PASSES, t=PACK),
+            w2_raw[:].bitcast(U16).rearrange("p (b m t) -> p b t m", b=PASSES, t=PACK),
+        )
+        for b in range(PASSES):
+            order_w2_scales(b)
+        pages.append(at("page1", [T2], F32, "pages", 8))
+        nc.gpsimd.memset(pages[1][:], 0.0)
+        nc.vector.tensor_copy(v_scales[:], tab_s[:].indirect(list1[:]))
+        for piece in range(2):
+            for u in range(2):
+                round_w1(0, u, slice(piece * P // 2, (piece + 1) * P // 2), w1_raw[piece], nc.scalar.copy)
+        for u in range(2):
+            quantise_w1(0, u)
+        gather_words(0)
+        gather_words(1)
+        for piece in range(2):
+            for u in range(2):
+                round_w1(1, u, slice(piece * P // 2, (piece + 1) * P // 2), w1_raw[2 + piece], gpsimd_copy)
+
+        def team_product(i, half, u):
             b, t = pass_and_byte(i)
             cols = slice((b * PACK + t) * P, (b * PACK + t + 1) * P)
-            js = slice(half * BANK, (half + 1) * BANK)
-            team = psum.tile([P, BANK], F32, name="team", tag="bank%d" % (4 * (i % 2) + 2 * half))
+            team = bank(u)
             nc.tensor.matmul_mx(
                 out=team[:], lhsT=w2_codes[:, 2 * cols.start : 2 * cols.stop].bitcast(FP4X4), lhsT_scale=w2_planes[:, cols],
-                rhs=v_words[half][:].bitcast(FP8X4), rhs_scale=v_scales[:, js], start=True, stop=True,
+                rhs=v_words[half][:].bitcast(FP8X4), rhs_scale=v_scales[:, half * BANK : (half + 1) * BANK], start=True, stop=True,
             )
-            room = psum.tile([P, BANK], F32, name="room", tag="bank%d" % (4 * (i % 2) + 2 * half + 1))
+            return team
+
+        def room_product(i, half, u):
+            b, t = pass_and_byte(i)
+            room = bank(u)
             nc.tensor.matmul_mx(
                 out=room[:], lhsT=w1_codes[b][:, t * P : (t + 1) * P].bitcast(FP8X4),
                 lhsT_scale=w1_planes[b][:, t * P : (t + 1) * P],
-                rhs=v_words[half][:].bitcast(FP8X4), rhs_scale=v_scales[:, js], start=True, stop=True,
+                rhs=v_words[half][:].bitcast(FP8X4), rhs_scale=v_scales[:, half * BANK : (half + 1) * BANK], start=True, stop=True,
             )
-            return team, room
+            return room
 
-        def turn(bank, *terms):
-            turned = psum.tile([P, BANK], F32, name="turned", tag="bank%d" % bank)
+        larger, weighted = {}, {}
+        WEIGHTED_AT = (None, ("weighted", 0), ("weighted", 4), ("weighted", 8), ("staff", 0), ("staff", 8), ("staff", 24), ("staff", 32))
+
+        def weigh(i):
+            weighted[i] = at("weighted%d" % i, [S], F32, *WEIGHTED_AT[i])
+            nc.gpsimd.tensor_tensor(weighted[i][:], larger[i][:], gains[pass_and_byte(i)[1]], ALU.mult)
+
+        for i in range(PACK):
+            larger[i] = at("larger%d" % i, [S], F32, "larger", 4 * i)
+        early = at("team_early", [2, 2, BANK], F32, "loaded0")
+        for i in range(PACK):
+            for half in range(2):
+                js, u = slice(half * BANK, (half + 1) * BANK), 2 * (i % 2) + half
+                team_sb = early[:, i, half] if i < 2 else at("team", [BANK], F32, *(("weighted", 13), ("weighted", 15), ("weighted", 3), ("pairs1", 12))[u])[:]
+                nc.scalar.copy(team_sb, team_product(i, half, PACK + u)[:])
+                nc.vector.tensor_tensor(larger[i][:, js], room_product(i, half, u)[:], team_sb, ALU.max)
+            if i == 0:
+                for e in range(2):
+                    quantise_w1(1, e)
+        first_halves = [at("weighted0%d" % half, [BANK], F32, "weighted", 12 + 2 * half) for half in range(2)]
+        for half in range(2):
+            js = slice(half * BANK, (half + 1) * BANK)
+            nc.gpsimd.tensor_tensor(first_halves[half][:], larger[0][:, js], gains[0][:, js], ALU.mult)
+        for i in range(1, PACK):
+            weigh(i)
+
+        def turn(u, *terms):
+            turned = bank(u)
             for q in range(BANK // P):
-                for u, rows in enumerate(terms):
+                for e, rows in enumerate(terms):
                     nc.tensor.matmul(
                         turned[:, q * P : (q + 1) * P], rows[:, q * P : (q + 1) * P], identity[:],
-                        start=(u == 0), stop=(u == len(terms) - 1), is_transpose=True,
+                        start=(e == 0), stop=(e == len(terms) - 1), is_transpose=True,
                     )
             return turned
 
-        side, pending = {}, {}
+        WORK_AT = {
+            (4, 0): (("z_codes", 4), ("z_codes", 6), ("z_codes", 4), ("z_codes", 6)),
+            (4, 1): (("z_codes", 8), ("z_codes", 10), ("z_codes", 8), ("z_codes", 10)),
+            (5, 0): (("z_codes", 14), ("loaded0", 2), ("loaded1", 0), ("loaded1", 2)),
+            (5, 1): (("work", 8), ("work", 10), ("work", 8), ("work", 10)),
+            (6, 0): (("work", 4), ("loaded0", 7), ("loaded1", 8), ("z_codes", 6)),
+            (6, 1): (("z_codes", 8), ("z_codes", 10), ("staff", 4), ("staff", 6)),
+            (7, 0): (("work", 2.5), ("work", 5.5), ("loaded0", 0), ("loaded0", 2)),
+            (7, 1): (("loaded0", 8), ("z_codes", 12), ("loaded0", 4), ("work", 8)),
+        }
+        pending = {}
 
-        def excess_begin(i, tag):
-            side[i] = held.tile([P, 2, 2, BANK], F32, name="side", tag=tag, align_bytes=64)
-            for half in range(2):
-                work = side[i][:, half]
-                bank = 4 * (i % 2) + 2 * half
-                team, room = products(i, half)
-                nc.scalar.copy(work[:, 0], room[:])
-                nc.scalar.activation(work[:, 1], team[:], ACT.Copy, scale=-1.0)
-                pending[i, half] = (turn(bank, work[:, 0], work[:, 1]), turn(bank + 1, work[:, 1]))
+        def work_tile(i, half, e):
+            return at("work%d%d%d" % (i, half, e), [BANK], F32, *WORK_AT[i, half][e])
 
-        def excess_clip(i):
-            for half in range(2):
-                work = side[i][:, half]
-                difference, negated = pending[i, half]
-                nc.scalar.activation(work[:, 0], difference[:], ACT.Relu)
-                nc.scalar.activation(work[:, 1], negated[:], ACT.Copy, scale=-1.0)
-                pending[i, half] = turn(4 * (i % 2) + 2 * half, work[:, 0], work[:, 1])
+        def subtract(i, half):
+            u = 4 * ((i + 1) % 2) + 2 * half
+            team, room = team_product(i, half, u), room_product(i, half, u + 1)
+            minus_team, room_sb = work_tile(i, half, 0), work_tile(i, half, 1)
+            nc.scalar.activation(minus_team[:], team[:], ACT.Copy, scale=-1.0)
+            nc.scalar.copy(room_sb[:], room[:])
+            difference = turn(u + 1, minus_team, room_sb)
+            pending[i, half] = (turn(u, minus_team), difference)
 
-        def scores(i):
-            larger = held.tile([P, S], F32, name="larger", tag="larger%d" % (i % SLOTS), align_bytes=64)
-            largers[i] = larger
-            if i == 0:
-                weighted[i] = held.tile([P, S], F32, name="weighted", tag="slot%d" % (i % SLOTS), align_bytes=64)
-            for half in range(S // BANK):
-                js = slice(half * BANK, (half + 1) * BANK)
-                if i in side:
-                    nc.scalar.copy(larger[:, js], pending[i, half][:])
-                    continue
-                team, room = products(i, half)
-                team_sb = ring.tile([P, BANK], F32, name="team_sb", tag="team_sb", bufs=4)
-                nc.scalar.copy(team_sb[:], team[:])
-                nc.vector.tensor_tensor(larger[:, js], room[:], team_sb[:], ALU.max)
-                if i == 0:
-                    nc.gpsimd.tensor_tensor(weighted[i][:, js], larger[:, js], gains[0][:, js], ALU.mult)
+        def clip(i, half):
+            negated, difference = pending[i, half]
+            team_sb, excess = work_tile(i, half, 2), work_tile(i, half, 3)
+            nc.scalar.activation(excess[:], difference[:], ACT.Relu)
+            nc.scalar.activation(team_sb[:], negated[:], ACT.Copy, scale=-1.0)
+            pending[i, half] = turn(4 * ((i + 1) % 2) + 2 * half, team_sb, excess)
 
-        def weigh(i):
-            tag = "grouped0" if i == SLOTS else "slot%d" % (i % SLOTS)
-            weighted[i] = held.tile([P, S], F32, name="weighted", tag=tag, align_bytes=64)
-            nc.gpsimd.tensor_tensor(weighted[i][:], largers[i][:], gains[pass_and_byte(i)[1]], ALU.mult)
+        def collect(i, half):
+            js = slice(half * BANK, (half + 1) * BANK)
+            if i in FROM_BANK:
+                if half == 0:
+                    weighted[i] = at("weighted%d" % i, [S], F32, *WEIGHTED_AT[i])
+                nc.vector.tensor_tensor(weighted[i][:, js], pending[i, half][:], gains[pass_and_byte(i)[1]][:, js], ALU.mult)
+                return
+            if half == 0:
+                larger[i] = at("larger%d" % i, [S], F32, *(("staff", 12) if i == 6 else ("larger", 4 * (i % PACK))))
+            nc.scalar.copy(larger[i][:, js], pending[i, half][:])
+            if half == 1:
+                weigh(i)
 
         def place(i):
-            nc.vector.tensor_copy(pages[i % 2][:].indirect(list2[:]), weighted[i][:])
+            if i == 0:
+                for half in range(2):
+                    nc.vector.tensor_copy(pages[0][:].indirect(list2[:, half * 32 : (half + 1) * 32]), first_halves[half][:])
+            else:
+                nc.vector.tensor_copy(pages[i % 2][:].indirect(list2[:]), weighted[i][:])
+
+        z_pairs = [at("z_pairs%d" % b, [CHUNKS, 2, BANK, 2], BF16, "pairs%d" % b) for b in range(PASSES)]
+        last = ROW_TILES - 1
 
         def staffed(i):
             b, t = pass_and_byte(i)
-            loaded = held.tile([P, T2], F32, name="loaded", tag="slot%d" % (i % SLOTS), align_bytes=64)
-            split = 1 if i == ROW_TILES - 2 else 2
-            for chunks in (slice(0, split), slice(split, CHUNKS)):
+            loaded = at("loaded%d" % i, [T2], F32, *(("pairs0", 0) if i == 5 else ("pairs0", 15.9375) if i == 6 else ("loaded%d" % (i % 2), 0.0625 * (i == 3))))
+            for chunks in (slice(0, 1), slice(1, CHUNKS)) if i in (0, last - 1) else (slice(0, CHUNKS),):
                 cols = slice(chunks.start * BANK, chunks.stop * BANK)
                 nc.scalar.activation(loaded[:, cols], pages[i % 2][:, cols], ACT.Identity, bias=load_sb[:, b, t : t + 1])
                 nc.gpsimd.tensor_tensor(
@@ -270,77 +316,74 @@ def tile_list_theatre_turnover_slots_kernel(
                     staff_sb[i][:, cols].rearrange("p (c j) -> p c j", j=BANK), ALU.mult,
                 )
 
+        z_grouped = {}
+
         def interleave(b, c):
             nc.scalar.copy(
-                z_grouped[b, c].rearrange("p j t -> p (j t)").bitcast(U32).rearrange("p (j u) -> p j u", u=2),
+                z_grouped[b][:, c].rearrange("p j t -> p (j t)").bitcast(U32).rearrange("p (j u) -> p j u", u=2),
                 z_pairs[b][:, c].rearrange("p u j e -> p u (j e)").bitcast(U32).rearrange("p u j -> p j u"),
             )
+
+        ahead = [(subtract, 4, 0), (subtract, 4, 1), (subtract, 5, 0), (subtract, 5, 1), (clip, 4, 0), (clip, 4, 1)]
+        beside = {
+            1: [(collect, 4, 0), (collect, 4, 1), (clip, 5, 0), (clip, 5, 1)],
+            2: [(subtract, 6, 0), (subtract, 6, 1), (collect, 5, 0), (collect, 5, 1)],
+            3: [(clip, 6, 0), (clip, 6, 1), (subtract, 7, 0), (subtract, 7, 1)],
+            4: [(collect, 6, 0), (collect, 6, 1), (clip, 7, 0), (clip, 7, 1)],
+            5: [(collect, 7, 0), (collect, 7, 1)],
+        }
+        for step, i, half in ahead:
+            step(i, half)
+        for i in range(ROW_TILES):
+            if i > 0:
+                staffed(i - 1)
+            for step, j, half in beside.get(i, ()):
+                step(j, half)
+            if i == 5:
+                wgo_sb = at("wgo", [PK], F32, "wgo")
+                nc.sync.dma_start(wgo_sb[:], wgo)
+                delay_sb = [at("delay%d" % n, [PK], F32, "gains", 4 * n) for n in range(OUT_TILES)]
+                for n in range(OUT_TILES):
+                    nc.sync.dma_start(delay_sb[n][:], delay[n * P : (n + 1) * P, :])
+            if i == 5:
+                z_grouped[0] = at("z_grouped0", [CHUNKS, BANK, PACK], BF16, "work")
+                for c in range(CHUNKS):
+                    interleave(0, c)
+            if i == 6:
+                turned_sb = at("turned", [CHUNKS - 1, BANK], F32, "pairs0", 10)
+                for c in range(CHUNKS - 1):
+                    nc.scalar.copy(turned_sb[:, c], turn(c, staff_sb[last][:, c * BANK : (c + 1) * BANK])[:])
+                staff_banks = [turn(RESULT_BANKS + c, turned_sb[:, c]) for c in range(CHUNKS - 1)]
+            place(i)
+            if i in (3, 4, 5):
+                load_staff({3: 5, 4: 7, 5: 6}[i])
+
+        load_last = load_sb[:, PASSES - 1, PACK - 1 : PACK]
+        loaded_last = at("loaded_last", [BANK], F32, "pairs0", 10)
+        nc.scalar.activation(loaded_last[:], pages[last % 2][:, T2 - BANK :], ACT.Identity, bias=load_last)
+        nc.gpsimd.tensor_tensor(z_pairs[1][:, CHUNKS - 1, 1, :, 1], loaded_last[:], staff_sb[last][:, T2 - BANK :], ALU.mult)
+        for c in range(CHUNKS - 1):
+            nc.vector.scalar_tensor_tensor(
+                z_pairs[1][:, c, 1, :, 1], pages[last % 2][:, c * BANK : (c + 1) * BANK], load_last, staff_banks[c][:],
+                ALU.add, ALU.mult,
+            )
+        z_grouped[1] = at("z_grouped1", [CHUNKS, BANK, PACK], BF16, "woven")
+        z_codes = [at("z_codes%d" % b, [T2], U32, "z_codes", 8 * b) for b in range(PASSES)]
+        z_planes = at("z_planes", [PASSES, T2], U8, "pages", 8)
+        y_sb = [at("y%d" % n, [T2], F32, "staff", 8 * (2, 3, 1)[n]) for n in range(OUT_TILES)]
+        sums = []
 
         def quantise_z(b, first, width):
             cols = slice(first, first + width)
             c, j = divmod(first, BANK)
             nc.vector.quantize_mx(
                 out=z_codes[b][:, cols].bitcast(FP8X4), scales=z_planes[:, b, cols],
-                in_=z_grouped[b, c][:, j : j + width].rearrange("p j t -> p (j t)"),
+                in_=z_grouped[b][:, c, j : j + width].rearrange("p j t -> p (j t)"),
             )
-
-        last = ROW_TILES - 1
-        scores(0)
-        scores(1)
-        weigh(1)
-        scores(2)
-        weigh(2)
-        excess_begin(3, "z_codes1")
-        excess_clip(3)
-        scores(3)
-        weigh(3)
-        halves = [
-            held.tile([P, 2, BANK, PACK], BF16, name="z_half", tag="grouped%d" % u, align_bytes=64) for u in range(2)
-        ]
-        for c in range(CHUNKS):
-            z_grouped[0, c] = halves[c // 2][:, c % 2]
-        for i in range(ROW_TILES):
-            place(i)
-            if i < last:
-                staffed(i)
-            if i == 0:
-                round_w1(1, ALL, ALL, nc.scalar.copy)
-            elif i + SLOTS <= last:
-                if i + SLOTS == PACK:
-                    quantise_w1(1)
-                scores(i + SLOTS)
-                weigh(i + SLOTS)
-            if i == 1:
-                excess_begin(5, "z_codes1")
-                excess_clip(5)
-            if i == 2:
-                excess_begin(6, "z_codes0")
-                excess_begin(7, "z_codes1")
-                excess_clip(6)
-            if i == 3:
-                excess_clip(7)
-            if i + 3 <= last:
-                load_staff(i + 3)
-            for c in {4: (0, 1), 5: (2, 3)}.get(i, ()):
-                interleave(0, c)
-        z_codes = [held.tile([P, T2], U32, name="z_codes", tag="z_codes%d" % b, align_bytes=64) for b in range(PASSES)]
-        turned_early = tail.tile([P, CHUNKS - 2, BANK], F32, name="turned_early", tag="woven", align_bytes=64)
-        turned_late = held.tile([P, BANK], F32, name="turned_late", tag="larger2", align_bytes=64)
-        turned_sb = [turned_early[:, c] for c in range(CHUNKS - 2)] + [turned_late[:]]
-        for c in range(CHUNKS - 1):
-            nc.scalar.copy(turned_sb[c], turn(c, staff_sb[last][:, c * BANK : (c + 1) * BANK])[:])
-        staff_banks = [turn(RESULT_BANKS + c, turned_sb[c]) for c in range(CHUNKS - 1)]
-        woven = tail.tile([P, CHUNKS, BANK, PACK], BF16, name="woven", align_bytes=64)
-        for c in range(CHUNKS):
-            z_grouped[1, c] = woven[:, c]
-
-        y_sb = [ring.tile([P, T2], F32, name="y", tag="wide", bufs=3, align_bytes=64) for n in range(OUT_TILES)]
-
-        sums = []
 
         def features(n, first, width, engine_copy):
             cols = slice(first, first + width)
-            acc = psum.tile([P, BANK], F32, name="acc", tag="bank%d" % (len(sums) % RESULT_BANKS))
+            acc = bank(len(sums) % RESULT_BANKS)
             sums.append(acc)
             for b in range(PASSES):
                 nc.tensor.matmul_mx(
@@ -350,16 +393,6 @@ def tile_list_theatre_turnover_slots_kernel(
                 )
             engine_copy(y_sb[n][:, cols], acc[:, :width])
 
-        load_last = load_sb[:, PASSES - 1, PACK - 1 : PACK]
-        for c in range(CHUNKS - 1):
-            nc.vector.scalar_tensor_tensor(
-                z_pairs[1][:, c, 1, :, 1], pages[last % 2][:, c * BANK : (c + 1) * BANK], load_last, staff_banks[c][:],
-                ALU.add, ALU.mult,
-            )
-        loaded_last = held.tile([P, BANK], F32, name="loaded", tag="slot%d" % ((last - 1) % SLOTS), align_bytes=64)
-        nc.gpsimd.tensor_scalar(loaded_last[:], pages[last % 2][:, T2 - BANK :], 1.0, load_last, ALU.mult, ALU.add)
-        nc.gpsimd.tensor_tensor(z_pairs[1][:, CHUNKS - 1, 1, :, 1], loaded_last[:], staff_sb[last][:, T2 - BANK :], ALU.mult)
-        z_planes = held.tile([P, PASSES, T2], U8, name="z_planes", tag="larger2", align_bytes=64)
         for c in range(CHUNKS):
             interleave(1, c)
         for c in range(CHUNKS):
@@ -375,28 +408,27 @@ def tile_list_theatre_turnover_slots_kernel(
         for first, width, engine_copy in pieces:
             features(0, first, width, engine_copy)
 
+        crew = [at("crew%d" % u, [T2], F32, "woven", 8 * u) for u in range(2)]
+        for u in range(2):
+            nc.gpsimd.memset(crew[u][:], 0.0)
         nc.scalar.activation(neg_low[:], low_sb[:], ACT.Copy, scale=-1.0)
         floored = {}
 
         def pick(n):
-            picked = held.tile([P, PK], F32, name="picked", tag="larger%d" % (n % 2), align_bytes=64)
+            picked = at("picked%d" % n, [PK], F32, "larger", 4 * (n % 2))
             nc.vector.tensor_tensor(picked[:], y_sb[n][:].indirect(list3[:]), delay_sb[n][:], ALU.add)
             return picked
 
         def floor(n, picked):
-            if n + 1 < OUT_TILES:
-                above = tail.tile([P, PK], F32, name="above", tag="w3_codes%d" % (n + 1), align_bytes=64)
-            else:
-                above = held.tile([P, PK], F32, name="above", tag="page0")
+            above = at("above%d" % n, [PK], F32, *(("w3", 2), ("w3", 6), ("larger", 8))[n])
             nc.scalar.activation(above[:], picked[:], ACT.Relu, bias=neg_low[:, n : n + 1])
-            floored[n] = held.tile([P, PK], F32, name="floored", tag="grouped%d" % (n % 2), align_bytes=64)
+            floored[n] = at("floored%d" % n, [PK], F32, "weighted", 4 * (n % 2))
             nc.scalar.activation(floored[n][:], above[:], ACT.Identity, bias=low_sb[:, n : n + 1])
 
         def hand_over(n):
             nc.vector.tensor_tensor(crew[n % 2][:].indirect(list4[:]), floored[n][:], wgo_sb[:], ALU.mult)
             nc.sync.dma_start(out[n * P : (n + 1) * P, :], crew[n % 2][:])
 
-        crew = [crew_even, crew_odd]
         picked = {0: pick(0)}
         for n in range(OUT_TILES):
             if n + 1 < OUT_TILES:

@@ -27,6 +27,7 @@ OUT_TILES = N // P
 STAFF_SLOTS = 5
 RESULT_BANKS = 4
 FROM_BANK = ()
+SHARE = T2 - 768
 
 KB = 1024
 AREAS = (
@@ -80,7 +81,7 @@ def tile_list_theatre_turnover_slots_kernel(
         w1_grouped = {
             (0, 0): at("w1_grouped00", [2, P, PACK], BF16, "w1_early"),
             (0, 1): at("w1_grouped01", [2, P, PACK], BF16, "w1_early", 2),
-            (1, 0): at("w1_grouped10", [2, P, PACK], BF16, "weighted", 11),
+            (1, 0): at("w1_grouped10", [2, P, PACK], BF16, "weighted", 15),
             (1, 1): at("w1_grouped11", [2, P, PACK], BF16, "larger", 8),
         }
         w1_rows = w1.rearrange("(p j) c -> p j c", j=PACK)
@@ -123,10 +124,10 @@ def tile_list_theatre_turnover_slots_kernel(
             nc.sync.dma_start(staff_sb[i][:], staff_rows[pass_and_byte(i)])
 
         load_gains(0, 1)
-        list2 = load_list(offs2, "list2")
         load_gains(1, 1)
         load_sb = at("load_sb", [PASSES, PACK], F32, "small", 0.5)
         nc.sync.dma_start(load_sb[:], load.rearrange("(b p t) -> p b t", p=P, t=PACK))
+        list2 = load_list(offs2, "list2")
         load_gains(2, 2)
         for i in range(STAFF_SLOTS):
             load_staff(i)
@@ -215,7 +216,7 @@ def tile_list_theatre_turnover_slots_kernel(
             return room
 
         larger, weighted = {}, {}
-        WEIGHTED_AT = (None, ("weighted", 0), ("weighted", 4), ("weighted", 8), ("staff", 0), ("staff", 8), ("staff", 24), ("staff", 32))
+        WEIGHTED_AT = (("weighted", 12), ("weighted", 16), ("weighted", 4), ("weighted", 8), ("staff", 0), ("staff", 8), ("staff", 24), ("staff", 32))
 
         def weigh(i):
             weighted[i] = at("weighted%d" % i, [S], F32, *WEIGHTED_AT[i])
@@ -227,22 +228,18 @@ def tile_list_theatre_turnover_slots_kernel(
         for i in range(PACK):
             for half in range(2):
                 js, u = slice(half * BANK, (half + 1) * BANK), 2 * (i % 2) + half
-                team_sb = early[:, i, half] if i < 2 else at("team", [BANK], F32, *(("weighted", 13), ("weighted", 15), ("weighted", 3), ("pairs1", 12))[u])[:]
+                team_sb = early[:, i, half] if i < 2 else at("team", [BANK], F32, "woven", 2 * u)[:]
                 nc.scalar.copy(team_sb, team_product(i, half, PACK + u)[:])
                 nc.vector.tensor_tensor(larger[i][:, js], room_product(i, half, u)[:], team_sb, ALU.max)
             if i == 0:
                 for e in range(2):
                     quantise_w1(1, e)
-        first_halves = [at("weighted0%d" % half, [BANK], F32, "weighted", 12 + 2 * half) for half in range(2)]
-        for half in range(2):
-            js = slice(half * BANK, (half + 1) * BANK)
-            nc.gpsimd.tensor_tensor(first_halves[half][:], larger[0][:, js], gains[0][:, js], ALU.mult)
-        for i in range(1, PACK):
+        for i in range(PACK):
             weigh(i)
 
         def turn(u, *terms):
             turned = bank(u)
-            for q in range(BANK // P):
+            for q in range(terms[0].shape[-1] // P):
                 for e, rows in enumerate(terms):
                     nc.tensor.matmul(
                         turned[:, q * P : (q + 1) * P], rows[:, q * P : (q + 1) * P], identity[:],
@@ -295,18 +292,14 @@ def tile_list_theatre_turnover_slots_kernel(
                 weigh(i)
 
         def place(i):
-            if i == 0:
-                for half in range(2):
-                    nc.vector.tensor_copy(pages[0][:].indirect(list2[:, half * 32 : (half + 1) * 32]), first_halves[half][:])
-            else:
-                nc.vector.tensor_copy(pages[i % 2][:].indirect(list2[:]), weighted[i][:])
+            nc.vector.tensor_copy(pages[i % 2][:].indirect(list2[:]), weighted[i][:])
 
         z_pairs = [at("z_pairs%d" % b, [CHUNKS, 2, BANK, 2], BF16, "pairs%d" % b) for b in range(PASSES)]
         last = ROW_TILES - 1
 
         def staffed(i):
             b, t = pass_and_byte(i)
-            loaded = at("loaded%d" % i, [T2], F32, *(("pairs0", 0) if i == 5 else ("pairs0", 15.9375) if i == 6 else ("loaded%d" % (i % 2), 0.0625 * (i == 3))))
+            loaded = at("loaded%d" % i, [T2], F32, *(("pairs0", 0) if i == 5 else ("pairs0", 14.9375) if i == 6 else ("loaded%d" % (i % 2), 0.0625 * (i == 3))))
             for chunks in (slice(0, 1), slice(1, CHUNKS)) if i in (0, last - 1) else (slice(0, CHUNKS),):
                 cols = slice(chunks.start * BANK, chunks.stop * BANK)
                 nc.scalar.activation(loaded[:, cols], pages[i % 2][:, cols], ACT.Identity, bias=load_sb[:, b, t : t + 1])
@@ -350,28 +343,32 @@ def tile_list_theatre_turnover_slots_kernel(
                 for c in range(CHUNKS):
                     interleave(0, c)
             if i == 6:
-                turned_sb = at("turned", [CHUNKS - 1, BANK], F32, "pairs0", 10)
-                for c in range(CHUNKS - 1):
-                    nc.scalar.copy(turned_sb[:, c], turn(c, staff_sb[last][:, c * BANK : (c + 1) * BANK])[:])
-                staff_banks = [turn(RESULT_BANKS + c, turned_sb[:, c]) for c in range(CHUNKS - 1)]
+                turned_sb = at("turned", [SHARE], F32, "pairs0", 10)
+                spans = [slice(first, min(first + BANK, SHARE)) for first in range(0, SHARE, BANK)]
+                for c, cols in enumerate(spans):
+                    nc.scalar.copy(turned_sb[:, cols], turn(c, staff_sb[last][:, cols])[:, : cols.stop - cols.start])
+                staff_banks = [turn(RESULT_BANKS + c, turned_sb[:, cols]) for c, cols in enumerate(spans)]
             place(i)
             if i in (3, 4, 5):
                 load_staff({3: 5, 4: 7, 5: 6}[i])
 
         load_last = load_sb[:, PASSES - 1, PACK - 1 : PACK]
-        loaded_last = at("loaded_last", [BANK], F32, "pairs0", 10)
-        nc.scalar.activation(loaded_last[:], pages[last % 2][:, T2 - BANK :], ACT.Identity, bias=load_last)
-        nc.gpsimd.tensor_tensor(z_pairs[1][:, CHUNKS - 1, 1, :, 1], loaded_last[:], staff_sb[last][:, T2 - BANK :], ALU.mult)
-        for c in range(CHUNKS - 1):
+        loaded_last = at("loaded_last", [T2 - SHARE], F32, "pairs0", 10)
+        for first, stop in ((SHARE, T2 - BANK), (T2 - BANK, T2)):
+            c, j = divmod(first, BANK)
+            rows = loaded_last[:, first - SHARE : stop - SHARE]
+            nc.scalar.activation(rows, pages[last % 2][:, first:stop], ACT.Identity, bias=load_last)
+            nc.gpsimd.tensor_tensor(z_pairs[1][:, c, 1, j : j + stop - first, 1], rows, staff_sb[last][:, first:stop], ALU.mult)
+        for first in range(0, SHARE, BANK):
+            c, width = first // BANK, min(BANK, SHARE - first)
             nc.vector.scalar_tensor_tensor(
-                z_pairs[1][:, c, 1, :, 1], pages[last % 2][:, c * BANK : (c + 1) * BANK], load_last, staff_banks[c][:],
+                z_pairs[1][:, c, 1, :width, 1], pages[last % 2][:, first : first + width], load_last, staff_banks[c][:, :width],
                 ALU.add, ALU.mult,
             )
         z_grouped[1] = at("z_grouped1", [CHUNKS, BANK, PACK], BF16, "woven")
         z_codes = [at("z_codes%d" % b, [T2], U32, "z_codes", 8 * b) for b in range(PASSES)]
         z_planes = at("z_planes", [PASSES, T2], U8, "pages", 8)
         y_sb = [at("y%d" % n, [T2], F32, "staff", 8 * (2, 3, 1)[n]) for n in range(OUT_TILES)]
-        sums = []
 
         def quantise_z(b, first, width):
             cols = slice(first, first + width)
@@ -381,32 +378,36 @@ def tile_list_theatre_turnover_slots_kernel(
                 in_=z_grouped[b][:, c, j : j + width].rearrange("p j t -> p (j t)"),
             )
 
-        def features(n, first, width, engine_copy):
+        def features(n, first, width, u):
             cols = slice(first, first + width)
-            acc = bank(len(sums) % RESULT_BANKS)
-            sums.append(acc)
+            acc = bank(u)
             for b in range(PASSES):
                 nc.tensor.matmul_mx(
                     out=acc[:, :width], lhsT=w3_codes[n][:, b].bitcast(FP8X4),
                     lhsT_scale=w3_planes[:, b, n * P : (n + 1) * P],
                     rhs=z_codes[b][:, cols].bitcast(FP8X4), rhs_scale=z_planes[:, b, cols], start=(b == 0), stop=(b == PASSES - 1),
                 )
-            engine_copy(y_sb[n][:, cols], acc[:, :width])
+            return y_sb[n][:, cols], acc[:, :width]
 
         for c in range(CHUNKS):
             interleave(1, c)
+        second = []
         for c in range(CHUNKS):
             quantise_z(0, c * BANK, BANK)
             if c < CHUNKS - 1:
                 quantise_z(1, c * BANK, BANK)
-                features(0, c * BANK, BANK, nc.scalar.copy)
-            if c == 1:
-                features(1, 0, BANK, nc.scalar.copy)
-        pieces = ((T2 - BANK, 256, nc.scalar.copy), (T2 - 256, P, nc.vector.tensor_copy), (T2 - P, P, nc.vector.tensor_copy))
-        for first, width, engine_copy in pieces:
+                nc.scalar.copy(*features(0, c * BANK, BANK, c))
+            if c < 2:
+                second.append(features(1, c * BANK, BANK, (4, 1)[c]))
+        pieces = ((T2 - BANK, 256, 3), (T2 - 256, P, 7), (T2 - P, P, 0))
+        for first, width, u in pieces:
             quantise_z(1, first, width)
-        for first, width, engine_copy in pieces:
-            features(0, first, width, engine_copy)
+        for first, width, u in pieces:
+            nc.vector.tensor_copy(*features(0, first, width, u))
+        for c in range(2, CHUNKS):
+            second.append(features(1, c * BANK, BANK, (3, 7)[c - 2]))
+        for target, acc in second:
+            nc.scalar.copy(target, acc)
 
         crew = [at("crew%d" % u, [T2], F32, "woven", 8 * u) for u in range(2)]
         for u in range(2):
@@ -415,27 +416,23 @@ def tile_list_theatre_turnover_slots_kernel(
         floored = {}
 
         def pick(n):
-            picked = at("picked%d" % n, [PK], F32, "larger", 4 * (n % 2))
+            picked = at("picked%d" % n, [PK], F32, "larger", 4 * n)
             nc.vector.tensor_tensor(picked[:], y_sb[n][:].indirect(list3[:]), delay_sb[n][:], ALU.add)
             return picked
 
         def floor(n, picked):
-            above = at("above%d" % n, [PK], F32, *(("w3", 2), ("w3", 6), ("larger", 8))[n])
+            above = at("above%d" % n, [PK], F32, "w3", 6)
             nc.scalar.activation(above[:], picked[:], ACT.Relu, bias=neg_low[:, n : n + 1])
-            floored[n] = at("floored%d" % n, [PK], F32, "weighted", 4 * (n % 2))
+            floored[n] = at("floored%d" % n, [PK], F32, "weighted", 4 * n)
             nc.scalar.activation(floored[n][:], above[:], ACT.Identity, bias=low_sb[:, n : n + 1])
 
         def hand_over(n):
             nc.vector.tensor_tensor(crew[n % 2][:].indirect(list4[:]), floored[n][:], wgo_sb[:], ALU.mult)
             nc.sync.dma_start(out[n * P : (n + 1) * P, :], crew[n % 2][:])
 
-        picked = {0: pick(0)}
+        for c in range(CHUNKS):
+            nc.scalar.copy(*features(2, c * BANK, BANK, (4, 1, 3, 7)[c]))
+        picked = [pick(n) for n in range(OUT_TILES)]
         for n in range(OUT_TILES):
-            if n + 1 < OUT_TILES:
-                for c in range(1 if n == 0 else 0, CHUNKS):
-                    features(n + 1, c * BANK, BANK, nc.scalar.copy)
-                picked[n + 1] = pick(n + 1)
-            if n > 0:
-                hand_over(n - 1)
             floor(n, picked[n])
-        hand_over(OUT_TILES - 1)
+            hand_over(n)

@@ -189,6 +189,11 @@ def tile_list_theatre_turnover_slots_kernel(
                 round_w1(0, u, slice(piece * P // 2, (piece + 1) * P // 2), w1_raw[piece], nc.scalar.copy)
         for u in range(2):
             quantise_w1(0, u)
+        for moving, moving_scales in 3 * [(w1_codes[0], v_scales)] + 2 * [(tab_w, tab_s)]:
+            nc.tensor.matmul_mx(
+                out=bank(7)[:], lhsT=w1_codes[0][:, :P].bitcast(FP8X4), lhsT_scale=w1_planes[0][:, :P],
+                rhs=moving[:, :BANK].bitcast(FP8X4), rhs_scale=moving_scales[:, :BANK], start=True, stop=True,
+            )
         gather_words(0)
         gather_words(1)
         for piece in range(2):
@@ -230,7 +235,7 @@ def tile_list_theatre_turnover_slots_kernel(
                 js, u = slice(half * BANK, (half + 1) * BANK), 2 * (i % 2) + half
                 team_sb = early[:, i, half] if i < 2 else at("team", [BANK], F32, "woven", 2 * u)[:]
                 nc.scalar.copy(team_sb, team_product(i, half, PACK + u)[:])
-                nc.vector.tensor_tensor(larger[i][:, js], room_product(i, half, u)[:], team_sb, ALU.max)
+                nc.vector.tensor_tensor(larger[i][:, js], team_sb, room_product(i, half, u)[:], ALU.max)
             if i == 0:
                 for e in range(2):
                     quantise_w1(1, e)

@@ -124,10 +124,10 @@ def tile_list_theatre_turnover_slots_kernel(
             nc.sync.dma_start(staff_sb[i][:], staff_rows[pass_and_byte(i)])
 
         load_gains(0, 1)
+        list2 = load_list(offs2, "list2")
         load_gains(1, 1)
         load_sb = at("load_sb", [PASSES, PACK], F32, "small", 0.5)
         nc.sync.dma_start(load_sb[:], load.rearrange("(b p t) -> p b t", p=P, t=PACK))
-        list2 = load_list(offs2, "list2")
         load_gains(2, 2)
         for i in range(STAFF_SLOTS):
             load_staff(i)
@@ -189,9 +189,9 @@ def tile_list_theatre_turnover_slots_kernel(
                 round_w1(0, u, slice(piece * P // 2, (piece + 1) * P // 2), w1_raw[piece], nc.scalar.copy)
         for u in range(2):
             quantise_w1(0, u)
-        for moving, moving_scales in 3 * [(w1_codes[0], v_scales)] + 2 * [(tab_w, tab_s)]:
+        for u, (moving, moving_scales) in enumerate(3 * [(w1_codes[0], v_scales)] + 2 * [(tab_w, tab_s)]):
             nc.tensor.matmul_mx(
-                out=bank(7)[:], lhsT=w1_codes[0][:, :P].bitcast(FP8X4), lhsT_scale=w1_planes[0][:, :P],
+                out=bank(3 + u)[:], lhsT=w1_codes[0][:, :P].bitcast(FP8X4), lhsT_scale=w1_planes[0][:, :P],
                 rhs=moving[:, :BANK].bitcast(FP8X4), rhs_scale=moving_scales[:, :BANK], start=True, stop=True,
             )
         gather_words(0)
@@ -357,22 +357,9 @@ def tile_list_theatre_turnover_slots_kernel(
             if i in (3, 4, 5):
                 load_staff({3: 5, 4: 7, 5: 6}[i])
 
-        load_last = load_sb[:, PASSES - 1, PACK - 1 : PACK]
-        loaded_last = at("loaded_last", [T2 - SHARE], F32, "pairs0", 10)
-        for first, stop in ((SHARE, T2 - BANK), (T2 - BANK, T2)):
-            c, j = divmod(first, BANK)
-            rows = loaded_last[:, first - SHARE : stop - SHARE]
-            nc.scalar.activation(rows, pages[last % 2][:, first:stop], ACT.Identity, bias=load_last)
-            nc.gpsimd.tensor_tensor(z_pairs[1][:, c, 1, j : j + stop - first, 1], rows, staff_sb[last][:, first:stop], ALU.mult)
-        for first in range(0, SHARE, BANK):
-            c, width = first // BANK, min(BANK, SHARE - first)
-            nc.vector.scalar_tensor_tensor(
-                z_pairs[1][:, c, 1, :width, 1], pages[last % 2][:, first : first + width], load_last, staff_banks[c][:, :width],
-                ALU.add, ALU.mult,
-            )
         z_grouped[1] = at("z_grouped1", [CHUNKS, BANK, PACK], BF16, "woven")
         z_codes = [at("z_codes%d" % b, [T2], U32, "z_codes", 8 * b) for b in range(PASSES)]
-        z_planes = at("z_planes", [PASSES, T2], U8, "pages", 8)
+        z_planes = at("z_planes", [PASSES, T2], U8, "staff", 32)
         y_sb = [at("y%d" % n, [T2], F32, "staff", 8 * (2, 3, 1)[n]) for n in range(OUT_TILES)]
 
         def quantise_z(b, first, width):
@@ -394,11 +381,26 @@ def tile_list_theatre_turnover_slots_kernel(
                 )
             return y_sb[n][:, cols], acc[:, :width]
 
+        quantise_z(0, 0, BANK)
+        load_last = load_sb[:, PASSES - 1, PACK - 1 : PACK]
+        loaded_last = at("loaded_last", [T2 - SHARE], F32, "pairs0", 10)
+        for first, stop in ((SHARE, T2 - BANK), (T2 - BANK, T2)):
+            c, j = divmod(first, BANK)
+            rows = loaded_last[:, first - SHARE : stop - SHARE]
+            nc.scalar.activation(rows, pages[last % 2][:, first:stop], ACT.Identity, bias=load_last)
+            nc.gpsimd.tensor_tensor(z_pairs[1][:, c, 1, j : j + stop - first, 1], rows, staff_sb[last][:, first:stop], ALU.mult)
+        for first in range(0, SHARE, BANK):
+            c, width = first // BANK, min(BANK, SHARE - first)
+            nc.vector.scalar_tensor_tensor(
+                z_pairs[1][:, c, 1, :width, 1], pages[last % 2][:, first : first + width], load_last, staff_banks[c][:, :width],
+                ALU.add, ALU.mult,
+            )
         for c in range(CHUNKS):
             interleave(1, c)
         second = []
         for c in range(CHUNKS):
-            quantise_z(0, c * BANK, BANK)
+            if c > 0:
+                quantise_z(0, c * BANK, BANK)
             if c < CHUNKS - 1:
                 quantise_z(1, c * BANK, BANK)
                 nc.scalar.copy(*features(0, c * BANK, BANK, c))
@@ -408,7 +410,7 @@ def tile_list_theatre_turnover_slots_kernel(
         for first, width, u in pieces:
             quantise_z(1, first, width)
         for first, width, u in pieces:
-            nc.vector.tensor_copy(*features(0, first, width, u))
+            (nc.vector.tensor_copy if first + width == T2 - P else nc.scalar.copy)(*features(0, first, width, u))
         for c in range(2, CHUNKS):
             second.append(features(1, c * BANK, BANK, (3, 7)[c - 2]))
         for target, acc in second:

@@ -81,8 +81,8 @@ def tile_list_theatre_turnover_slots_kernel(
         w1_grouped = {
             (0, 0): at("w1_grouped00", [2, P, PACK], BF16, "w1_early"),
             (0, 1): at("w1_grouped01", [2, P, PACK], BF16, "w1_early", 2),
-            (1, 0): at("w1_grouped10", [2, P, PACK], BF16, "weighted", 15),
-            (1, 1): at("w1_grouped11", [2, P, PACK], BF16, "larger", 8),
+            (1, 0): at("w1_grouped10", [2, P, PACK], BF16, "larger", 8),
+            (1, 1): at("w1_grouped11", [2, P, PACK], BF16, "weighted", 15),
         }
         w1_rows = w1.rearrange("(p j) c -> p j c", j=PACK)
         v_scales = at("v_scales", [S], U8, "v_scales")

@@ -82,7 +82,7 @@ def tile_list_theatre_turnover_slots_kernel(
             (0, 0): at("w1_grouped00", [2, P, PACK], BF16, "w1_early"),
             (0, 1): at("w1_grouped01", [2, P, PACK], BF16, "w1_early", 2),
             (1, 0): at("w1_grouped10", [2, P, PACK], BF16, "larger", 8),
-            (1, 1): at("w1_grouped11", [2, P, PACK], BF16, "weighted", 15),
+            (1, 1): at("w1_grouped11", [4, P, PACK], BF16, "weighted", 13),
         }
         w1_rows = w1.rearrange("(p j) c -> p j c", j=PACK)
         v_scales = at("v_scales", [S], U8, "v_scales")
@@ -108,13 +108,11 @@ def tile_list_theatre_turnover_slots_kernel(
             load_w1(u)
 
         wgs_rows = wgs.rearrange("(q t) j -> q t j", t=PACK)
-        gains = []
+        gains = [at("gains%d" % t, [S], F32, "gains", 4 * t) for t in range(PACK)]
 
-        def load_gains(first, count):
-            rows = at("gains%d" % first, [count, S], F32, "gains", 4 * first)
+        def load_gains(t, js):
             for g in (0, 2, 1, 3):
-                nc.sync.dma_start(rows[32 * g : 32 * (g + 1)], wgs_rows[:, first : first + count])
-            gains.extend([rows[:, u] for u in range(count)])
+                nc.sync.dma_start(gains[t][32 * g : 32 * (g + 1), js], wgs_rows[:, t, js])
 
         staff_rows = staff.rearrange("(b p t) c -> b t p c", p=P, t=PACK)
         staff_sb = {}
@@ -123,12 +121,14 @@ def tile_list_theatre_turnover_slots_kernel(
             staff_sb[i] = at("staff%d" % i, [T2], F32, "staff", 8 * (0, 1, 2, 3, 4, 2, 1, 0)[i])
             nc.sync.dma_start(staff_sb[i][:], staff_rows[pass_and_byte(i)])
 
-        load_gains(0, 1)
+        load_gains(0, slice(0, BANK))
         list2 = load_list(offs2, "list2")
-        load_gains(1, 1)
+        load_gains(0, slice(BANK, S))
+        load_gains(1, slice(0, S))
         load_sb = at("load_sb", [PASSES, PACK], F32, "small", 0.5)
         nc.sync.dma_start(load_sb[:], load.rearrange("(b p t) -> p b t", p=P, t=PACK))
-        load_gains(2, 2)
+        for t in range(2, PACK):
+            load_gains(t, slice(0, S))
         for i in range(STAFF_SLOTS):
             load_staff(i)
         w3_codes = [at("w3_codes%d" % n, [PASSES, P], U32, "w3", (0, 2, 6)[n]) for n in range(OUT_TILES)]
@@ -148,7 +148,7 @@ def tile_list_theatre_turnover_slots_kernel(
 
         def round_w1(b, u, ms, rows, engine_copy):
             engine_copy(
-                w1_grouped[b, u][:].rearrange("p t m j -> p m t j")[:, ms],
+                w1_grouped[b, u][:, :2].rearrange("p t m j -> p m t j")[:, ms],
                 rows[:].rearrange("p j (m t) -> p m t j", t=PACK)[:, :, 2 * u : 2 * u + 2],
             )
 
@@ -159,7 +159,7 @@ def tile_list_theatre_turnover_slots_kernel(
             cols = slice(u * 2 * P, (u + 1) * 2 * P)
             nc.vector.quantize_mx(
                 out=w1_codes[b][:, cols].bitcast(FP8X4), scales=w1_planes[b][:, cols],
-                in_=w1_grouped[b, u][:].rearrange("p t m j -> p (t m j)"),
+                in_=w1_grouped[b, u][:, :2].rearrange("p t m j -> p (t m j)"),
             )
 
         def order_w2_scales(b):
@@ -221,11 +221,11 @@ def tile_list_theatre_turnover_slots_kernel(
             return room
 
         larger, weighted = {}, {}
-        WEIGHTED_AT = (("weighted", 12), ("weighted", 16), ("weighted", 4), ("weighted", 8), ("staff", 0), ("staff", 8), ("staff", 24), ("staff", 32))
+        WEIGHTED_AT = (None, ("weighted", 16), ("weighted", 4), ("weighted", 8), ("staff", 0), ("staff", 8), ("staff", 24), ("staff", 32))
 
         def weigh(i):
             weighted[i] = at("weighted%d" % i, [S], F32, *WEIGHTED_AT[i])
-            nc.gpsimd.tensor_tensor(weighted[i][:], larger[i][:], gains[pass_and_byte(i)[1]], ALU.mult)
+            nc.gpsimd.tensor_tensor(weighted[i][:], larger[i][:], gains[pass_and_byte(i)[1]][:], ALU.mult)
 
         for i in range(PACK):
             larger[i] = at("larger%d" % i, [S], F32, "larger", 4 * i)
@@ -239,7 +239,11 @@ def tile_list_theatre_turnover_slots_kernel(
             if i == 0:
                 for e in range(2):
                     quantise_w1(1, e)
-        for i in range(PACK):
+        first_halves = [at("weighted0%d" % half, [BANK], F32, "weighted", (14, 12)[half]) for half in range(2)]
+        for half in range(2):
+            js = slice(half * BANK, (half + 1) * BANK)
+            nc.gpsimd.tensor_tensor(first_halves[half][:], larger[0][:, js], gains[0][:, js], ALU.mult)
+        for i in range(1, PACK):
             weigh(i)
 
         def turn(u, *terms):
@@ -297,7 +301,11 @@ def tile_list_theatre_turnover_slots_kernel(
                 weigh(i)
 
         def place(i):
-            nc.vector.tensor_copy(pages[i % 2][:].indirect(list2[:]), weighted[i][:])
+            if i == 0:
+                for half in range(2):
+                    nc.vector.tensor_copy(pages[0][:].indirect(list2[:, half * 32 : (half + 1) * 32]), first_halves[half][:])
+            else:
+                nc.vector.tensor_copy(pages[i % 2][:].indirect(list2[:]), weighted[i][:])
 
         z_pairs = [at("z_pairs%d" % b, [CHUNKS, 2, BANK, 2], BF16, "pairs%d" % b) for b in range(PASSES)]
         last = ROW_TILES - 1
@@ -340,7 +348,7 @@ def tile_list_theatre_turnover_slots_kernel(
             if i == 5:
                 wgo_sb = at("wgo", [PK], F32, "wgo")
                 nc.sync.dma_start(wgo_sb[:], wgo)
-                delay_sb = [at("delay%d" % n, [PK], F32, "gains", 4 * n) for n in range(OUT_TILES)]
+                delay_sb = [at("delay%d" % n, [PK], F32, "weighted", (0, 12, 16)[n]) for n in range(OUT_TILES)]
                 for n in range(OUT_TILES):
                     nc.sync.dma_start(delay_sb[n][:], delay[n * P : (n + 1) * P, :])
             if i == 5:
@@ -430,7 +438,7 @@ def tile_list_theatre_turnover_slots_kernel(
         def floor(n, picked):
             above = at("above%d" % n, [PK], F32, "w3", 6)
             nc.scalar.activation(above[:], picked[:], ACT.Relu, bias=neg_low[:, n : n + 1])
-            floored[n] = at("floored%d" % n, [PK], F32, "weighted", 4 * n)
+            floored[n] = at("floored%d" % n, [PK], F32, "gains", 4 * n)
             nc.scalar.activation(floored[n][:], above[:], ACT.Identity, bias=low_sb[:, n : n + 1])
 
         def hand_over(n):

@@ -22,21 +22,45 @@ PACK = 4
 BANK = 512
 PASSES = H // (P * PACK)
 ROW_TILES = PASSES * PACK
+LAST = ROW_TILES - 1
 CHUNKS = T2 // BANK
 OUT_TILES = N // P
 STAFF_SLOTS = 5
-RESULT_BANKS = 4
-FROM_BANK = ()
-SHARE = T2 - 768
+ON_VECTOR = T2 - 768
+WARM_UPS = 3
 
 KB = 1024
 AREAS = (
-    ("small", 1), ("v_words", 4), ("v_scales", 1), ("w1_early", 4), ("w1_codes", 4), ("w1_planes", 1),
-    ("w2_codes", 2), ("w2_planes", 1), ("gains", 16), ("pages", 16), ("staff", 8 * STAFF_SLOTS), ("loaded0", 8),
-    ("z_codes", 16), ("loaded1", 8.25), ("work", 16), ("pairs1", 16), ("pairs0", 16), ("woven", 16), ("larger", 16), ("weighted", 20),
-    ("w3", 10), ("wgo", 4),
+    ("small", 1), ("v_words", 4), ("v_scales", 1), ("w1_early", 4), ("w1_codes", 4),
+    ("w2_codes", 2), ("w2_planes", 1), ("gains", 16), ("pages", 16), ("staff", 8 * STAFF_SLOTS), ("w1_planes", 1), ("loaded0", 8),
+    ("z_codes", 16), ("loaded1", 8.25), ("work", 16), ("pairs1", 16), ("pairs0", 16), ("woven", 16), ("larger", 16),
+    ("weighted", 20), ("w3", 10), ("wgo", 4),
 )
 AT = {name: int(KB * sum(size for other, size in AREAS[:u])) for u, (name, size) in enumerate(AREAS)}
+
+STAFF_SLOT = (0, 1, 2, 3, 4, 2, 1, 0)
+WEIGHTED_AT = (None, ("weighted", 16), ("weighted", 4), ("weighted", 8), ("staff", 0), ("staff", 8), ("staff", 24), ("staff", 32))
+LARGER_AT = (("larger", 0), ("larger", 4), ("larger", 8), ("larger", 12), ("larger", 0), ("larger", 4), ("staff", 12), ("larger", 12))
+LOADED_AT = (("loaded0", 0), ("loaded1", 0), ("loaded0", 0), ("loaded1", 0.0625), ("loaded0", 0), ("pairs0", 0), ("pairs0", 14.9375))
+WORK_AT = {
+    (4, 0): (("z_codes", 4), ("z_codes", 6), ("z_codes", 4), ("z_codes", 6)),
+    (4, 1): (("z_codes", 8), ("z_codes", 10), ("z_codes", 8), ("z_codes", 10)),
+    (5, 0): (("z_codes", 14), ("loaded0", 2), ("loaded1", 0), ("loaded1", 2)),
+    (5, 1): (("work", 8), ("work", 10), ("work", 8), ("work", 10)),
+    (6, 0): (("work", 4), ("loaded0", 7), ("loaded1", 8), ("z_codes", 6)),
+    (6, 1): (("z_codes", 8), ("z_codes", 10), ("staff", 4), ("staff", 6)),
+    (7, 0): (("work", 2.5), ("work", 5.5), ("loaded0", 0), ("loaded0", 2)),
+    (7, 1): (("z_codes", 0), ("z_codes", 12), ("loaded0", 4), ("work", 8)),
+}
+
+
+def pass_and_byte(i):
+    b, s = divmod(i, PACK)
+    return b, (s if b == 0 else (2, 0, 1, 3)[s])
+
+
+def half_cols(half):
+    return slice(half * BANK, (half + 1) * BANK)
 
 
 def tile_list_theatre_turnover_slots_kernel(
@@ -61,51 +85,44 @@ def tile_list_theatre_turnover_slots_kernel(
             nc.sync.dma_start(tile[:], source)
             return tile
 
-        def load_scale_rows(plane, rows):
-            for r in range(4):
-                nc.sync.dma_start(plane[r:P:32].bitcast(I32), rows[r:16:4].bitcast(I32))
-
-        def pass_and_byte(i):
-            b, s = divmod(i, PACK)
-            return b, (s if b == 0 else (2, 0, 1, 3)[s])
+        def zero_on_vector(tile):
+            words = tile[:].bitcast(I32)
+            cut = words.shape[1] // 2 + 1
+            nc.vector.memset(words[:, :cut], 0)
+            nc.vector.memset(words[:, cut:], 0)
 
         tab_s = at("tab_s", [T], U8, "work")
         tab_w = at("tab_w", [T], U32, "pairs0")
-        w2_raw = at("w2_raw", [2 * H], U8, "woven", 8)
-        w2_s_raw = at("w2_s_raw", [H], U8, "pages", 8)
-        w2_codes = at("w2_codes", [2 * H], U8, "w2_codes")
-        w2_planes = at("w2_planes", [H], U8, "w2_planes")
-        w1_codes = [at("w1_codes%d" % b, [BANK], U32, "w1_codes", 2 * b) for b in range(PASSES)]
-        w1_planes = [at("w1_planes%d" % b, [BANK], U8, "w1_planes", b / 2) for b in range(PASSES)]
-        w1_raw = [at("w1_raw%d" % u, [PACK, BANK // 2], F32, ("pairs1", "loaded0", "pairs1", "pairs1")[u], (0, 0, 4, 8)[u]) for u in range(4)]
-        w1_grouped = {
-            (0, 0): at("w1_grouped00", [2, P, PACK], BF16, "w1_early"),
-            (0, 1): at("w1_grouped01", [2, P, PACK], BF16, "w1_early", 2),
-            (1, 0): at("w1_grouped10", [2, P, PACK], BF16, "larger", 8),
-            (1, 1): at("w1_grouped11", [4, P, PACK], BF16, "weighted", 13),
-        }
-        w1_rows = w1.rearrange("(p j) c -> p j c", j=PACK)
+        picked_s = at("picked_s", [S], U8, "woven", 11)
         v_scales = at("v_scales", [S], U8, "v_scales")
+        w2_raw = at("w2_raw", [2 * H], U8, "woven", 8)
+        w2_s_raw = at("w2_s_raw", [H], U8, "woven", 10)
+        w3_planes = at("w3_planes", [PASSES * N], U8, "w3", 1)
+        pages = [at("page%d" % u, [T2], F32, "pages", 8 * u) for u in range(2)]
         identity = at("identity", [P], F32, "small")
-        pages = [at("page0", [T2], F32, "pages")]
+        w1_first = at("w1_first", [PACK, BANK], F32, "loaded0")
+        w1_late = [at("w1_late%d" % u, [PACK, BANK // 2], F32, "pairs1", 4 + 4 * u) for u in range(2)]
 
-        nc.gpsimd.memset(w2_s_raw[:].bitcast(I32), 0)
-        nc.vector.memset(tab_s[:, : T // 2].bitcast(I32), 0)
-        nc.gpsimd.memset(tab_s[:, T // 2 :].bitcast(I32), 0)
+        nc.gpsimd.memset(tab_s[:].bitcast(I32), 0)
+        for tile in (w2_s_raw, v_scales, w3_planes, pages[0]):
+            zero_on_vector(tile)
+        nc.gpsimd.memset(pages[1][:], 0.0)
         make_identity(nc, identity[:])
 
-        def load_w1(u):
-            nc.sync.dma_start(w1_raw[u][:], w1_rows[:, :, u * BANK // 2 : (u + 1) * BANK // 2])
+        w1_rows = w1.rearrange("(p j) c -> p j c", j=PACK)
 
-        load_w1(0)
-        load_scale_rows(w2_s_raw, w2_scales[0])
-        load_w1(1)
-        nc.sync.dma_start(w2_raw[:].bitcast(I32), w2_words[0].bitcast(I32))
         list1 = load_list(offs, "list1")
-        load_scale_rows(tab_s, tab_scales[0])
+        nc.sync.dma_start(w1_first[:], w1_rows[:, :, :BANK])
+        nc.sync.dma_start(tab_s[0:P:8].bitcast(I32), tab_scales[0].bitcast(I32))
+        nc.sync.dma_start(w2_raw[:].bitcast(I32), w2_words[0].bitcast(I32))
+        for r in range(4):
+            nc.sync.dma_start(w2_s_raw[r:P:32].bitcast(I32), w2_scales[0][r:16:4].bitcast(I32))
         nc.sync.dma_start(tab_w[:].bitcast(I32), tab_words[0].rearrange("p t i -> p (t i)").bitcast(I32))
-        for u in range(2, 4):
-            load_w1(u)
+        nc.vector.tensor_copy(picked_s[:], tab_s[:].indirect(list1[:]))
+        for r in range(4):
+            nc.sync.dma_start(v_scales[r:P:32].bitcast(I32), picked_s[8 * r : P : 32].bitcast(I32))
+        for u in range(2):
+            nc.sync.dma_start(w1_late[u][:], w1_rows[:, :, BANK + u * BANK // 2 : BANK + (u + 1) * BANK // 2])
 
         wgs_rows = wgs.rearrange("(q t) j -> q t j", t=PACK)
         gains = [at("gains%d" % t, [S], F32, "gains", 4 * t) for t in range(PACK)]
@@ -118,12 +135,12 @@ def tile_list_theatre_turnover_slots_kernel(
         staff_sb = {}
 
         def load_staff(i):
-            staff_sb[i] = at("staff%d" % i, [T2], F32, "staff", 8 * (0, 1, 2, 3, 4, 2, 1, 0)[i])
+            staff_sb[i] = at("staff%d" % i, [T2], F32, "staff", 8 * STAFF_SLOT[i])
             nc.sync.dma_start(staff_sb[i][:], staff_rows[pass_and_byte(i)])
 
-        load_gains(0, slice(0, BANK))
+        load_gains(0, half_cols(0))
         list2 = load_list(offs2, "list2")
-        load_gains(0, slice(BANK, S))
+        load_gains(0, half_cols(1))
         load_gains(1, slice(0, S))
         load_sb = at("load_sb", [PASSES, PACK], F32, "small", 0.5)
         nc.sync.dma_start(load_sb[:], load.rearrange("(b p t) -> p b t", p=P, t=PACK))
@@ -132,13 +149,15 @@ def tile_list_theatre_turnover_slots_kernel(
         for i in range(STAFF_SLOTS):
             load_staff(i)
         w3_codes = [at("w3_codes%d" % n, [PASSES, P], U32, "w3", (0, 2, 6)[n]) for n in range(OUT_TILES)]
-        w3_planes = at("w3_planes", [PASSES, N], U8, "w3", 1)
-        nc.gpsimd.memset(w3_planes[:].bitcast(I32), 0)
         for n in range(OUT_TILES):
             nc.sync.dma_start(
                 w3_codes[n][:].bitcast(I32), w3_words[:, :, n * P : (n + 1) * P].rearrange("a p c i -> p a (c i)").bitcast(I32)
             )
-        load_scale_rows(w3_planes, w3_scales.rearrange("a q c -> q a c"))
+        for r in range(4):
+            nc.sync.dma_start(
+                w3_planes[r:P:32].bitcast(I32).rearrange("q (a c) -> q a c", a=PASSES),
+                w3_scales.rearrange("a q c -> q a c")[r:16:4].bitcast(I32),
+            )
         list3 = load_list(offs3, "list3")
         list4 = load_list(offs4, "list4")
         low_sb = at("low_sb", [OUT_TILES], F32, "small", 0.5625)
@@ -146,67 +165,59 @@ def tile_list_theatre_turnover_slots_kernel(
         with nc.allow_non_contiguous_dma(reason="one value a partition"):
             nc.sync.dma_start(low_sb[:], low.rearrange("(n p) -> p n", p=P))
 
+        w2_codes = at("w2_codes", [2 * H], U8, "w2_codes")
+        w2_planes = at("w2_planes", [H], U8, "w2_planes")
+        w1_codes = [at("w1_codes%d" % b, [BANK], U32, "w1_codes", 2 * b) for b in range(PASSES)]
+        w1_planes = [at("w1_planes%d" % b, [BANK], U8, "w1_planes", b / 2) for b in range(PASSES)]
+        w1_grouped = [at("w1_grouped%d" % b, [PACK, P, PACK], BF16, *(("w1_early", 0), ("weighted", 13))[b]) for b in range(PASSES)]
+
         def round_w1(b, u, ms, rows, engine_copy):
             engine_copy(
-                w1_grouped[b, u][:, :2].rearrange("p t m j -> p m t j")[:, ms],
+                w1_grouped[b][:, 2 * u : 2 * u + 2].rearrange("p t m j -> p m t j")[:, ms],
                 rows[:].rearrange("p j (m t) -> p m t j", t=PACK)[:, :, 2 * u : 2 * u + 2],
             )
 
         def gpsimd_copy(target, source):
             nc.gpsimd.tensor_scalar(target, source, 1.0, 0.0, ALU.mult, ALU.add)
 
-        def quantise_w1(b, u):
-            cols = slice(u * 2 * P, (u + 1) * 2 * P)
+        def quantise_w1(b):
             nc.vector.quantize_mx(
-                out=w1_codes[b][:, cols].bitcast(FP8X4), scales=w1_planes[b][:, cols],
-                in_=w1_grouped[b, u][:, :2].rearrange("p t m j -> p (t m j)"),
+                out=w1_codes[b][:].bitcast(FP8X4), scales=w1_planes[b][:], in_=w1_grouped[b][:].rearrange("p t m j -> p (t m j)"),
             )
 
-        def order_w2_scales(b):
-            nc.vector.tensor_copy(
-                w2_planes[:, b * BANK : (b + 1) * BANK].rearrange("p (t m) -> p t m", t=PACK),
-                w2_s_raw[:, b * BANK : (b + 1) * BANK].rearrange("p (m t) -> p t m", t=PACK),
-            )
-
-        v_words = []
-
-        def gather_words(half):
-            v_words.append(at("v_words%d" % half, [BANK], U32, "v_words", 2 * half))
-            nc.vector.tensor_copy(v_words[half][:], tab_w[:].indirect(list1[:, half * 32 : (half + 1) * 32]))
-
-        nc.vector.memset(pages[0][:], 0.0)
+        for u in range(2):
+            round_w1(0, u, slice(0, P), w1_first, nc.scalar.copy)
+        quantise_w1(0)
         nc.vector.tensor_copy(
             w2_codes[:].bitcast(U16).rearrange("p (b t m) -> p b t m", b=PASSES, t=PACK),
             w2_raw[:].bitcast(U16).rearrange("p (b m t) -> p b t m", b=PASSES, t=PACK),
         )
         for b in range(PASSES):
-            order_w2_scales(b)
-        pages.append(at("page1", [T2], F32, "pages", 8))
-        nc.gpsimd.memset(pages[1][:], 0.0)
-        nc.vector.tensor_copy(v_scales[:], tab_s[:].indirect(list1[:]))
-        for piece in range(2):
-            for u in range(2):
-                round_w1(0, u, slice(piece * P // 2, (piece + 1) * P // 2), w1_raw[piece], nc.scalar.copy)
-        for u in range(2):
-            quantise_w1(0, u)
-        for u, (moving, moving_scales) in enumerate(3 * [(w1_codes[0], v_scales)] + 2 * [(tab_w, tab_s)]):
-            nc.tensor.matmul_mx(
-                out=bank(3 + u)[:], lhsT=w1_codes[0][:, :P].bitcast(FP8X4), lhsT_scale=w1_planes[0][:, :P],
-                rhs=moving[:, :BANK].bitcast(FP8X4), rhs_scale=moving_scales[:, :BANK], start=True, stop=True,
+            nc.vector.tensor_copy(
+                w2_planes[:, half_cols(b)].rearrange("p (t m) -> p t m", t=PACK),
+                w2_s_raw[:, half_cols(b)].rearrange("p (m t) -> p t m", t=PACK),
             )
-        gather_words(0)
-        gather_words(1)
+        for u in range(WARM_UPS):
+            nc.tensor.matmul_mx(
+                out=bank(1 + u)[:], lhsT=w2_codes[:, : 2 * P].bitcast(FP4X4), lhsT_scale=w2_planes[:, :P],
+                rhs=w1_codes[0][:].bitcast(FP8X4), rhs_scale=w1_planes[0][:], start=True, stop=True,
+            )
+        v_words = [at("v_words%d" % half, [BANK], U32, "v_words", 2 * half) for half in range(2)]
+        for half, first, stop in ((0, 0, BANK // 2), (0, BANK // 2, BANK), (1, 0, BANK)):
+            entries = list1[:, (half * BANK + first) // 16 : (half * BANK + stop) // 16]
+            nc.vector.tensor_copy(v_words[half][:, first:stop], tab_w[:].indirect(entries))
         for piece in range(2):
             for u in range(2):
-                round_w1(1, u, slice(piece * P // 2, (piece + 1) * P // 2), w1_raw[2 + piece], gpsimd_copy)
+                round_w1(1, u, slice(piece * P // 2, (piece + 1) * P // 2), w1_late[piece], gpsimd_copy)
 
-        def team_product(i, half, u):
+        def team_product(i, half, u, first=0, stop=BANK):
             b, t = pass_and_byte(i)
             cols = slice((b * PACK + t) * P, (b * PACK + t + 1) * P)
-            team = bank(u)
+            team = bank(u)[:, : stop - first]
             nc.tensor.matmul_mx(
-                out=team[:], lhsT=w2_codes[:, 2 * cols.start : 2 * cols.stop].bitcast(FP4X4), lhsT_scale=w2_planes[:, cols],
-                rhs=v_words[half][:].bitcast(FP8X4), rhs_scale=v_scales[:, half * BANK : (half + 1) * BANK], start=True, stop=True,
+                out=team, lhsT=w2_codes[:, 2 * cols.start : 2 * cols.stop].bitcast(FP4X4), lhsT_scale=w2_planes[:, cols],
+                rhs=v_words[half][:, first:stop].bitcast(FP8X4),
+                rhs_scale=v_scales[:, half * BANK + first : half * BANK + stop], start=True, stop=True,
             )
             return team
 
@@ -216,33 +227,34 @@ def tile_list_theatre_turnover_slots_kernel(
             nc.tensor.matmul_mx(
                 out=room[:], lhsT=w1_codes[b][:, t * P : (t + 1) * P].bitcast(FP8X4),
                 lhsT_scale=w1_planes[b][:, t * P : (t + 1) * P],
-                rhs=v_words[half][:].bitcast(FP8X4), rhs_scale=v_scales[:, half * BANK : (half + 1) * BANK], start=True, stop=True,
+                rhs=v_words[half][:].bitcast(FP8X4), rhs_scale=v_scales[:, half_cols(half)], start=True, stop=True,
             )
             return room
 
         larger, weighted = {}, {}
-        WEIGHTED_AT = (None, ("weighted", 16), ("weighted", 4), ("weighted", 8), ("staff", 0), ("staff", 8), ("staff", 24), ("staff", 32))
 
         def weigh(i):
             weighted[i] = at("weighted%d" % i, [S], F32, *WEIGHTED_AT[i])
             nc.gpsimd.tensor_tensor(weighted[i][:], larger[i][:], gains[pass_and_byte(i)[1]][:], ALU.mult)
 
         for i in range(PACK):
-            larger[i] = at("larger%d" % i, [S], F32, "larger", 4 * i)
-        early = at("team_early", [2, 2, BANK], F32, "loaded0")
-        for i in range(PACK):
-            for half in range(2):
-                js, u = slice(half * BANK, (half + 1) * BANK), 2 * (i % 2) + half
-                team_sb = early[:, i, half] if i < 2 else at("team", [BANK], F32, "woven", 2 * u)[:]
-                nc.scalar.copy(team_sb, team_product(i, half, PACK + u)[:])
-                nc.vector.tensor_tensor(larger[i][:, js], team_sb, room_product(i, half, u)[:], ALU.max)
-            if i == 0:
+            larger[i] = at("larger%d" % i, [S], F32, *LARGER_AT[i])
+        early = at("team_early", [2, 2, BANK], F32, "loaded0", -0.0625)
+        for i, half in ((0, 0), (1, 0), (0, 1), (1, 1), (2, 0), (2, 1), (3, 0), (3, 1)):
+            u = 2 * (i % 2) + half
+            team_sb = early[:, i, half] if i < 2 else at("team", [BANK], F32, "woven", 2 * u)[:]
+            if (i, half) == (0, 0):
                 for e in range(2):
-                    quantise_w1(1, e)
+                    first, stop = e * BANK // 2, (e + 1) * BANK // 2
+                    nc.scalar.copy(team_sb[:, first:stop], team_product(i, half, PACK + e, first, stop))
+            else:
+                nc.scalar.copy(team_sb, team_product(i, half, PACK + u))
+            nc.vector.tensor_tensor(larger[i][:, half_cols(half)], team_sb, room_product(i, half, u)[:], ALU.max)
+            if (i, half) == (1, 1):
+                quantise_w1(1)
         first_halves = [at("weighted0%d" % half, [BANK], F32, "weighted", (14, 12)[half]) for half in range(2)]
         for half in range(2):
-            js = slice(half * BANK, (half + 1) * BANK)
-            nc.gpsimd.tensor_tensor(first_halves[half][:], larger[0][:, js], gains[0][:, js], ALU.mult)
+            nc.gpsimd.tensor_tensor(first_halves[half][:], larger[0][:, half_cols(half)], gains[0][:, half_cols(half)], ALU.mult)
         for i in range(1, PACK):
             weigh(i)
 
@@ -256,16 +268,6 @@ def tile_list_theatre_turnover_slots_kernel(
                     )
             return turned
 
-        WORK_AT = {
-            (4, 0): (("z_codes", 4), ("z_codes", 6), ("z_codes", 4), ("z_codes", 6)),
-            (4, 1): (("z_codes", 8), ("z_codes", 10), ("z_codes", 8), ("z_codes", 10)),
-            (5, 0): (("z_codes", 14), ("loaded0", 2), ("loaded1", 0), ("loaded1", 2)),
-            (5, 1): (("work", 8), ("work", 10), ("work", 8), ("work", 10)),
-            (6, 0): (("work", 4), ("loaded0", 7), ("loaded1", 8), ("z_codes", 6)),
-            (6, 1): (("z_codes", 8), ("z_codes", 10), ("staff", 4), ("staff", 6)),
-            (7, 0): (("work", 2.5), ("work", 5.5), ("loaded0", 0), ("loaded0", 2)),
-            (7, 1): (("loaded0", 8), ("z_codes", 12), ("loaded0", 4), ("work", 8)),
-        }
         pending = {}
 
         def work_tile(i, half, e):
@@ -275,7 +277,7 @@ def tile_list_theatre_turnover_slots_kernel(
             u = 4 * ((i + 1) % 2) + 2 * half
             team, room = team_product(i, half, u), room_product(i, half, u + 1)
             minus_team, room_sb = work_tile(i, half, 0), work_tile(i, half, 1)
-            nc.scalar.activation(minus_team[:], team[:], ACT.Copy, scale=-1.0)
+            nc.scalar.activation(minus_team[:], team, ACT.Copy, scale=-1.0)
             nc.scalar.copy(room_sb[:], room[:])
             difference = turn(u + 1, minus_team, room_sb)
             pending[i, half] = (turn(u, minus_team), difference)
@@ -288,15 +290,9 @@ def tile_list_theatre_turnover_slots_kernel(
             pending[i, half] = turn(4 * ((i + 1) % 2) + 2 * half, team_sb, excess)
 
         def collect(i, half):
-            js = slice(half * BANK, (half + 1) * BANK)
-            if i in FROM_BANK:
-                if half == 0:
-                    weighted[i] = at("weighted%d" % i, [S], F32, *WEIGHTED_AT[i])
-                nc.vector.tensor_tensor(weighted[i][:, js], pending[i, half][:], gains[pass_and_byte(i)[1]][:, js], ALU.mult)
-                return
             if half == 0:
-                larger[i] = at("larger%d" % i, [S], F32, *(("staff", 12) if i == 6 else ("larger", 4 * (i % PACK))))
-            nc.scalar.copy(larger[i][:, js], pending[i, half][:])
+                larger[i] = at("larger%d" % i, [S], F32, *LARGER_AT[i])
+            nc.scalar.copy(larger[i][:, half_cols(half)], pending[i, half][:])
             if half == 1:
                 weigh(i)
 
@@ -308,12 +304,11 @@ def tile_list_theatre_turnover_slots_kernel(
                 nc.vector.tensor_copy(pages[i % 2][:].indirect(list2[:]), weighted[i][:])
 
         z_pairs = [at("z_pairs%d" % b, [CHUNKS, 2, BANK, 2], BF16, "pairs%d" % b) for b in range(PASSES)]
-        last = ROW_TILES - 1
 
         def staffed(i):
             b, t = pass_and_byte(i)
-            loaded = at("loaded%d" % i, [T2], F32, *(("pairs0", 0) if i == 5 else ("pairs0", 14.9375) if i == 6 else ("loaded%d" % (i % 2), 0.0625 * (i == 3))))
-            for chunks in (slice(0, 1), slice(1, CHUNKS)) if i in (0, last - 1) else (slice(0, CHUNKS),):
+            loaded = at("loaded%d" % i, [T2], F32, *LOADED_AT[i])
+            for chunks in (slice(0, 1), slice(1, CHUNKS)) if i in (0, LAST - 1) else (slice(0, CHUNKS),):
                 cols = slice(chunks.start * BANK, chunks.stop * BANK)
                 nc.scalar.activation(loaded[:, cols], pages[i % 2][:, cols], ACT.Identity, bias=load_sb[:, b, t : t + 1])
                 nc.gpsimd.tensor_tensor(
@@ -330,37 +325,38 @@ def tile_list_theatre_turnover_slots_kernel(
                 z_pairs[b][:, c].rearrange("p u j e -> p u (j e)").bitcast(U32).rearrange("p u j -> p j u"),
             )
 
-        ahead = [(subtract, 4, 0), (subtract, 4, 1), (subtract, 5, 0), (subtract, 5, 1), (clip, 4, 0), (clip, 4, 1)]
+        def both(step, i):
+            for half in range(2):
+                step(i, half)
+
         beside = {
-            1: [(collect, 4, 0), (collect, 4, 1), (clip, 5, 0), (clip, 5, 1)],
-            2: [(subtract, 6, 0), (subtract, 6, 1), (collect, 5, 0), (collect, 5, 1)],
-            3: [(clip, 6, 0), (clip, 6, 1), (subtract, 7, 0), (subtract, 7, 1)],
-            4: [(collect, 6, 0), (collect, 6, 1), (clip, 7, 0), (clip, 7, 1)],
-            5: [(collect, 7, 0), (collect, 7, 1)],
+            0: ((subtract, 4), (subtract, 5), (clip, 4)),
+            1: ((collect, 4), (clip, 5)),
+            2: ((subtract, 6), (collect, 5)),
+            3: ((clip, 6), (subtract, 7)),
+            4: ((collect, 6), (clip, 7)),
+            5: ((collect, 7),),
         }
-        for step, i, half in ahead:
-            step(i, half)
         for i in range(ROW_TILES):
             if i > 0:
                 staffed(i - 1)
-            for step, j, half in beside.get(i, ()):
-                step(j, half)
+            for step, j in beside.get(i, ()):
+                both(step, j)
             if i == 5:
                 wgo_sb = at("wgo", [PK], F32, "wgo")
                 nc.sync.dma_start(wgo_sb[:], wgo)
                 delay_sb = [at("delay%d" % n, [PK], F32, "weighted", (0, 12, 16)[n]) for n in range(OUT_TILES)]
                 for n in range(OUT_TILES):
                     nc.sync.dma_start(delay_sb[n][:], delay[n * P : (n + 1) * P, :])
-            if i == 5:
                 z_grouped[0] = at("z_grouped0", [CHUNKS, BANK, PACK], BF16, "work")
                 for c in range(CHUNKS):
                     interleave(0, c)
             if i == 6:
-                turned_sb = at("turned", [SHARE], F32, "pairs0", 10)
-                spans = [slice(first, min(first + BANK, SHARE)) for first in range(0, SHARE, BANK)]
+                turned_sb = at("turned", [ON_VECTOR], F32, "pairs0", 10)
+                spans = [slice(first, min(first + BANK, ON_VECTOR)) for first in range(0, ON_VECTOR, BANK)]
                 for c, cols in enumerate(spans):
-                    nc.scalar.copy(turned_sb[:, cols], turn(c, staff_sb[last][:, cols])[:, : cols.stop - cols.start])
-                staff_banks = [turn(RESULT_BANKS + c, turned_sb[:, cols]) for c, cols in enumerate(spans)]
+                    nc.scalar.copy(turned_sb[:, cols], turn(c, staff_sb[LAST][:, cols])[:, : cols.stop - cols.start])
+                staff_banks = [turn(PACK + c, turned_sb[:, cols]) for c, cols in enumerate(spans)]
             place(i)
             if i in (3, 4, 5):
                 load_staff({3: 5, 4: 7, 5: 6}[i])
@@ -384,24 +380,23 @@ def tile_list_theatre_turnover_slots_kernel(
             for b in range(PASSES):
                 nc.tensor.matmul_mx(
                     out=acc[:, :width], lhsT=w3_codes[n][:, b].bitcast(FP8X4),
-                    lhsT_scale=w3_planes[:, b, n * P : (n + 1) * P],
+                    lhsT_scale=w3_planes[:, b * N + n * P : b * N + (n + 1) * P],
                     rhs=z_codes[b][:, cols].bitcast(FP8X4), rhs_scale=z_planes[:, b, cols], start=(b == 0), stop=(b == PASSES - 1),
                 )
             return y_sb[n][:, cols], acc[:, :width]
 
         quantise_z(0, 0, BANK)
         load_last = load_sb[:, PASSES - 1, PACK - 1 : PACK]
-        loaded_last = at("loaded_last", [T2 - SHARE], F32, "pairs0", 10)
-        for first, stop in ((SHARE, T2 - BANK), (T2 - BANK, T2)):
+        loaded_last = at("loaded_last", [T2 - ON_VECTOR], F32, "pairs0", 10)
+        for first, stop in ((ON_VECTOR, T2 - BANK), (T2 - BANK, T2)):
             c, j = divmod(first, BANK)
-            rows = loaded_last[:, first - SHARE : stop - SHARE]
-            nc.scalar.activation(rows, pages[last % 2][:, first:stop], ACT.Identity, bias=load_last)
-            nc.gpsimd.tensor_tensor(z_pairs[1][:, c, 1, j : j + stop - first, 1], rows, staff_sb[last][:, first:stop], ALU.mult)
-        for first in range(0, SHARE, BANK):
-            c, width = first // BANK, min(BANK, SHARE - first)
+            rows = loaded_last[:, first - ON_VECTOR : stop - ON_VECTOR]
+            nc.scalar.activation(rows, pages[LAST % 2][:, first:stop], ACT.Identity, bias=load_last)
+            nc.gpsimd.tensor_tensor(z_pairs[1][:, c, 1, j : j + stop - first, 1], rows, staff_sb[LAST][:, first:stop], ALU.mult)
+        for c, cols in enumerate(spans):
+            width = cols.stop - cols.start
             nc.vector.scalar_tensor_tensor(
-                z_pairs[1][:, c, 1, :width, 1], pages[last % 2][:, first : first + width], load_last, staff_banks[c][:, :width],
-                ALU.add, ALU.mult,
+                z_pairs[1][:, c, 1, :width, 1], pages[LAST % 2][:, cols], load_last, staff_banks[c][:, :width], ALU.add, ALU.mult,
             )
         for c in range(CHUNKS):
             interleave(1, c)
@@ -413,14 +408,14 @@ def tile_list_theatre_turnover_slots_kernel(
                 quantise_z(1, c * BANK, BANK)
                 nc.scalar.copy(*features(0, c * BANK, BANK, c))
             if c < 2:
-                second.append(features(1, c * BANK, BANK, (4, 1)[c]))
-        pieces = ((T2 - BANK, 256, 3), (T2 - 256, P, 7), (T2 - P, P, 0))
+                second.append(features(1, c * BANK, BANK, PACK + c))
+        pieces = ((T2 - BANK, 256, 3), (T2 - 256, P, 7), (T2 - P, P, 6))
         for first, width, u in pieces:
             quantise_z(1, first, width)
         for first, width, u in pieces:
-            (nc.vector.tensor_copy if first + width == T2 - P else nc.scalar.copy)(*features(0, first, width, u))
+            nc.vector.tensor_copy(*features(0, first, width, u))
         for c in range(2, CHUNKS):
-            second.append(features(1, c * BANK, BANK, (3, 7)[c - 2]))
+            second.append(features(1, c * BANK, BANK, (1, 3)[c - 2]))
         for target, acc in second:
             nc.scalar.copy(target, acc)
 
@@ -428,26 +423,15 @@ def tile_list_theatre_turnover_slots_kernel(
         for u in range(2):
             nc.gpsimd.memset(crew[u][:], 0.0)
         nc.scalar.activation(neg_low[:], low_sb[:], ACT.Copy, scale=-1.0)
-        floored = {}
-
-        def pick(n):
-            picked = at("picked%d" % n, [PK], F32, "larger", 4 * n)
-            nc.vector.tensor_tensor(picked[:], y_sb[n][:].indirect(list3[:]), delay_sb[n][:], ALU.add)
-            return picked
-
-        def floor(n, picked):
-            above = at("above%d" % n, [PK], F32, "w3", 6)
-            nc.scalar.activation(above[:], picked[:], ACT.Relu, bias=neg_low[:, n : n + 1])
-            floored[n] = at("floored%d" % n, [PK], F32, "gains", 4 * n)
-            nc.scalar.activation(floored[n][:], above[:], ACT.Identity, bias=low_sb[:, n : n + 1])
-
-        def hand_over(n):
-            nc.vector.tensor_tensor(crew[n % 2][:].indirect(list4[:]), floored[n][:], wgo_sb[:], ALU.mult)
-            nc.sync.dma_start(out[n * P : (n + 1) * P, :], crew[n % 2][:])
-
         for c in range(CHUNKS):
-            nc.scalar.copy(*features(2, c * BANK, BANK, (4, 1, 3, 7)[c]))
-        picked = [pick(n) for n in range(OUT_TILES)]
+            nc.scalar.copy(*features(2, c * BANK, BANK, (4, 5, 1, 3)[c]))
+        picked = [at("picked%d" % n, [PK], F32, "larger", 4 * n) for n in range(OUT_TILES)]
         for n in range(OUT_TILES):
-            floor(n, picked[n])
-            hand_over(n)
+            nc.vector.tensor_tensor(picked[n][:], y_sb[n][:].indirect(list3[:]), delay_sb[n][:], ALU.add)
+        for n in range(OUT_TILES):
+            above = at("above%d" % n, [PK], F32, "w3", 6)
+            nc.scalar.activation(above[:], picked[n][:], ACT.Relu, bias=neg_low[:, n : n + 1])
+            floored = at("floored%d" % n, [PK], F32, "gains", 4 * n)
+            nc.scalar.activation(floored[:], above[:], ACT.Identity, bias=low_sb[:, n : n + 1])
+            nc.vector.tensor_tensor(crew[n % 2][:].indirect(list4[:]), floored[:], wgo_sb[:], ALU.mult)
+            nc.sync.dma_start(out[n * P : (n + 1) * P, :], crew[n % 2][:])

@@ -32,7 +32,7 @@ WARM_UPS = 3
 KB = 1024
 AREAS = (
     ("small", 1), ("v_words", 4), ("v_scales", 1), ("w1_early", 4), ("w1_codes", 4),
-    ("w2_codes", 2), ("w2_planes", 1), ("gains", 16), ("pages", 16), ("staff", 8 * STAFF_SLOTS), ("w1_planes", 1), ("loaded0", 8),
+    ("w2_codes", 3), ("w2_planes", 1), ("gains", 16), ("pages", 16), ("staff", 8 * STAFF_SLOTS), ("w1_planes", 1), ("loaded0", 8),
     ("z_codes", 16), ("loaded1", 8.25), ("work", 16), ("pairs1", 16), ("pairs0", 16), ("woven", 16), ("larger", 16),
     ("weighted", 20), ("w3", 10), ("wgo", 4),
 )
@@ -95,7 +95,7 @@ def tile_list_theatre_turnover_slots_kernel(
         tab_w = at("tab_w", [T], U32, "pairs0")
         picked_s = at("picked_s", [S], U8, "woven", 11)
         v_scales = at("v_scales", [S], U8, "v_scales")
-        w2_raw = at("w2_raw", [2 * H], U8, "woven", 8)
+        w2_raw = [at("w2_raw%d" % b, [H], U8, "woven", 8 + 4 * b) for b in range(PASSES)]
         w2_s_raw = at("w2_s_raw", [H], U8, "woven", 10)
         w3_planes = at("w3_planes", [PASSES * N], U8, "w3", 1)
         pages = [at("page%d" % u, [T2], F32, "pages", 8 * u) for u in range(2)]
@@ -114,7 +114,7 @@ def tile_list_theatre_turnover_slots_kernel(
         list1 = load_list(offs, "list1")
         nc.sync.dma_start(w1_first[:], w1_rows[:, :, :BANK])
         nc.sync.dma_start(tab_s[0:P:8].bitcast(I32), tab_scales[0].bitcast(I32))
-        nc.sync.dma_start(w2_raw[:].bitcast(I32), w2_words[0].bitcast(I32))
+        nc.sync.dma_start(w2_raw[0][:].bitcast(I32), w2_words[0][:, :H].bitcast(I32))
         for r in range(4):
             nc.sync.dma_start(w2_s_raw[r:P:32].bitcast(I32), w2_scales[0][r:16:4].bitcast(I32))
         nc.sync.dma_start(tab_w[:].bitcast(I32), tab_words[0].rearrange("p t i -> p (t i)").bitcast(I32))
@@ -141,6 +141,7 @@ def tile_list_theatre_turnover_slots_kernel(
         load_gains(0, half_cols(0))
         list2 = load_list(offs2, "list2")
         load_gains(0, half_cols(1))
+        nc.sync.dma_start(w2_raw[1][:].bitcast(I32), w2_words[0][:, H:].bitcast(I32))
         load_gains(1, slice(0, S))
         load_sb = at("load_sb", [PASSES, PACK], F32, "small", 0.5)
         nc.sync.dma_start(load_sb[:], load.rearrange("(b p t) -> p b t", p=P, t=PACK))
@@ -165,17 +166,22 @@ def tile_list_theatre_turnover_slots_kernel(
         with nc.allow_non_contiguous_dma(reason="one value a partition"):
             nc.sync.dma_start(low_sb[:], low.rearrange("(n p) -> p n", p=P))
 
-        w2_codes = at("w2_codes", [2 * H], U8, "w2_codes")
+        w2_codes = {}
+
+        def order_w2(b, engine_copy):
+            w2_codes[b] = at("w2_codes%d" % b, [H], U8, "w2_codes", b)
+            engine_copy(
+                w2_codes[b][:].bitcast(U16).rearrange("p (t m) -> p t m", t=PACK),
+                w2_raw[b][:].bitcast(U16).rearrange("p (m t) -> p t m", t=PACK),
+            )
+
         w2_planes = at("w2_planes", [H], U8, "w2_planes")
         w1_codes = [at("w1_codes%d" % b, [BANK], U32, "w1_codes", 2 * b) for b in range(PASSES)]
         w1_planes = [at("w1_planes%d" % b, [BANK], U8, "w1_planes", b / 2) for b in range(PASSES)]
         w1_grouped = [at("w1_grouped%d" % b, [PACK, P, PACK], BF16, *(("w1_early", 0), ("weighted", 13))[b]) for b in range(PASSES)]
 
-        def round_w1(b, u, ms, rows, engine_copy):
-            engine_copy(
-                w1_grouped[b][:, 2 * u : 2 * u + 2].rearrange("p t m j -> p m t j")[:, ms],
-                rows[:].rearrange("p j (m t) -> p m t j", t=PACK)[:, :, 2 * u : 2 * u + 2],
-            )
+        def round_w1(b, ms, rows, engine_copy):
+            engine_copy(w1_grouped[b][:].rearrange("p t m j -> p m t j")[:, ms], rows[:].rearrange("p j (m t) -> p m t j", t=PACK))
 
         def gpsimd_copy(target, source):
             nc.gpsimd.tensor_scalar(target, source, 1.0, 0.0, ALU.mult, ALU.add)
@@ -185,13 +191,9 @@ def tile_list_theatre_turnover_slots_kernel(
                 out=w1_codes[b][:].bitcast(FP8X4), scales=w1_planes[b][:], in_=w1_grouped[b][:].rearrange("p t m j -> p (t m j)"),
             )
 
-        for u in range(2):
-            round_w1(0, u, slice(0, P), w1_first, nc.scalar.copy)
+        round_w1(0, slice(0, P), w1_first, nc.scalar.copy)
         quantise_w1(0)
-        nc.vector.tensor_copy(
-            w2_codes[:].bitcast(U16).rearrange("p (b t m) -> p b t m", b=PASSES, t=PACK),
-            w2_raw[:].bitcast(U16).rearrange("p (b m t) -> p b t m", b=PASSES, t=PACK),
-        )
+        order_w2(0, nc.vector.tensor_copy)
         for b in range(PASSES):
             nc.vector.tensor_copy(
                 w2_planes[:, half_cols(b)].rearrange("p (t m) -> p t m", t=PACK),
@@ -199,7 +201,7 @@ def tile_list_theatre_turnover_slots_kernel(
             )
         for u in range(WARM_UPS):
             nc.tensor.matmul_mx(
-                out=bank(1 + u)[:], lhsT=w2_codes[:, : 2 * P].bitcast(FP4X4), lhsT_scale=w2_planes[:, :P],
+                out=bank(1 + u)[:], lhsT=w2_codes[0][:, : 2 * P].bitcast(FP4X4), lhsT_scale=w2_planes[:, :P],
                 rhs=w1_codes[0][:].bitcast(FP8X4), rhs_scale=w1_planes[0][:], start=True, stop=True,
             )
         v_words = [at("v_words%d" % half, [BANK], U32, "v_words", 2 * half) for half in range(2)]
@@ -207,15 +209,14 @@ def tile_list_theatre_turnover_slots_kernel(
             entries = list1[:, (half * BANK + first) // 16 : (half * BANK + stop) // 16]
             nc.vector.tensor_copy(v_words[half][:, first:stop], tab_w[:].indirect(entries))
         for piece in range(2):
-            for u in range(2):
-                round_w1(1, u, slice(piece * P // 2, (piece + 1) * P // 2), w1_late[piece], gpsimd_copy)
+            round_w1(1, slice(piece * P // 2, (piece + 1) * P // 2), w1_late[piece], gpsimd_copy)
 
         def team_product(i, half, u, first=0, stop=BANK):
             b, t = pass_and_byte(i)
             cols = slice((b * PACK + t) * P, (b * PACK + t + 1) * P)
             team = bank(u)[:, : stop - first]
             nc.tensor.matmul_mx(
-                out=team, lhsT=w2_codes[:, 2 * cols.start : 2 * cols.stop].bitcast(FP4X4), lhsT_scale=w2_planes[:, cols],
+                out=team, lhsT=w2_codes[b][:, 2 * t * P : 2 * (t + 1) * P].bitcast(FP4X4), lhsT_scale=w2_planes[:, cols],
                 rhs=v_words[half][:, first:stop].bitcast(FP8X4),
                 rhs_scale=v_scales[:, half * BANK + first : half * BANK + stop], start=True, stop=True,
             )
@@ -242,7 +243,7 @@ def tile_list_theatre_turnover_slots_kernel(
         early = at("team_early", [2, 2, BANK], F32, "loaded0", -0.0625)
         for i, half in ((0, 0), (1, 0), (0, 1), (1, 1), (2, 0), (2, 1), (3, 0), (3, 1)):
             u = 2 * (i % 2) + half
-            team_sb = early[:, i, half] if i < 2 else at("team", [BANK], F32, "woven", 2 * u)[:]
+            team_sb = early[:, i, half] if i < 2 else at("team", [BANK], F32, *(("w2_codes", 1) if u == 2 else ("woven", 2 * u)))[:]
             if (i, half) == (0, 0):
                 for e in range(2):
                     first, stop = e * BANK // 2, (e + 1) * BANK // 2
@@ -252,6 +253,7 @@ def tile_list_theatre_turnover_slots_kernel(
             nc.vector.tensor_tensor(larger[i][:, half_cols(half)], team_sb, room_product(i, half, u)[:], ALU.max)
             if (i, half) == (1, 1):
                 quantise_w1(1)
+        order_w2(1, nc.scalar.copy)
         first_halves = [at("weighted0%d" % half, [BANK], F32, "weighted", (14, 12)[half]) for half in range(2)]
         for half in range(2):
             nc.gpsimd.tensor_tensor(first_halves[half][:], larger[0][:, half_cols(half)], gains[0][:, half_cols(half)], ALU.mult)

@@ -26,7 +26,7 @@ LAST = ROW_TILES - 1
 CHUNKS = T2 // BANK
 OUT_TILES = N // P
 STAFF_SLOTS = 5
-ON_VECTOR = T2 - 768
+ON_VECTOR = T2 - 640
 WARM_UPS = 3
 
 KB = 1024
@@ -387,7 +387,6 @@ def tile_list_theatre_turnover_slots_kernel(
                 )
             return y_sb[n][:, cols], acc[:, :width]
 
-        quantise_z(0, 0, BANK)
         load_last = load_sb[:, PASSES - 1, PACK - 1 : PACK]
         loaded_last = at("loaded_last", [T2 - ON_VECTOR], F32, "pairs0", 10)
         for first, stop in ((ON_VECTOR, T2 - BANK), (T2 - BANK, T2)):
@@ -404,8 +403,7 @@ def tile_list_theatre_turnover_slots_kernel(
             interleave(1, c)
         second = []
         for c in range(CHUNKS):
-            if c > 0:
-                quantise_z(0, c * BANK, BANK)
+            quantise_z(0, c * BANK, BANK)
             if c < CHUNKS - 1:
                 quantise_z(1, c * BANK, BANK)
                 nc.scalar.copy(*features(0, c * BANK, BANK, c))

@@ -243,7 +243,7 @@ def tile_list_theatre_turnover_slots_kernel(
         early = at("team_early", [2, 2, BANK], F32, "loaded0", -0.0625)
         for i, half in ((0, 0), (1, 0), (0, 1), (1, 1), (2, 0), (2, 1), (3, 0), (3, 1)):
             u = 2 * (i % 2) + half
-            team_sb = early[:, i, half] if i < 2 else at("team", [BANK], F32, *(("w2_codes", 1) if u == 2 else ("woven", 2 * u)))[:]
+            team_sb = early[:, i, half] if i < 2 else at("team", [BANK], F32, "woven", 2 * u)[:]
             if (i, half) == (0, 0):
                 for e in range(2):
                     first, stop = e * BANK // 2, (e + 1) * BANK // 2
@@ -253,7 +253,7 @@ def tile_list_theatre_turnover_slots_kernel(
             nc.vector.tensor_tensor(larger[i][:, half_cols(half)], team_sb, room_product(i, half, u)[:], ALU.max)
             if (i, half) == (1, 1):
                 quantise_w1(1)
-        order_w2(1, nc.scalar.copy)
+                order_w2(1, nc.scalar.copy)
         first_halves = [at("weighted0%d" % half, [BANK], F32, "weighted", (14, 12)[half]) for half in range(2)]
         for half in range(2):
             nc.gpsimd.tensor_tensor(first_halves[half][:], larger[0][:, half_cols(half)], gains[0][:, half_cols(half)], ALU.mult)
@@ -270,6 +270,18 @@ def tile_list_theatre_turnover_slots_kernel(
                     )
             return turned
 
+        def team_turned(i, half, u):
+            b, t = pass_and_byte(i)
+            turned = bank(u)
+            for q in range(BANK // P):
+                first = half * BANK + q * P
+                nc.tensor.matmul_mx(
+                    out=turned[:, q * P : (q + 1) * P], lhsT=v_words[half][:, q * P : (q + 1) * P].bitcast(FP8X4),
+                    lhsT_scale=v_scales[:, first : first + P], rhs=w2_codes[b][:, 2 * t * P : 2 * (t + 1) * P].bitcast(FP4X4),
+                    rhs_scale=w2_planes[:, (b * PACK + t) * P : (b * PACK + t + 1) * P], start=True, stop=True,
+                )
+            return turned
+
         pending = {}
 
         def work_tile(i, half, e):
@@ -282,13 +294,13 @@ def tile_list_theatre_turnover_slots_kernel(
             nc.scalar.activation(minus_team[:], team, ACT.Copy, scale=-1.0)
             nc.scalar.copy(room_sb[:], room[:])
             difference = turn(u + 1, minus_team, room_sb)
-            pending[i, half] = (turn(u, minus_team), difference)
+            pending[i, half] = (team_turned(i, half, u) if i == LAST else turn(u, minus_team), difference)
 
         def clip(i, half):
             negated, difference = pending[i, half]
             team_sb, excess = work_tile(i, half, 2), work_tile(i, half, 3)
             nc.scalar.activation(excess[:], difference[:], ACT.Relu)
-            nc.scalar.activation(team_sb[:], negated[:], ACT.Copy, scale=-1.0)
+            nc.scalar.activation(team_sb[:], negated[:], ACT.Copy, scale=1.0 if i == LAST else -1.0)
             pending[i, half] = turn(4 * ((i + 1) % 2) + 2 * half, team_sb, excess)
 
         def collect(i, half):

@@ -26,7 +26,7 @@ LAST = ROW_TILES - 1
 CHUNKS = T2 // BANK
 OUT_TILES = N // P
 STAFF_SLOTS = 5
-ON_VECTOR = T2 - 640
+ON_VECTOR = T2 - 768
 WARM_UPS = 3
 
 KB = 1024

@@ -27,7 +27,7 @@ CHUNKS = T2 // BANK
 OUT_TILES = N // P
 STAFF_SLOTS = 5
 ON_VECTOR = T2 - 768
-WARM_UPS = 3
+WARM_UPS = 5
 
 KB = 1024
 AREAS = (
@@ -201,7 +201,7 @@ def tile_list_theatre_turnover_slots_kernel(
             )
         for u in range(WARM_UPS):
             nc.tensor.matmul_mx(
-                out=bank(1 + u)[:], lhsT=w2_codes[0][:, : 2 * P].bitcast(FP4X4), lhsT_scale=w2_planes[:, :P],
+                out=bank((1, 2, 3, 7, 6)[u])[:], lhsT=w1_codes[0][:, :P].bitcast(FP8X4), lhsT_scale=w1_planes[0][:, :P],
                 rhs=w1_codes[0][:].bitcast(FP8X4), rhs_scale=w1_planes[0][:], start=True, stop=True,
             )
         v_words = [at("v_words%d" % half, [BANK], U32, "v_words", 2 * half) for half in range(2)]
@@ -270,18 +270,6 @@ def tile_list_theatre_turnover_slots_kernel(
                     )
             return turned
 
-        def team_turned(i, half, u):
-            b, t = pass_and_byte(i)
-            turned = bank(u)
-            for q in range(BANK // P):
-                first = half * BANK + q * P
-                nc.tensor.matmul_mx(
-                    out=turned[:, q * P : (q + 1) * P], lhsT=v_words[half][:, q * P : (q + 1) * P].bitcast(FP8X4),
-                    lhsT_scale=v_scales[:, first : first + P], rhs=w2_codes[b][:, 2 * t * P : 2 * (t + 1) * P].bitcast(FP4X4),
-                    rhs_scale=w2_planes[:, (b * PACK + t) * P : (b * PACK + t + 1) * P], start=True, stop=True,
-                )
-            return turned
-
         pending = {}
 
         def work_tile(i, half, e):
@@ -294,13 +282,13 @@ def tile_list_theatre_turnover_slots_kernel(
             nc.scalar.activation(minus_team[:], team, ACT.Copy, scale=-1.0)
             nc.scalar.copy(room_sb[:], room[:])
             difference = turn(u + 1, minus_team, room_sb)
-            pending[i, half] = (team_turned(i, half, u) if i == LAST else turn(u, minus_team), difference)
+            pending[i, half] = (turn(u, minus_team), difference)
 
         def clip(i, half):
             negated, difference = pending[i, half]
             team_sb, excess = work_tile(i, half, 2), work_tile(i, half, 3)
             nc.scalar.activation(excess[:], difference[:], ACT.Relu)
-            nc.scalar.activation(team_sb[:], negated[:], ACT.Copy, scale=1.0 if i == LAST else -1.0)
+            nc.scalar.activation(team_sb[:], negated[:], ACT.Copy, scale=-1.0)
             pending[i, half] = turn(4 * ((i + 1) % 2) + 2 * half, team_sb, excess)
 
         def collect(i, half):

@@ -111,13 +111,13 @@ def tile_list_theatre_turnover_slots_kernel(
 
         w1_rows = w1.rearrange("(p j) c -> p j c", j=PACK)
 
-        list1 = load_list(offs, "list1")
         nc.sync.dma_start(w1_first[:], w1_rows[:, :, :BANK])
+        list1 = load_list(offs, "list1")
         nc.sync.dma_start(tab_s[0:P:8].bitcast(I32), tab_scales[0].bitcast(I32))
-        nc.sync.dma_start(w2_raw[0][:].bitcast(I32), w2_words[0][:, :H].bitcast(I32))
         for r in range(4):
             nc.sync.dma_start(w2_s_raw[r:P:32].bitcast(I32), w2_scales[0][r:16:4].bitcast(I32))
         nc.sync.dma_start(tab_w[:].bitcast(I32), tab_words[0].rearrange("p t i -> p (t i)").bitcast(I32))
+        nc.sync.dma_start(w2_raw[0][:].bitcast(I32), w2_words[0][:, :H].bitcast(I32))
         nc.vector.tensor_copy(picked_s[:], tab_s[:].indirect(list1[:]))
         for r in range(4):
             nc.sync.dma_start(v_scales[r:P:32].bitcast(I32), picked_s[8 * r : P : 32].bitcast(I32))
@@ -193,7 +193,7 @@ def tile_list_theatre_turnover_slots_kernel(
 
         round_w1(0, slice(0, P), w1_first, nc.scalar.copy)
         quantise_w1(0)
-        order_w2(0, nc.vector.tensor_copy)
+        order_w2(0, nc.scalar.copy)
         for b in range(PASSES):
             nc.vector.tensor_copy(
                 w2_planes[:, half_cols(b)].rearrange("p (t m) -> p t m", t=PACK),
@@ -211,24 +211,24 @@ def tile_list_theatre_turnover_slots_kernel(
         for piece in range(2):
             round_w1(1, slice(piece * P // 2, (piece + 1) * P // 2), w1_late[piece], gpsimd_copy)
 
-        def team_product(i, half, u, first=0, stop=BANK):
+        def team_product(i, half, u):
             b, t = pass_and_byte(i)
             cols = slice((b * PACK + t) * P, (b * PACK + t + 1) * P)
-            team = bank(u)[:, : stop - first]
+            team = bank(u)[:]
             nc.tensor.matmul_mx(
                 out=team, lhsT=w2_codes[b][:, 2 * t * P : 2 * (t + 1) * P].bitcast(FP4X4), lhsT_scale=w2_planes[:, cols],
-                rhs=v_words[half][:, first:stop].bitcast(FP8X4),
-                rhs_scale=v_scales[:, half * BANK + first : half * BANK + stop], start=True, stop=True,
+                rhs=v_words[half][:].bitcast(FP8X4), rhs_scale=v_scales[:, half_cols(half)], start=True, stop=True,
             )
             return team
 
-        def room_product(i, half, u):
+        def room_product(i, half, u, first=0, stop=BANK):
             b, t = pass_and_byte(i)
-            room = bank(u)
+            room = bank(u)[:, : stop - first]
             nc.tensor.matmul_mx(
-                out=room[:], lhsT=w1_codes[b][:, t * P : (t + 1) * P].bitcast(FP8X4),
+                out=room, lhsT=w1_codes[b][:, t * P : (t + 1) * P].bitcast(FP8X4),
                 lhsT_scale=w1_planes[b][:, t * P : (t + 1) * P],
-                rhs=v_words[half][:].bitcast(FP8X4), rhs_scale=v_scales[:, half_cols(half)], start=True, stop=True,
+                rhs=v_words[half][:, first:stop].bitcast(FP8X4),
+                rhs_scale=v_scales[:, half * BANK + first : half * BANK + stop], start=True, stop=True,
             )
             return room
 
@@ -247,10 +247,10 @@ def tile_list_theatre_turnover_slots_kernel(
             if (i, half) == (0, 0):
                 for e in range(2):
                     first, stop = e * BANK // 2, (e + 1) * BANK // 2
-                    nc.scalar.copy(team_sb[:, first:stop], team_product(i, half, PACK + e, first, stop))
+                    nc.scalar.copy(team_sb[:, first:stop], room_product(i, half, PACK + e, first, stop))
             else:
-                nc.scalar.copy(team_sb, team_product(i, half, PACK + u))
-            nc.vector.tensor_tensor(larger[i][:, half_cols(half)], team_sb, room_product(i, half, u)[:], ALU.max)
+                nc.scalar.copy(team_sb, room_product(i, half, PACK + u))
+            nc.vector.tensor_tensor(larger[i][:, half_cols(half)], team_sb, team_product(i, half, u), ALU.max)
             if (i, half) == (1, 1):
                 quantise_w1(1)
                 order_w2(1, nc.scalar.copy)
@@ -280,7 +280,7 @@ def tile_list_theatre_turnover_slots_kernel(
             team, room = team_product(i, half, u), room_product(i, half, u + 1)
             minus_team, room_sb = work_tile(i, half, 0), work_tile(i, half, 1)
             nc.scalar.activation(minus_team[:], team, ACT.Copy, scale=-1.0)
-            nc.scalar.copy(room_sb[:], room[:])
+            nc.scalar.copy(room_sb[:], room)
             difference = turn(u + 1, minus_team, room_sb)
             pending[i, half] = (turn(u, minus_team), difference)
 

@@ -27,7 +27,6 @@ CHUNKS = T2 // BANK
 OUT_TILES = N // P
 STAFF_SLOTS = 5
 ON_VECTOR = T2 - 768
-WARM_UPS = 5
 
 KB = 1024
 AREAS = (
@@ -198,11 +197,6 @@ def tile_list_theatre_turnover_slots_kernel(
             nc.vector.tensor_copy(
                 w2_planes[:, half_cols(b)].rearrange("p (t m) -> p t m", t=PACK),
                 w2_s_raw[:, half_cols(b)].rearrange("p (m t) -> p t m", t=PACK),
-            )
-        for u in range(WARM_UPS):
-            nc.tensor.matmul_mx(
-                out=bank((1, 2, 3, 7, 6)[u])[:], lhsT=w1_codes[0][:, :P].bitcast(FP8X4), lhsT_scale=w1_planes[0][:, :P],
-                rhs=w1_codes[0][:].bitcast(FP8X4), rhs_scale=w1_planes[0][:], start=True, stop=True,
             )
         v_words = [at("v_words%d" % half, [BANK], U32, "v_words", 2 * half) for half in range(2)]
         for half, first, stop in ((0, 0, BANK // 2), (0, BANK // 2, BANK), (1, 0, BANK)):

from contextlib import ExitStack

import concourse.mybir as mybir
from concourse.masks import make_identity

K, H, N, T, S, T2, PK = 512, 1024, 384, 4096, 1024, 2048, 1024
FLOPS = 2 * 2 * K * H * S + 2 * H * N * T2

F32 = mybir.dt.float32
BF16 = mybir.dt.bfloat16
I32 = mybir.dt.int32
U32 = mybir.dt.uint32
U16 = mybir.dt.uint16
U8 = mybir.dt.uint8
FP8X4 = mybir.dt.float8_e4m3fn_x4
FP4X4 = mybir.dt.float4_e2m1fn_x4
ALU = mybir.AluOpType
ACT = mybir.ActivationFunctionType

P = 128
PACK = 4
BANK = 512
PASSES = H // (P * PACK)
ROW_TILES = PASSES * PACK
LAST = ROW_TILES - 1
CHUNKS = T2 // BANK
OUT_TILES = N // P
STAFF_SLOTS = 5
ON_VECTOR = T2 - 768

KB = 1024
AREAS = (
    ("small", 1), ("v_words", 4), ("v_scales", 1), ("w1_early", 4), ("w1_codes", 4),
    ("w2_codes", 3), ("w2_planes", 1), ("gains", 16), ("pages", 16), ("staff", 8 * STAFF_SLOTS), ("w1_planes", 1), ("loaded0", 8),
    ("z_codes", 16), ("loaded1", 8.25), ("work", 16), ("pairs1", 16), ("pairs0", 16), ("woven", 16), ("larger", 16),
    ("weighted", 20), ("w3", 10), ("wgo", 4),
)
AT = {name: int(KB * sum(size for other, size in AREAS[:u])) for u, (name, size) in enumerate(AREAS)}

STAFF_SLOT = (0, 1, 2, 3, 4, 2, 1, 0)
WEIGHTED_AT = (None, ("weighted", 16), ("weighted", 4), ("weighted", 8), ("staff", 0), ("staff", 8), ("staff", 24), ("staff", 32))
LARGER_AT = (("larger", 0), ("larger", 4), ("larger", 8), ("larger", 12), ("larger", 0), ("larger", 4), ("staff", 12), ("larger", 12))
LOADED_AT = (("loaded0", 0), ("loaded1", 0), ("loaded0", 0), ("loaded1", 0.0625), ("loaded0", 0), ("pairs0", 0), ("pairs0", 14.9375))
WORK_AT = {
    (4, 0): (("z_codes", 4), ("z_codes", 6), ("z_codes", 4), ("z_codes", 6)),
    (4, 1): (("z_codes", 8), ("z_codes", 10), ("z_codes", 8), ("z_codes", 10)),
    (5, 0): (("z_codes", 14), ("loaded0", 2), ("loaded1", 0), ("loaded1", 2)),
    (5, 1): (("work", 8), ("work", 10), ("work", 8), ("work", 10)),
    (6, 0): (("work", 4), ("loaded0", 7), ("loaded1", 8), ("z_codes", 6)),
    (6, 1): (("z_codes", 8), ("z_codes", 10), ("staff", 4), ("staff", 6)),
    (7, 0): (("work", 2.5), ("work", 5.5), ("loaded0", 0), ("loaded0", 2)),
    (7, 1): (("z_codes", 0), ("z_codes", 12), ("loaded0", 4), ("work", 8)),
}


def pass_and_byte(i):
    b, s = divmod(i, PACK)
    return b, (s if b == 0 else (2, 0, 1, 3)[s])


def half_cols(half):
    return slice(half * BANK, (half + 1) * BANK)


def tile_list_theatre_turnover_slots_kernel(
    tc, tab_words, tab_scales, offs, offs2, offs3, offs4, w1, w2_words, w2_scales,
    wgs, load, staff, w3_words, w3_scales, delay, low, wgo, out,
):
    nc = tc.nc
    with ExitStack() as ctx:
        lists = ctx.enter_context(tc.tile_pool(name="lists", bufs=1))
        sbuf = ctx.enter_context(tc.tile_pool(name="sbuf", bufs=1))
        psum = ctx.enter_context(tc.psum_pool(name="psum", bufs=1))

        def at(name, shape, dtype, area, kb=0):
            start = AT[area] + int(kb * KB)
            return sbuf.tile([P] + shape, dtype, name=name, tag="%s%d" % (name, start), offset=start, align_bytes=64)

        def bank(u):
            return psum.tile([P, BANK], F32, name="bank", tag="bank%d" % u)

        def load_list(source, name):
            tile = lists.tile([P, S // 16], U16, name=name)
            nc.sync.dma_start(tile[:], source)
            return tile

        def zero_on_vector(tile):
            words = tile[:].bitcast(I32)
            cut = words.shape[1] // 2 + 1
            nc.vector.memset(words[:, :cut], 0)
            nc.vector.memset(words[:, cut:], 0)

        tab_s = at("tab_s", [T], U8, "work")
        tab_w = at("tab_w", [T], U32, "pairs0")
        picked_s = at("picked_s", [S], U8, "woven", 11)
        v_scales = at("v_scales", [S], U8, "v_scales")
        w2_raw = [at("w2_raw%d" % b, [H], U8, "woven", 8 + 4 * b) for b in range(PASSES)]
        w2_s_raw = at("w2_s_raw", [H], U8, "woven", 10)
        w3_planes = at("w3_planes", [PASSES * N], U8, "w3", 1)
        pages = [at("page%d" % u, [T2], F32, "pages", 8 * u) for u in range(2)]
        identity = at("identity", [P], F32, "small")
        w1_first = at("w1_first", [PACK, BANK], F32, "loaded0")
        w1_late = [at("w1_late%d" % u, [PACK, BANK // 2], F32, "pairs1", 4 + 4 * u) for u in range(2)]

        nc.gpsimd.memset(tab_s[:].bitcast(I32), 0)
        for tile in (w2_s_raw, v_scales, w3_planes, pages[0]):
            zero_on_vector(tile)
        nc.gpsimd.memset(pages[1][:], 0.0)
        make_identity(nc, identity[:])

        w1_rows = w1.rearrange("(p j) c -> p j c", j=PACK)

        nc.sync.dma_start(w1_first[:], w1_rows[:, :, :BANK])
        list1 = load_list(offs, "list1")
        nc.sync.dma_start(tab_s[0:P:8].bitcast(I32), tab_scales[0].bitcast(I32))
        for r in range(4):
            nc.sync.dma_start(w2_s_raw[r:P:32].bitcast(I32), w2_scales[0][r:16:4].bitcast(I32))
        nc.sync.dma_start(tab_w[:].bitcast(I32), tab_words[0].rearrange("p t i -> p (t i)").bitcast(I32))
        nc.sync.dma_start(w2_raw[0][:].bitcast(I32), w2_words[0][:, :H].bitcast(I32))
        nc.vector.tensor_copy(picked_s[:], tab_s[:].indirect(list1[:]))
        for r in range(4):
            nc.sync.dma_start(v_scales[r:P:32].bitcast(I32), picked_s[8 * r : P : 32].bitcast(I32))
        for u in range(2):
            nc.sync.dma_start(w1_late[u][:], w1_rows[:, :, BANK + u * BANK // 2 : BANK + (u + 1) * BANK // 2])

        wgs_rows = wgs.rearrange("(q t) j -> q t j", t=PACK)
        gains = [at("gains%d" % t, [S], F32, "gains", 4 * t) for t in range(PACK)]

        def load_gains(t, js):
            for g in (0, 2, 1, 3):
                nc.sync.dma_start(gains[t][32 * g : 32 * (g + 1), js], wgs_rows[:, t, js])

        staff_rows = staff.rearrange("(b p t) c -> b t p c", p=P, t=PACK)
        staff_sb = {}

        def load_staff(i):
            staff_sb[i] = at("staff%d" % i, [T2], F32, "staff", 8 * STAFF_SLOT[i])
            nc.sync.dma_start(staff_sb[i][:], staff_rows[pass_and_byte(i)])

        load_gains(0, half_cols(0))
        list2 = load_list(offs2, "list2")
        load_gains(0, half_cols(1))
        nc.sync.dma_start(w2_raw[1][:].bitcast(I32), w2_words[0][:, H:].bitcast(I32))
        load_gains(1, slice(0, S))
        load_sb = at("load_sb", [PASSES, PACK], F32, "small", 0.5)
        nc.sync.dma_start(load_sb[:], load.rearrange("(b p t) -> p b t", p=P, t=PACK))
        for t in range(2, PACK):
            load_gains(t, slice(0, S))
        for i in range(STAFF_SLOTS):
            load_staff(i)
        w3_codes = [at("w3_codes%d" % n, [PASSES, P], U32, "w3", (0, 2, 6)[n]) for n in range(OUT_TILES)]
        for n in range(OUT_TILES):
            nc.sync.dma_start(
                w3_codes[n][:].bitcast(I32), w3_words[:, :, n * P : (n + 1) * P].rearrange("a p c i -> p a (c i)").bitcast(I32)
            )
        for r in range(4):
            nc.sync.dma_start(
                w3_planes[r:P:32].bitcast(I32).rearrange("q (a c) -> q a c", a=PASSES),
                w3_scales.rearrange("a q c -> q a c")[r:16:4].bitcast(I32),
            )
        list3 = load_list(offs3, "list3")
        list4 = load_list(offs4, "list4")
        low_sb = at("low_sb", [OUT_TILES], F32, "small", 0.5625)
        neg_low = at("neg_low", [OUT_TILES], F32, "small", 0.625)
        with nc.allow_non_contiguous_dma(reason="one value a partition"):
            nc.sync.dma_start(low_sb[:], low.rearrange("(n p) -> p n", p=P))

        w2_codes = {}

        def order_w2(b, engine_copy):
            w2_codes[b] = at("w2_codes%d" % b, [H], U8, "w2_codes", b)
            engine_copy(
                w2_codes[b][:].bitcast(U16).rearrange("p (t m) -> p t m", t=PACK),
                w2_raw[b][:].bitcast(U16).rearrange("p (m t) -> p t m", t=PACK),
            )

        w2_planes = at("w2_planes", [H], U8, "w2_planes")
        w1_codes = [at("w1_codes%d" % b, [BANK], U32, "w1_codes", 2 * b) for b in range(PASSES)]
        w1_planes = [at("w1_planes%d" % b, [BANK], U8, "w1_planes", b / 2) for b in range(PASSES)]
        w1_grouped = [at("w1_grouped%d" % b, [PACK, P, PACK], BF16, *(("w1_early", 0), ("weighted", 13))[b]) for b in range(PASSES)]

        def round_w1(b, ms, rows, engine_copy):
            engine_copy(w1_grouped[b][:].rearrange("p t m j -> p m t j")[:, ms], rows[:].rearrange("p j (m t) -> p m t j", t=PACK))

        def gpsimd_copy(target, source):
            nc.gpsimd.tensor_scalar(target, source, 1.0, 0.0, ALU.mult, ALU.add)

        def quantise_w1(b):
            nc.vector.quantize_mx(
                out=w1_codes[b][:].bitcast(FP8X4), scales=w1_planes[b][:], in_=w1_grouped[b][:].rearrange("p t m j -> p (t m j)"),
            )

        round_w1(0, slice(0, P), w1_first, nc.scalar.copy)
        quantise_w1(0)
        order_w2(0, nc.scalar.copy)
        for b in range(PASSES):
            nc.vector.tensor_copy(
                w2_planes[:, half_cols(b)].rearrange("p (t m) -> p t m", t=PACK),
                w2_s_raw[:, half_cols(b)].rearrange("p (m t) -> p t m", t=PACK),
            )
        v_words = [at("v_words%d" % half, [BANK], U32, "v_words", 2 * half) for half in range(2)]
        for half, first, stop in ((0, 0, BANK // 2), (0, BANK // 2, BANK), (1, 0, BANK)):
            entries = list1[:, (half * BANK + first) // 16 : (half * BANK + stop) // 16]
            nc.vector.tensor_copy(v_words[half][:, first:stop], tab_w[:].indirect(entries))
        for piece in range(2):
            round_w1(1, slice(piece * P // 2, (piece + 1) * P // 2), w1_late[piece], gpsimd_copy)

        def team_product(i, half, u):
            b, t = pass_and_byte(i)
            cols = slice((b * PACK + t) * P, (b * PACK + t + 1) * P)
            team = bank(u)[:]
            nc.tensor.matmul_mx(
                out=team, lhsT=w2_codes[b][:, 2 * t * P : 2 * (t + 1) * P].bitcast(FP4X4), lhsT_scale=w2_planes[:, cols],
                rhs=v_words[half][:].bitcast(FP8X4), rhs_scale=v_scales[:, half_cols(half)], start=True, stop=True,
            )
            return team

        def room_product(i, half, u, first=0, stop=BANK):
            b, t = pass_and_byte(i)
            room = bank(u)[:, : stop - first]
            nc.tensor.matmul_mx(
                out=room, lhsT=w1_codes[b][:, t * P : (t + 1) * P].bitcast(FP8X4),
                lhsT_scale=w1_planes[b][:, t * P : (t + 1) * P],
                rhs=v_words[half][:, first:stop].bitcast(FP8X4),
                rhs_scale=v_scales[:, half * BANK + first : half * BANK + stop], start=True, stop=True,
            )
            return room

        larger, weighted = {}, {}

        def weigh(i):
            weighted[i] = at("weighted%d" % i, [S], F32, *WEIGHTED_AT[i])
            nc.gpsimd.tensor_tensor(weighted[i][:], larger[i][:], gains[pass_and_byte(i)[1]][:], ALU.mult)

        for i in range(PACK):
            larger[i] = at("larger%d" % i, [S], F32, *LARGER_AT[i])
        early = at("team_early", [2, 2, BANK], F32, "loaded0", -0.0625)
        for i, half in ((0, 0), (1, 0), (0, 1), (1, 1), (2, 0), (2, 1), (3, 0), (3, 1)):
            u = 2 * (i % 2) + half
            team_sb = early[:, i, half] if i < 2 else at("team", [BANK], F32, "woven", 2 * u)[:]
            if (i, half) == (0, 0):
                for e in range(2):
                    first, stop = e * BANK // 2, (e + 1) * BANK // 2
                    nc.scalar.copy(team_sb[:, first:stop], room_product(i, half, PACK + e, first, stop))
            else:
                nc.scalar.copy(team_sb, room_product(i, half, PACK + u))
            nc.vector.tensor_tensor(larger[i][:, half_cols(half)], team_sb, team_product(i, half, u), ALU.max)
            if (i, half) == (1, 1):
                quantise_w1(1)
                order_w2(1, nc.scalar.copy)
        first_halves = [at("weighted0%d" % half, [BANK], F32, "weighted", (14, 12)[half]) for half in range(2)]
        for half in range(2):
            nc.gpsimd.tensor_tensor(first_halves[half][:], larger[0][:, half_cols(half)], gains[0][:, half_cols(half)], ALU.mult)
        for i in range(1, PACK):
            weigh(i)

        def turn(u, *terms):
            turned = bank(u)
            for q in range(terms[0].shape[-1] // P):
                for e, rows in enumerate(terms):
                    nc.tensor.matmul(
                        turned[:, q * P : (q + 1) * P], rows[:, q * P : (q + 1) * P], identity[:],
                        start=(e == 0), stop=(e == len(terms) - 1), is_transpose=True,
                    )
            return turned

        pending = {}

        def work_tile(i, half, e):
            return at("work%d%d%d" % (i, half, e), [BANK], F32, *WORK_AT[i, half][e])

        def subtract(i, half):
            u = 4 * ((i + 1) % 2) + 2 * half
            team, room = team_product(i, half, u), room_product(i, half, u + 1)
            minus_team, room_sb = work_tile(i, half, 0), work_tile(i, half, 1)
            nc.scalar.activation(minus_team[:], team, ACT.Copy, scale=-1.0)
            nc.scalar.copy(room_sb[:], room)
            difference = turn(u + 1, minus_team, room_sb)
            pending[i, half] = (turn(u, minus_team), difference)

        def clip(i, half):
            negated, difference = pending[i, half]
            team_sb, excess = work_tile(i, half, 2), work_tile(i, half, 3)
            nc.scalar.activation(excess[:], difference[:], ACT.Relu)
            nc.scalar.activation(team_sb[:], negated[:], ACT.Copy, scale=-1.0)
            pending[i, half] = turn(4 * ((i + 1) % 2) + 2 * half, team_sb, excess)

        def collect(i, half):
            if half == 0:
                larger[i] = at("larger%d" % i, [S], F32, *LARGER_AT[i])
            nc.scalar.copy(larger[i][:, half_cols(half)], pending[i, half][:])
            if half == 1:
                weigh(i)

        def place(i):
            if i == 0:
                for half in range(2):
                    nc.vector.tensor_copy(pages[0][:].indirect(list2[:, half * 32 : (half + 1) * 32]), first_halves[half][:])
            else:
                nc.vector.tensor_copy(pages[i % 2][:].indirect(list2[:]), weighted[i][:])

        z_pairs = [at("z_pairs%d" % b, [CHUNKS, 2, BANK, 2], BF16, "pairs%d" % b) for b in range(PASSES)]

        def staffed(i):
            b, t = pass_and_byte(i)
            loaded = at("loaded%d" % i, [T2], F32, *LOADED_AT[i])
            for chunks in (slice(0, 1), slice(1, CHUNKS)) if i in (0, LAST - 1) else (slice(0, CHUNKS),):
                cols = slice(chunks.start * BANK, chunks.stop * BANK)
                nc.scalar.activation(loaded[:, cols], pages[i % 2][:, cols], ACT.Identity, bias=load_sb[:, b, t : t + 1])
                nc.gpsimd.tensor_tensor(
                    z_pairs[b][:, chunks, t // 2, :, t % 2],
                    loaded[:, cols].rearrange("p (c j) -> p c j", j=BANK),
                    staff_sb[i][:, cols].rearrange("p (c j) -> p c j", j=BANK), ALU.mult,
                )

        z_grouped = {}

        def interleave(b, c):
            nc.scalar.copy(
                z_grouped[b][:, c].rearrange("p j t -> p (j t)").bitcast(U32).rearrange("p (j u) -> p j u", u=2),
                z_pairs[b][:, c].rearrange("p u j e -> p u (j e)").bitcast(U32).rearrange("p u j -> p j u"),
            )

        def both(step, i):
            for half in range(2):
                step(i, half)

        beside = {
            0: ((subtract, 4), (subtract, 5), (clip, 4)),
            1: ((collect, 4), (clip, 5)),
            2: ((subtract, 6), (collect, 5)),
            3: ((clip, 6), (subtract, 7)),
            4: ((collect, 6), (clip, 7)),
            5: ((collect, 7),),
        }
        for i in range(ROW_TILES):
            if i > 0:
                staffed(i - 1)
            for step, j in beside.get(i, ()):
                both(step, j)
            if i == 5:
                wgo_sb = at("wgo", [PK], F32, "wgo")
                nc.sync.dma_start(wgo_sb[:], wgo)
                delay_sb = [at("delay%d" % n, [PK], F32, "weighted", (0, 12, 16)[n]) for n in range(OUT_TILES)]
                for n in range(OUT_TILES):
                    nc.sync.dma_start(delay_sb[n][:], delay[n * P : (n + 1) * P, :])
                z_grouped[0] = at("z_grouped0", [CHUNKS, BANK, PACK], BF16, "work")
                for c in range(CHUNKS):
                    interleave(0, c)
            if i == 6:
                turned_sb = at("turned", [ON_VECTOR], F32, "pairs0", 10)
                spans = [slice(first, min(first + BANK, ON_VECTOR)) for first in range(0, ON_VECTOR, BANK)]
                for c, cols in enumerate(spans):
                    nc.scalar.copy(turned_sb[:, cols], turn(c, staff_sb[LAST][:, cols])[:, : cols.stop - cols.start])
                staff_banks = [turn(PACK + c, turned_sb[:, cols]) for c, cols in enumerate(spans)]
            place(i)
            if i in (3, 4, 5):
                load_staff({3: 5, 4: 7, 5: 6}[i])

        z_grouped[1] = at("z_grouped1", [CHUNKS, BANK, PACK], BF16, "woven")
        z_codes = [at("z_codes%d" % b, [T2], U32, "z_codes", 8 * b) for b in range(PASSES)]
        z_planes = at("z_planes", [PASSES, T2], U8, "staff", 32)
        y_sb = [at("y%d" % n, [T2], F32, "staff", 8 * (2, 3, 1)[n]) for n in range(OUT_TILES)]

        def quantise_z(b, first, width):
            cols = slice(first, first + width)
            c, j = divmod(first, BANK)
            nc.vector.quantize_mx(
                out=z_codes[b][:, cols].bitcast(FP8X4), scales=z_planes[:, b, cols],
                in_=z_grouped[b][:, c, j : j + width].rearrange("p j t -> p (j t)"),
            )

        def features(n, first, width, u):
            cols = slice(first, first + width)
            acc = bank(u)
            for b in range(PASSES):
                nc.tensor.matmul_mx(
                    out=acc[:, :width], lhsT=w3_codes[n][:, b].bitcast(FP8X4),
                    lhsT_scale=w3_planes[:, b * N + n * P : b * N + (n + 1) * P],
                    rhs=z_codes[b][:, cols].bitcast(FP8X4), rhs_scale=z_planes[:, b, cols], start=(b == 0), stop=(b == PASSES - 1),
                )
            return y_sb[n][:, cols], acc[:, :width]

        load_last = load_sb[:, PASSES - 1, PACK - 1 : PACK]
        loaded_last = at("loaded_last", [T2 - ON_VECTOR], F32, "pairs0", 10)
        for first, stop in ((ON_VECTOR, T2 - BANK), (T2 - BANK, T2)):
            c, j = divmod(first, BANK)
            rows = loaded_last[:, first - ON_VECTOR : stop - ON_VECTOR]
            nc.scalar.activation(rows, pages[LAST % 2][:, first:stop], ACT.Identity, bias=load_last)
            nc.gpsimd.tensor_tensor(z_pairs[1][:, c, 1, j : j + stop - first, 1], rows, staff_sb[LAST][:, first:stop], ALU.mult)
        for c, cols in enumerate(spans):
            width = cols.stop - cols.start
            nc.vector.scalar_tensor_tensor(
                z_pairs[1][:, c, 1, :width, 1], pages[LAST % 2][:, cols], load_last, staff_banks[c][:, :width], ALU.add, ALU.mult,
            )
        for c in range(CHUNKS):
            interleave(1, c)
        second = []
        for c in range(CHUNKS):
            quantise_z(0, c * BANK, BANK)
            if c < CHUNKS - 1:
                quantise_z(1, c * BANK, BANK)
                nc.scalar.copy(*features(0, c * BANK, BANK, c))
            if c < 2:
                second.append(features(1, c * BANK, BANK, PACK + c))
        pieces = ((T2 - BANK, 256, 3), (T2 - 256, P, 7), (T2 - P, P, 6))
        for first, width, u in pieces:
            quantise_z(1, first, width)
        for first, width, u in pieces:
            nc.vector.tensor_copy(*features(0, first, width, u))
        for c in range(2, CHUNKS):
            second.append(features(1, c * BANK, BANK, (1, 3)[c - 2]))
        for target, acc in second:
            nc.scalar.copy(target, acc)

        crew = [at("crew%d" % u, [T2], F32, "woven", 8 * u) for u in range(2)]
        for u in range(2):
            nc.gpsimd.memset(crew[u][:], 0.0)
        nc.scalar.activation(neg_low[:], low_sb[:], ACT.Copy, scale=-1.0)
        for c in range(CHUNKS):
            nc.scalar.copy(*features(2, c * BANK, BANK, (4, 5, 1, 3)[c]))
        picked = [at("picked%d" % n, [PK], F32, "larger", 4 * n) for n in range(OUT_TILES)]
        for n in range(OUT_TILES):
            nc.vector.tensor_tensor(picked[n][:], y_sb[n][:].indirect(list3[:]), delay_sb[n][:], ALU.add)
        for n in range(OUT_TILES):
            above = at("above%d" % n, [PK], F32, "w3", 6)
            nc.scalar.activation(above[:], picked[n][:], ACT.Relu, bias=neg_low[:, n : n + 1])
            floored = at("floored%d" % n, [PK], F32, "gains", 4 * n)
            nc.scalar.activation(floored[:], above[:], ACT.Identity, bias=low_sb[:, n : n + 1])
            nc.vector.tensor_tensor(crew[n % 2][:].indirect(list4[:]), floored[:], wgo_sb[:], ALU.mult)
            nc.sync.dma_start(out[n * P : (n + 1) * P, :], crew[n % 2][:])
